import numpy as np
import ml_dtypes


def mxq(x, axis, fmt="e4m3"):
    dtype, down = {"e4m3": (ml_dtypes.float8_e4m3fn, 7), "e5m2": (ml_dtypes.float8_e5m2, 14)}[fmt]
    v = np.moveaxis(np.asarray(x, np.float32).astype(ml_dtypes.bfloat16).astype(np.float64), axis, -1)
    blocks = v.reshape(v.shape[:-1] + (-1, 32))
    amax = np.abs(blocks).max(-1, keepdims=True)
    byte = np.maximum(np.where(amax > 0, np.frexp(amax)[1] - 1 + 127, 0) - down, 1)
    scale = np.exp2(byte - 127.0)
    codes = (blocks / scale).astype(np.float32).astype(dtype).astype(np.float64)
    return np.moveaxis((codes * scale).reshape(v.shape), -1, axis)


WIDE = False


def mx_kscale(k):
    if not WIDE:
        return np.ones(k)
    levels = np.array([10, -10, 5, -5, 0])
    if k % 512:
        return np.exp2(np.random.permutation(np.resize(levels, k // 32))).repeat(32)
    a = np.empty((k // 512, 16))
    for p in range(k // 512):
        a[p, :8] = np.random.permutation(np.resize(levels, 8))
        for g in range(8):
            far = levels[np.abs(levels - a[p, g]) >= 10]
            a[p, g + 8] = far[np.random.randint(len(far))]
    return np.exp2(a.ravel()).repeat(32)


def f64(x):
    return np.asarray(x).astype(np.float64)


def striped(idx):
    return np.tile(idx.reshape(-1, 16).T, (8, 1)).astype(np.uint16)


def unstriped(offs):
    return offs[:16].T.reshape(-1).astype(np.int64)


def pack_weight(w):
    k, n = w.shape
    w = f64(np.asarray(w, np.float32).astype(ml_dtypes.bfloat16)).reshape(k // 32, 32, n)
    amax = np.abs(w).max(1)
    byte = np.clip(np.where(amax > 0, np.frexp(amax)[1] - 1 + 127 - 7, 1), 1, 254)
    scaled = (w * np.exp2(127.0 - byte)[:, None, :]).reshape(k, n).astype(np.float32)
    words = np.ascontiguousarray(scaled.reshape(k // 512, 128, 4, n).transpose(0, 1, 3, 2)).astype(ml_dtypes.float8_e4m3fn).view(np.uint8)
    return words, np.ascontiguousarray(byte.astype(np.uint8).reshape(k // 512, 16, n))


def unpack_weight(words, scales):
    g, p, n, _ = words.shape
    vals = np.ascontiguousarray(words).view(ml_dtypes.float8_e4m3fn).astype(np.float64) * np.repeat(np.exp2(scales.astype(np.float64) - 127.0), 8, axis=1)[..., None]
    return vals.transpose(0, 1, 3, 2).reshape(g * 512, n)


def relu(v):
    return np.maximum(v, 0.0)


K, T, S, D, V, H, N, U = 1024, 2048, 1024, 2, 512, 512, 256, 256
P = 2 ** 7


def setup_inputs():
    n = np.random.standard_normal
    s = mx_kscale(K)[:, None]
    u = mx_kscale(H)
    packed_w2 = pack_weight(n((H, N)) / np.sqrt(H) / u[:, None])
    return {
        "xT": (n((K, T)) * s).astype(np.float32),
        "w1": (n((K, H)) / np.sqrt(K) / s * u).astype(np.float32),
        "w2_words": packed_w2[0],
        "w2_scales": packed_w2[1],
        "gate": (np.tile(np.random.uniform(0.2, 1.0, (D, 1, V)) / np.sqrt(D), (1, P, 1))).astype(np.float32),
        "gate2": (np.tile(np.random.uniform(0.2, 1.0, (D, 1, U)) / np.sqrt(D), (1, P, 1))).astype(np.float32),
        "offs": striped(np.random.permutation(T)[:S]),
        "pos1": striped(np.random.permutation(S)[:V]),
        "pos2": striped(np.random.permutation(S)[:V]),
        "nxt1": striped(np.random.permutation(V)[:U]),
        "nxt2": striped(np.random.permutation(V)[:U]),
    }


def reference(xT, w1, w2_words, w2_scales, gate, gate2, offs, pos1, pos2, nxt1, nxt2):
    xq = mxq(f64(xT)[:, unstriped(offs)], 0, "e4m3")
    h = relu(mxq(f64(w1), 0, "e4m3").T @ xq)
    z = h[:, unstriped(pos1)] * f64(gate)[0, :1] + h[:, unstriped(pos2)] * f64(gate)[1, :1]
    g = relu(unpack_weight(w2_words, w2_scales).T @ mxq(z, 0, "e4m3"))
    return g[:, unstriped(nxt1)] * f64(gate2)[0, :1] + g[:, unstriped(nxt2)] * f64(gate2)[1, :1]

@@ -1,0 +1,199 @@
+from contextlib import ExitStack
+
+import concourse.mybir as mybir
+
+K, T, S, V, H, N, U = 1024, 2048, 1024, 512, 512, 256, 256
+FLOPS = 2 * K * H * S + 2 * H * N * V
+
+F32 = mybir.dt.float32
+BF16 = mybir.dt.bfloat16
+I32 = mybir.dt.int32
+U32 = mybir.dt.uint32
+U16 = mybir.dt.uint16
+U8 = mybir.dt.uint8
+FP8X4 = mybir.dt.float8_e4m3fn_x4
+COPY = mybir.ActivationFunctionType.Copy
+RELU = mybir.ActivationFunctionType.Relu
+MULT = mybir.AluOpType.mult
+ADD = mybir.AluOpType.add
+
+P = 128
+PACK = 4
+K_PASS = P * PACK
+PASSES = K // K_PASS
+LIST_ROWS = 16
+LINE = 4
+X_CHUNKS = ((512, 512, 512, 512), (512, 512, 512, 256, 256))
+SCALAR_SHARE = {512: 320, 256: 96}
+W_CHUNK = 256
+BANK = 512
+
+
+def tile_picked_hop2_relu_e_kernel(
+    tc, xT, w1, w2_words, w2_scales, gate, gate2, offs, pos1, pos2, nxt1, nxt2, out
+):
+    nc = tc.nc
+    with ExitStack() as ctx:
+        keep = ctx.enter_context(tc.tile_pool(name="keep", bufs=1))
+        psum = ctx.enter_context(tc.psum_pool(name="psum", bufs=8))
+
+        def load_list(name, source):
+            tile = keep.tile(list(source.shape), U16, name=name)
+            nc.sync.dma_start(tile[:], source)
+            return tile
+
+        def entries(tile, start, count):
+            return tile[:, start // LIST_ROWS : (start + count) // LIST_ROWS]
+
+        x_scales = keep.tile([P, T], U8, name="x_scales", align_bytes=64)
+        nc.vector.memset(x_scales[:].bitcast(I32), 0)
+        w2_scale_tile = keep.tile([P, N], U8, name="w2_scale_tile", align_bytes=64)
+        nc.vector.memset(w2_scale_tile[:].bitcast(I32), 0)
+
+        x_raw = {}
+        for g in range(PASSES):
+            rows = xT[g * K_PASS : (g + 1) * K_PASS, :].rearrange("(p j) c -> p j c", j=PACK)
+            c0 = 0
+            for width in X_CHUNKS[g]:
+                raw = keep.tile([P, PACK, width], F32, name="x_raw_%d_%d" % (g, c0))
+                nc.sync.dma_start(raw[:], rows[:, :, c0 : c0 + width])
+                x_raw[g, c0] = raw
+                c0 = c0 + width
+            if g == 0:
+                offs_tile = load_list("offs_tile", offs)
+        w_raw = {}
+        for g in range(PASSES):
+            rows = w1[g * K_PASS : (g + 1) * K_PASS, :].rearrange("(p j) c -> p j c", j=PACK)
+            for c0 in range(0, H, W_CHUNK):
+                raw = keep.tile([P, PACK, W_CHUNK], F32, name="w_raw_%d_%d" % (g, c0))
+                nc.sync.dma_start(raw[:], rows[:, :, c0 : c0 + W_CHUNK])
+                w_raw[g, c0] = raw
+        pos_tiles = [load_list("pos1_tile", pos1), load_list("pos2_tile", pos2)]
+        gate_tile = keep.tile([P, 2, V], F32, name="gate_tile")
+        nc.sync.dma_start(gate_tile[:], gate.rearrange("d p v -> p d v"))
+        w2_codes = keep.tile([P, N], U32, name="w2_codes", align_bytes=64)
+        nc.sync.dma_start(w2_codes[:].bitcast(I32), w2_words[0].rearrange("p n t -> p (n t)").bitcast(I32))
+        for q in range(4):
+            nc.sync.dma_start(
+                w2_scale_tile[32 * q : 32 * q + 4, :].bitcast(I32), w2_scales[0, 4 * q : 4 * q + 4, :].bitcast(I32)
+            )
+        nxt_tiles = [load_list("nxt1_tile", nxt1), load_list("nxt2_tile", nxt2)]
+        gate2_tile = keep.tile([P, 2, U], F32, name="gate2_tile")
+        nc.sync.dma_start(gate2_tile[:], gate2.rearrange("d p v -> p d v"))
+
+        x_words = [keep.tile([P, T], U32, name="x_words_%d" % g, align_bytes=64) for g in range(PASSES)]
+        picked_words = {}
+        picked_scales = [keep.tile([P, BANK], U8, name="picked_scales_%d" % s, align_bytes=64) for s in range(2)]
+
+        def round_chunk(g, c0, width):
+            grouped = keep.tile([P, width * PACK], BF16, name="x_grouped_%d_%d" % (g, c0), align_bytes=64)
+            src = x_raw[g, c0][:].rearrange("p j (c i) -> p c j i", i=LINE)
+            dst = grouped[:].rearrange("p (c i j) -> p c j i", i=LINE, j=PACK)
+            split = SCALAR_SHARE[width] // LINE
+            nc.scalar.activation(dst[:, :split], src[:, :split], COPY)
+            nc.vector.tensor_copy(dst[:, split:], src[:, split:])
+            return grouped
+
+        def quantize_chunk(g, c0, width, grouped):
+            nc.vector.quantize_mx(
+                out=x_words[g][:, c0 : c0 + width].bitcast(FP8X4),
+                scales=x_scales[4 * g :, c0 : c0 + width],
+                in_=grouped[:],
+            )
+
+        def pick_words(g, s, tag):
+            picked_words[g, s] = keep.tile([P, BANK], U32, name="picked_words_%d_%d" % (g, s), tag=tag, align_bytes=64)
+            nc.vector.tensor_copy(picked_words[g, s][:], x_words[g][:].indirect(entries(offs_tile, s * BANK, BANK)))
+
+        def pick_scales(s):
+            nc.vector.tensor_copy(picked_scales[s][:], x_scales[:].indirect(entries(offs_tile, s * BANK, BANK)))
+
+        for g in range(PASSES):
+            c0 = 0
+            for index, width in enumerate(X_CHUNKS[g]):
+                quantize_chunk(g, c0, width, round_chunk(g, c0, width))
+                if g == 1 and index < 2:
+                    pick_words(0, index, "picked_0_%d" % index)
+                c0 = c0 + width
+
+        w_grouped = [keep.tile([P, H * PACK], BF16, name="w_grouped_%d" % g, tag="w_grouped_%d" % g, align_bytes=64) for g in range(PASSES)]
+        w_codes = [keep.tile([P, H], U32, name="w_codes_%d" % g, align_bytes=64) for g in range(PASSES)]
+        w_scales = [keep.tile([P, H], U8, name="w_scales_%d" % g, align_bytes=64) for g in range(PASSES)]
+        for g in range(PASSES):
+            dst = w_grouped[g][:].rearrange("p (t m j) -> p m j t", t=PACK, j=PACK)
+            for c0 in range(0, H, W_CHUNK):
+                src = w_raw[g, c0][:].rearrange("p j (m t) -> p m j t", t=PACK)
+                nc.scalar.activation(dst[:, c0 // PACK : (c0 + W_CHUNK) // PACK], src, COPY)
+
+        def quantize_w(g, c0, width):
+            nc.vector.quantize_mx(
+                out=w_codes[g][:, c0 : c0 + width].bitcast(FP8X4),
+                scales=w_scales[g][:, c0 : c0 + width],
+                in_=w_grouped[g][:, PACK * c0 : PACK * (c0 + width)],
+            )
+
+        pick_scales(0)
+        pick_scales(1)
+        pick_words(1, 0, "picked_1_0")
+        quantize_w(0, 0, H)
+        pick_words(1, 1, "w_grouped_0")
+        quantize_w(1, 0, P)
+        quantize_w(1, P, P)
+        quantize_w(1, 2 * P, 2 * P)
+
+        h_banks = [[psum.tile([P, BANK], F32, name="bank") for s in range(2)] for t in range(PACK)]
+        for t in range(PACK):
+            for g in range(PASSES):
+                for s in range(2):
+                    nc.tensor.matmul_mx(
+                        out=h_banks[t][s][:],
+                        lhsT=w_codes[g][:, t * P : (t + 1) * P].bitcast(FP8X4),
+                        lhsT_scale=w_scales[g][:, t * P : (t + 1) * P],
+                        rhs=picked_words[g, s][:].bitcast(FP8X4),
+                        rhs_scale=picked_scales[s][4 * g :, :],
+                        start=(g == 0),
+                        stop=(g == PASSES - 1),
+                    )
+
+        terms = [keep.tile([P, PACK, V], F32, name="term_%d" % d) for d in range(2)]
+        for t in range(PACK):
+            h = keep.tile([P, S], F32, name="h_%d" % t)
+            for s in range(2):
+                nc.scalar.activation(h[:, s * BANK : (s + 1) * BANK], h_banks[t][s][:], RELU)
+            for d in range(2):
+                nc.vector.tensor_tensor(terms[d][:, t, :], h[:].indirect(pos_tiles[d][:]), gate_tile[:, d, :], MULT)
+
+        half = V // 2
+        z_grouped = [keep.tile([P, half * PACK], BF16, name="z_grouped_%d" % s, align_bytes=64) for s in range(2)]
+        z_codes = [keep.tile([P, half], U32, name="z_codes_%d" % s, align_bytes=64) for s in range(2)]
+        z_scales = [keep.tile([P, half], U8, name="z_scales_%d" % s, align_bytes=64) for s in range(2)]
+        for s in range(2):
+            a, b = [
+                term[:, :, s * half : (s + 1) * half].rearrange("p t (c i) -> p c t i", i=LINE) for term in terms
+            ]
+            nc.vector.tensor_tensor(z_grouped[s][:].rearrange("p (c i t) -> p c t i", i=LINE, t=PACK), a, b, ADD)
+        for s in range(2):
+            nc.vector.quantize_mx(out=z_codes[s][:].bitcast(FP8X4), scales=z_scales[s][:], in_=z_grouped[s][:])
+
+        for m in range(N // P):
+            g_tile = keep.tile([P, V], F32, name="g_%d" % m)
+            for s in range(2):
+                bank = psum.tile([P, BANK], F32, name="bank")
+                nc.tensor.matmul_mx(
+                    out=bank[:, :half],
+                    lhsT=w2_codes[:, m * P : (m + 1) * P].bitcast(FP8X4),
+                    lhsT_scale=w2_scale_tile[:, m * P : (m + 1) * P],
+                    rhs=z_codes[s][:].bitcast(FP8X4),
+                    rhs_scale=z_scales[s][:],
+                    start=True,
+                    stop=True,
+                )
+                nc.scalar.activation(g_tile[:, s * half : (s + 1) * half], bank[:, :half], RELU)
+            root_terms = [keep.tile([P, U], F32, name="root_term_%d_%d" % (m, d)) for d in range(2)]
+            for d in range(2):
+                nc.vector.tensor_tensor(
+                    root_terms[d][:], g_tile[:].indirect(nxt_tiles[d][:]), gate2_tile[:, d, :], MULT
+                )
+            result = keep.tile([P, U], F32, name="result_%d" % m)
+            nc.vector.tensor_tensor(result[:], root_terms[0][:], root_terms[1][:], ADD)
+            nc.sync.dma_start(out[m * P : (m + 1) * P, :], result[:])

@@ -1,6 +1,7 @@
 from contextlib import ExitStack
 
 import concourse.mybir as mybir
+from concourse.masks import make_identity
 
 K, T, S, V, H, N, U = 1024, 2048, 1024, 512, 512, 256, 256
 FLOPS = 2 * K * H * S + 2 * H * N * V
@@ -23,10 +24,12 @@ K_PASS = P * PACK
 PASSES = K // K_PASS
 LIST_ROWS = 16
 LINE = 4
-X_CHUNKS = ((512, 512, 512, 512), (512, 512, 512, 256, 256))
-SCALAR_SHARE = {512: 320, 256: 96}
-W_CHUNK = 256
 BANK = 512
+X_LOADS = (
+    (((512, 0), (512, 384)), ((512, 256),), ((512, 256),)),
+    (((512, 0), (512, 384)), ((512, 320),), ((256, 128),), ((256, 96),)),
+)
+TURNED = 384
 
 
 def tile_picked_hop2_relu_e_kernel(
@@ -35,7 +38,7 @@ def tile_picked_hop2_relu_e_kernel(
     nc = tc.nc
     with ExitStack() as ctx:
         keep = ctx.enter_context(tc.tile_pool(name="keep", bufs=1))
-        psum = ctx.enter_context(tc.psum_pool(name="psum", bufs=8))
+        psum = ctx.enter_context(tc.psum_pool(name="psum", bufs=1))
 
         def load_list(name, source):
             tile = keep.tile(list(source.shape), U16, name=name)
@@ -45,32 +48,39 @@ def tile_picked_hop2_relu_e_kernel(
         def entries(tile, start, count):
             return tile[:, start // LIST_ROWS : (start + count) // LIST_ROWS]
 
+        def bank(number, name):
+            return psum.tile([P, BANK], F32, name=name, tag="bank_%d" % number)
+
         x_scales = keep.tile([P, T], U8, name="x_scales", align_bytes=64)
         nc.vector.memset(x_scales[:].bitcast(I32), 0)
         w2_scale_tile = keep.tile([P, N], U8, name="w2_scale_tile", align_bytes=64)
         nc.vector.memset(w2_scale_tile[:].bitcast(I32), 0)
+        identity = keep.tile([P, P], F32, name="identity")
+        make_identity(nc, identity[:])
 
-        x_raw = {}
+        x_blocks = []
         for g in range(PASSES):
             rows = xT[g * K_PASS : (g + 1) * K_PASS, :].rearrange("(p j) c -> p j c", j=PACK)
             c0 = 0
-            for width in X_CHUNKS[g]:
+            for blocks in X_LOADS[g]:
+                width = sum(nodes for nodes, share in blocks)
                 raw = keep.tile([P, PACK, width], F32, name="x_raw_%d_%d" % (g, c0))
                 nc.sync.dma_start(raw[:], rows[:, :, c0 : c0 + width])
-                x_raw[g, c0] = raw
+                first = 0
+                for nodes, share in blocks:
+                    x_blocks.append((g, c0 + first, nodes, share, raw[:, :, first : first + nodes]))
+                    first = first + nodes
                 c0 = c0 + width
             if g == 0:
                 offs_tile = load_list("offs_tile", offs)
-        w_raw = {}
+        w_raw = [keep.tile([P, PACK, H], F32, name="w_raw_%d" % g) for g in range(PASSES)]
         for g in range(PASSES):
-            rows = w1[g * K_PASS : (g + 1) * K_PASS, :].rearrange("(p j) c -> p j c", j=PACK)
-            for c0 in range(0, H, W_CHUNK):
-                raw = keep.tile([P, PACK, W_CHUNK], F32, name="w_raw_%d_%d" % (g, c0))
-                nc.sync.dma_start(raw[:], rows[:, :, c0 : c0 + W_CHUNK])
-                w_raw[g, c0] = raw
+            nc.sync.dma_start(w_raw[g][:], w1[g * K_PASS : (g + 1) * K_PASS, :].rearrange("(p j) c -> p j c", j=PACK))
         pos_tiles = [load_list("pos1_tile", pos1), load_list("pos2_tile", pos2)]
-        gate_tile = keep.tile([P, 2, V], F32, name="gate_tile")
-        nc.sync.dma_start(gate_tile[:], gate.rearrange("d p v -> p d v"))
+        gate_turned = keep.tile([P, 2, TURNED], F32, name="gate_turned", tag="gate_turned")
+        nc.sync.dma_start(gate_turned[:], gate[:, :, :TURNED].rearrange("d p v -> p d v"))
+        gate_rest = keep.tile([P, 2, V - TURNED], F32, name="gate_rest")
+        nc.sync.dma_start(gate_rest[:], gate[:, :, TURNED:].rearrange("d p v -> p d v"))
         w2_codes = keep.tile([P, N], U32, name="w2_codes", align_bytes=64)
         nc.sync.dma_start(w2_codes[:].bitcast(I32), w2_words[0].rearrange("p n t -> p (n t)").bitcast(I32))
         for q in range(4):
@@ -85,114 +95,173 @@ def tile_picked_hop2_relu_e_kernel(
         picked_words = {}
         picked_scales = [keep.tile([P, BANK], U8, name="picked_scales_%d" % s, align_bytes=64) for s in range(2)]
 
-        def round_chunk(g, c0, width):
-            grouped = keep.tile([P, width * PACK], BF16, name="x_grouped_%d_%d" % (g, c0), align_bytes=64)
-            src = x_raw[g, c0][:].rearrange("p j (c i) -> p c j i", i=LINE)
-            dst = grouped[:].rearrange("p (c i j) -> p c j i", i=LINE, j=PACK)
-            split = SCALAR_SHARE[width] // LINE
-            nc.scalar.activation(dst[:, :split], src[:, :split], COPY)
-            nc.vector.tensor_copy(dst[:, split:], src[:, split:])
-            return grouped
-
-        def quantize_chunk(g, c0, width, grouped):
-            nc.vector.quantize_mx(
-                out=x_words[g][:, c0 : c0 + width].bitcast(FP8X4),
-                scales=x_scales[4 * g :, c0 : c0 + width],
-                in_=grouped[:],
-            )
-
-        def pick_words(g, s, tag):
-            picked_words[g, s] = keep.tile([P, BANK], U32, name="picked_words_%d_%d" % (g, s), tag=tag, align_bytes=64)
-            nc.vector.tensor_copy(picked_words[g, s][:], x_words[g][:].indirect(entries(offs_tile, s * BANK, BANK)))
+        def pick_words(g, tag):
+            picked_words[g] = keep.tile([P, S], U32, name="picked_words_%d" % g, tag=tag, align_bytes=64)
+            for s in range(2):
+                nc.vector.tensor_copy(
+                    picked_words[g][:, s * BANK : (s + 1) * BANK],
+                    x_words[g][:].indirect(entries(offs_tile, s * BANK, BANK)),
+                )
 
         def pick_scales(s):
             nc.vector.tensor_copy(picked_scales[s][:], x_scales[:].indirect(entries(offs_tile, s * BANK, BANK)))
 
-        for g in range(PASSES):
-            c0 = 0
-            for index, width in enumerate(X_CHUNKS[g]):
-                quantize_chunk(g, c0, width, round_chunk(g, c0, width))
-                if g == 1 and index < 2:
-                    pick_words(0, index, "picked_0_%d" % index)
-                c0 = c0 + width
-
-        w_grouped = [keep.tile([P, H * PACK], BF16, name="w_grouped_%d" % g, tag="w_grouped_%d" % g, align_bytes=64) for g in range(PASSES)]
-        w_codes = [keep.tile([P, H], U32, name="w_codes_%d" % g, align_bytes=64) for g in range(PASSES)]
-        w_scales = [keep.tile([P, H], U8, name="w_scales_%d" % g, align_bytes=64) for g in range(PASSES)]
-        for g in range(PASSES):
-            dst = w_grouped[g][:].rearrange("p (t m j) -> p m j t", t=PACK, j=PACK)
-            for c0 in range(0, H, W_CHUNK):
-                src = w_raw[g, c0][:].rearrange("p j (m t) -> p m j t", t=PACK)
-                nc.scalar.activation(dst[:, c0 // PACK : (c0 + W_CHUNK) // PACK], src, COPY)
-
-        def quantize_w(g, c0, width):
+        for g, c0, nodes, share, raw in x_blocks:
+            grouped = keep.tile([P, nodes * PACK], BF16, name="x_grouped_%d_%d" % (g, c0), align_bytes=64)
+            src = raw.rearrange("p j (c i) -> p c j i", i=LINE)
+            dst = grouped[:].rearrange("p (c i j) -> p c j i", i=LINE, j=PACK)
+            split = share // LINE
+            if share > 0:
+                nc.scalar.activation(dst[:, :split], src[:, :split], COPY)
+            if share < nodes:
+                nc.vector.tensor_copy(dst[:, split:], src[:, split:])
             nc.vector.quantize_mx(
-                out=w_codes[g][:, c0 : c0 + width].bitcast(FP8X4),
-                scales=w_scales[g][:, c0 : c0 + width],
-                in_=w_grouped[g][:, PACK * c0 : PACK * (c0 + width)],
+                out=x_words[g][:, c0 : c0 + nodes].bitcast(FP8X4),
+                scales=x_scales[4 * g :, c0 : c0 + nodes],
+                in_=grouped[:],
             )
+            if g == 0 and c0 + nodes == T:
+                pick_words(0, "picked_0")
 
+        w_grouped, w_codes, w_scales = {}, {}, {}
+
+        def round_w(g, u, tag, on_scalar):
+            w_grouped[g, u] = keep.tile([P, 2 * P * PACK], BF16, name="w_grouped_%d_%d" % (g, u), tag=tag, align_bytes=64)
+            dst = w_grouped[g, u][:].rearrange("p (e m j) -> p m j e", e=2, j=PACK)
+            src = w_raw[g][:].rearrange("p j (m t) -> p m j t", t=PACK)[:, :, :, 2 * u : 2 * u + 2]
+            if on_scalar:
+                nc.scalar.activation(dst, src, COPY)
+            else:
+                nc.vector.tensor_copy(dst, src)
+
+        def quantize_w(g, u, tag):
+            w_codes[g, u] = keep.tile([P, 2 * P], U32, name="w_codes_%d_%d" % (g, u), tag=tag, align_bytes=64)
+            w_scales[g, u] = keep.tile([P, 2 * P], U8, name="w_scales_%d_%d" % (g, u), align_bytes=64)
+            nc.vector.quantize_mx(out=w_codes[g, u][:].bitcast(FP8X4), scales=w_scales[g, u][:], in_=w_grouped[g, u][:])
+
+        round_w(0, 0, "after_w00", True)
+        round_w(0, 1, "w_grouped_0_1", True)
+        round_w(1, 0, "after_w10", True)
         pick_scales(0)
         pick_scales(1)
-        pick_words(1, 0, "picked_1_0")
-        quantize_w(0, 0, H)
-        pick_words(1, 1, "w_grouped_0")
-        quantize_w(1, 0, P)
-        quantize_w(1, P, P)
-        quantize_w(1, 2 * P, 2 * P)
+        quantize_w(0, 0, "w_codes_0_0")
+        pick_words(1, "after_w00")
+        quantize_w(1, 0, "w_codes_1_0")
+        round_w(1, 1, "after_w10", False)
+        quantize_w(1, 1, "w_codes_1_1")
+        quantize_w(0, 1, "after_w10")
 
-        h_banks = [[psum.tile([P, BANK], F32, name="bank") for s in range(2)] for t in range(PACK)]
+        h_tiles = []
         for t in range(PACK):
+            banks = [bank(2 * t + s, "h_bank_%d_%d" % (t, s)) for s in range(2)]
+            cols = slice((t % 2) * P, (t % 2 + 1) * P)
             for g in range(PASSES):
                 for s in range(2):
                     nc.tensor.matmul_mx(
-                        out=h_banks[t][s][:],
-                        lhsT=w_codes[g][:, t * P : (t + 1) * P].bitcast(FP8X4),
-                        lhsT_scale=w_scales[g][:, t * P : (t + 1) * P],
-                        rhs=picked_words[g, s][:].bitcast(FP8X4),
+                        out=banks[s][:],
+                        lhsT=w_codes[g, t // 2][:, cols].bitcast(FP8X4),
+                        lhsT_scale=w_scales[g, t // 2][:, cols],
+                        rhs=picked_words[g][:, s * BANK : (s + 1) * BANK].bitcast(FP8X4),
                         rhs_scale=picked_scales[s][4 * g :, :],
                         start=(g == 0),
                         stop=(g == PASSES - 1),
                     )
-
-        terms = [keep.tile([P, PACK, V], F32, name="term_%d" % d) for d in range(2)]
-        for t in range(PACK):
             h = keep.tile([P, S], F32, name="h_%d" % t)
             for s in range(2):
-                nc.scalar.activation(h[:, s * BANK : (s + 1) * BANK], h_banks[t][s][:], RELU)
-            for d in range(2):
-                nc.vector.tensor_tensor(terms[d][:, t, :], h[:].indirect(pos_tiles[d][:]), gate_tile[:, d, :], MULT)
+                nc.scalar.activation(h[:, s * BANK : (s + 1) * BANK], banks[s][:], RELU)
+            h_tiles.append(h)
 
-        half = V // 2
-        z_grouped = [keep.tile([P, half * PACK], BF16, name="z_grouped_%d" % s, align_bytes=64) for s in range(2)]
-        z_codes = [keep.tile([P, half], U32, name="z_codes_%d" % s, align_bytes=64) for s in range(2)]
-        z_scales = [keep.tile([P, half], U8, name="z_scales_%d" % s, align_bytes=64) for s in range(2)]
-        for s in range(2):
-            a, b = [
-                term[:, :, s * half : (s + 1) * half].rearrange("p t (c i) -> p c t i", i=LINE) for term in terms
-            ]
-            nc.vector.tensor_tensor(z_grouped[s][:].rearrange("p (c i t) -> p c t i", i=LINE, t=PACK), a, b, ADD)
-        for s in range(2):
-            nc.vector.quantize_mx(out=z_codes[s][:].bitcast(FP8X4), scales=z_scales[s][:], in_=z_grouped[s][:])
+        blocks = TURNED // P
+        pieces = ((0, 2 * P), (2 * P, P), (TURNED, V - TURNED))
+        sum_banks = [bank(b, "sum_bank_%d" % b) for b in range(blocks)]
+        back_banks = [bank(blocks + index, "back_bank_%d" % index) for index in range(2)]
+        for t in range(PACK):
+            terms = [keep.tile([P, TURNED], F32, name="term_%d_%d" % (t, d)) for d in range(2)]
+            for d in range(2):
+                nc.vector.tensor_tensor(
+                    terms[d][:], h_tiles[t][:].indirect(entries(pos_tiles[d], 0, TURNED)), gate_turned[:, d, :], MULT
+                )
+            for b in range(blocks):
+                for d in range(2):
+                    nc.tensor.matmul(
+                        sum_banks[b][:, t * P : (t + 1) * P],
+                        terms[d][:, b * P : (b + 1) * P],
+                        identity[:],
+                        start=(d == 0),
+                        stop=(d == 1),
+                        is_transpose=True,
+                    )
+            if t % 2 == 1:
+                u = t // 2
+                for b in range(blocks):
+                    pairs = keep.tile([P, 2 * P], BF16, name="pairs_%d_%d" % (u, b))
+                    nc.scalar.activation(
+                        pairs[:].rearrange("v (p e) -> v p e", e=2),
+                        sum_banks[b][:, 2 * u * P : (2 * u + 2) * P].rearrange("v (e p) -> v p e", e=2),
+                        COPY,
+                    )
+                    first, width = pieces[b // 2]
+                    start = u * width + b * P - first
+                    nc.tensor.transpose(back_banks[b // 2][:, start : start + P], pairs[:].bitcast(F32), identity[:])
+
+        z_grouped = [
+            keep.tile([P, width * PACK], BF16, name="z_grouped_%d" % first, align_bytes=64) for first, width in pieces
+        ]
+        for index in range(2):
+            width = pieces[index][1]
+            nc.scalar.copy(
+                z_grouped[index][:].bitcast(F32).rearrange("p (v u) -> p v u", u=2),
+                back_banks[index][:, : 2 * width].rearrange("p (u v) -> p v u", u=2),
+            )
+
+        rest = V - TURNED
+        rest_terms = keep.tile([P, 2, PACK, rest], F32, name="rest_terms", tag="gate_turned")
+        for t in range(PACK):
+            for d in range(2):
+                nc.vector.tensor_tensor(
+                    rest_terms[:, d, t, :],
+                    h_tiles[t][:].indirect(entries(pos_tiles[d], TURNED, rest)),
+                    gate_rest[:, d, :],
+                    MULT,
+                )
+        nc.vector.tensor_tensor(
+            z_grouped[2][:].rearrange("p (c i t) -> p c t i", i=LINE, t=PACK),
+            rest_terms[:, 0].rearrange("p t (c i) -> p c t i", i=LINE),
+            rest_terms[:, 1].rearrange("p t (c i) -> p c t i", i=LINE),
+            ADD,
+        )
+        z_codes, z_scales = [], []
+        for index, (first, width) in enumerate(pieces):
+            z_codes.append(keep.tile([P, width], U32, name="z_codes_%d" % first, align_bytes=64))
+            z_scales.append(keep.tile([P, width], U8, name="z_scales_%d" % first, align_bytes=64))
+            nc.vector.quantize_mx(out=z_codes[index][:].bitcast(FP8X4), scales=z_scales[index][:], in_=z_grouped[index][:])
+
+        def second_product(target, m, index):
+            nc.tensor.matmul_mx(
+                out=target,
+                lhsT=w2_codes[:, m * P : (m + 1) * P].bitcast(FP8X4),
+                lhsT_scale=w2_scale_tile[:, m * P : (m + 1) * P],
+                rhs=z_codes[index][:].bitcast(FP8X4),
+                rhs_scale=z_scales[index][:],
+                start=True,
+                stop=True,
+            )
+
+        g_tiles = [keep.tile([P, V], F32, name="g_%d" % m) for m in range(N // P)]
+        for index, (first, width) in enumerate(pieces):
+            piece_bank = bank(5 + index, "g_bank_0_%d" % index)
+            second_product(piece_bank[:, :width], 0, index)
+            nc.scalar.activation(g_tiles[0][:, first : first + width], piece_bank[:, :width], RELU)
+        whole_bank = bank(0, "g_bank_1")
+        for index, (first, width) in enumerate(pieces):
+            second_product(whole_bank[:, first : first + width], 1, index)
+        nc.scalar.activation(g_tiles[1][:], whole_bank[:], RELU)
 
         for m in range(N // P):
-            g_tile = keep.tile([P, V], F32, name="g_%d" % m)
-            for s in range(2):
-                bank = psum.tile([P, BANK], F32, name="bank")
-                nc.tensor.matmul_mx(
-                    out=bank[:, :half],
-                    lhsT=w2_codes[:, m * P : (m + 1) * P].bitcast(FP8X4),
-                    lhsT_scale=w2_scale_tile[:, m * P : (m + 1) * P],
-                    rhs=z_codes[s][:].bitcast(FP8X4),
-                    rhs_scale=z_scales[s][:],
-                    start=True,
-                    stop=True,
-                )
-                nc.scalar.activation(g_tile[:, s * half : (s + 1) * half], bank[:, :half], RELU)
             root_terms = [keep.tile([P, U], F32, name="root_term_%d_%d" % (m, d)) for d in range(2)]
             for d in range(2):
                 nc.vector.tensor_tensor(
-                    root_terms[d][:], g_tile[:].indirect(nxt_tiles[d][:]), gate2_tile[:, d, :], MULT
+                    root_terms[d][:], g_tiles[m][:].indirect(nxt_tiles[d][:]), gate2_tile[:, d, :], MULT
                 )
             result = keep.tile([P, U], F32, name="result_%d" % m)
             nc.vector.tensor_tensor(result[:], root_terms[0][:], root_terms[1][:], ADD)

@@ -25,11 +25,15 @@ PASSES = K // K_PASS
 LIST_ROWS = 16
 LINE = 4
 BANK = 512
-X_LOADS = (
-    (((512, 0), (512, 384)), ((512, 256),), ((512, 256),)),
-    (((512, 0), (512, 384)), ((512, 320),), ((256, 128),), ((256, 96),)),
-)
+QUADRANT = 32
+SCALE_ROWS = 4
+
+LOAD_NODES = ((1024, 512, 256, 256), (512, 512, 256, 256, 256, 128, 128))
+BLOCK_NODES = 512
+SCALAR_NODES = {(1, 0): 384, (1, 512): 320}
+ENTRY_PIECES = ((0, 512), (512, 256), (768, 256))
 TURNED = 384
+Z_PIECES = ((0, 256), (256, 128), (TURNED, V - TURNED))
 
 
 def tile_picked_hop2_relu_e_kernel(
@@ -45,8 +49,8 @@ def tile_picked_hop2_relu_e_kernel(
             nc.sync.dma_start(tile[:], source)
             return tile
 
-        def entries(tile, start, count):
-            return tile[:, start // LIST_ROWS : (start + count) // LIST_ROWS]
+        def entries(tile, first, count):
+            return tile[:, first // LIST_ROWS : (first + count) // LIST_ROWS]
 
         def bank(number, name):
             return psum.tile([P, BANK], F32, name=name, tag="bank_%d" % number)
@@ -61,21 +65,22 @@ def tile_picked_hop2_relu_e_kernel(
         x_blocks = []
         for g in range(PASSES):
             rows = xT[g * K_PASS : (g + 1) * K_PASS, :].rearrange("(p j) c -> p j c", j=PACK)
-            c0 = 0
-            for blocks in X_LOADS[g]:
-                width = sum(nodes for nodes, share in blocks)
-                raw = keep.tile([P, PACK, width], F32, name="x_raw_%d_%d" % (g, c0))
-                nc.sync.dma_start(raw[:], rows[:, :, c0 : c0 + width])
-                first = 0
-                for nodes, share in blocks:
-                    x_blocks.append((g, c0 + first, nodes, share, raw[:, :, first : first + nodes]))
-                    first = first + nodes
-                c0 = c0 + width
+            load_first = 0
+            for load_nodes in LOAD_NODES[g]:
+                raw = keep.tile([P, PACK, load_nodes], F32, name="x_raw_%d_%d" % (g, load_first))
+                nc.sync.dma_start(raw[:], rows[:, :, load_first : load_first + load_nodes])
+                nodes = min(load_nodes, BLOCK_NODES)
+                for start in range(0, load_nodes, nodes):
+                    x_blocks.append((g, load_first + start, nodes, raw[:, :, start : start + nodes]))
+                load_first = load_first + load_nodes
             if g == 0:
                 offs_tile = load_list("offs_tile", offs)
-        w_raw = [keep.tile([P, PACK, H], F32, name="w_raw_%d" % g) for g in range(PASSES)]
+        w_raw = {}
         for g in range(PASSES):
-            nc.sync.dma_start(w_raw[g][:], w1[g * K_PASS : (g + 1) * K_PASS, :].rearrange("(p j) c -> p j c", j=PACK))
+            rows = w1[g * K_PASS : (g + 1) * K_PASS, :].rearrange("(p j) c -> p j c", j=PACK)
+            for half in range(2):
+                w_raw[g, half] = keep.tile([P, PACK, H // 2], F32, name="w_raw_%d_%d" % (g, half))
+                nc.sync.dma_start(w_raw[g, half][:], rows[:, :, half * (H // 2) : (half + 1) * (H // 2)])
         pos_tiles = [load_list("pos1_tile", pos1), load_list("pos2_tile", pos2)]
         gate_turned = keep.tile([P, 2, TURNED], F32, name="gate_turned", tag="gate_turned")
         nc.sync.dma_start(gate_turned[:], gate[:, :, :TURNED].rearrange("d p v -> p d v"))
@@ -83,106 +88,116 @@ def tile_picked_hop2_relu_e_kernel(
         nc.sync.dma_start(gate_rest[:], gate[:, :, TURNED:].rearrange("d p v -> p d v"))
         w2_codes = keep.tile([P, N], U32, name="w2_codes", align_bytes=64)
         nc.sync.dma_start(w2_codes[:].bitcast(I32), w2_words[0].rearrange("p n t -> p (n t)").bitcast(I32))
-        for q in range(4):
+        for q in range(P // QUADRANT):
             nc.sync.dma_start(
-                w2_scale_tile[32 * q : 32 * q + 4, :].bitcast(I32), w2_scales[0, 4 * q : 4 * q + 4, :].bitcast(I32)
+                w2_scale_tile[QUADRANT * q : QUADRANT * q + SCALE_ROWS, :].bitcast(I32),
+                w2_scales[0, SCALE_ROWS * q : SCALE_ROWS * (q + 1), :].bitcast(I32),
             )
         nxt_tiles = [load_list("nxt1_tile", nxt1), load_list("nxt2_tile", nxt2)]
-        gate2_tile = keep.tile([P, 2, U], F32, name="gate2_tile")
+        gate2_tile = keep.tile([P, 2, U], F32, name="gate2_tile", tag="gate2_tile")
         nc.sync.dma_start(gate2_tile[:], gate2.rearrange("d p v -> p d v"))
 
-        x_words = [keep.tile([P, T], U32, name="x_words_%d" % g, align_bytes=64) for g in range(PASSES)]
+        x_words = [
+            keep.tile([P, T], U32, name="x_words_%d" % g, tag="x_words_%d" % g, align_bytes=64) for g in range(PASSES)
+        ]
         picked_words = {}
-        picked_scales = [keep.tile([P, BANK], U8, name="picked_scales_%d" % s, align_bytes=64) for s in range(2)]
+        picked_scales = keep.tile([P, S], U8, name="picked_scales", align_bytes=64)
 
-        def pick_words(g, tag):
-            picked_words[g] = keep.tile([P, S], U32, name="picked_words_%d" % g, tag=tag, align_bytes=64)
-            for s in range(2):
-                nc.vector.tensor_copy(
-                    picked_words[g][:, s * BANK : (s + 1) * BANK],
-                    x_words[g][:].indirect(entries(offs_tile, s * BANK, BANK)),
-                )
+        def pick(target, window, first):
+            nc.vector.tensor_copy(target, window[:].indirect(entries(offs_tile, first, target.shape[1])))
 
-        def pick_scales(s):
-            nc.vector.tensor_copy(picked_scales[s][:], x_scales[:].indirect(entries(offs_tile, s * BANK, BANK)))
+        def picked_tile(name, count, tag):
+            return keep.tile([P, count], U32, name=name, tag=tag, align_bytes=64)
 
-        for g, c0, nodes, share, raw in x_blocks:
-            grouped = keep.tile([P, nodes * PACK], BF16, name="x_grouped_%d_%d" % (g, c0), align_bytes=64)
+        for g, first, nodes, raw in x_blocks:
+            grouped = keep.tile([P, nodes * PACK], BF16, name="x_grouped_%d_%d" % (g, first), align_bytes=64)
             src = raw.rearrange("p j (c i) -> p c j i", i=LINE)
             dst = grouped[:].rearrange("p (c i j) -> p c j i", i=LINE, j=PACK)
-            split = share // LINE
-            if share > 0:
-                nc.scalar.activation(dst[:, :split], src[:, :split], COPY)
-            if share < nodes:
-                nc.vector.tensor_copy(dst[:, split:], src[:, split:])
+            split = SCALAR_NODES.get((g, first), nodes // 2) // LINE
+            nc.scalar.activation(dst[:, :split], src[:, :split], COPY)
+            nc.vector.tensor_copy(dst[:, split:], src[:, split:])
             nc.vector.quantize_mx(
-                out=x_words[g][:, c0 : c0 + nodes].bitcast(FP8X4),
-                scales=x_scales[4 * g :, c0 : c0 + nodes],
+                out=x_words[g][:, first : first + nodes].bitcast(FP8X4),
+                scales=x_scales[SCALE_ROWS * g :, first : first + nodes],
                 in_=grouped[:],
             )
-            if g == 0 and c0 + nodes == T:
-                pick_words(0, "picked_0")
+            if g == 0 and first + nodes == T:
+                picked_first = picked_tile("picked_first", S, "picked_first")
+                pick(picked_first[:], x_words[0], 0)
+                for entry, count in ENTRY_PIECES:
+                    picked_words[0, entry] = picked_first[:, entry : entry + count]
 
         w_grouped, w_codes, w_scales = {}, {}, {}
-
-        def round_w(g, u, tag, on_scalar):
-            w_grouped[g, u] = keep.tile([P, 2 * P * PACK], BF16, name="w_grouped_%d_%d" % (g, u), tag=tag, align_bytes=64)
-            dst = w_grouped[g, u][:].rearrange("p (e m j) -> p m j e", e=2, j=PACK)
-            src = w_raw[g][:].rearrange("p j (m t) -> p m j t", t=PACK)[:, :, :, 2 * u : 2 * u + 2]
-            if on_scalar:
-                nc.scalar.activation(dst, src, COPY)
-            else:
-                nc.vector.tensor_copy(dst, src)
+        for g in range(PASSES):
+            for u in range(2):
+                name = "w_grouped_%d_%d" % (g, u)
+                w_grouped[g, u] = keep.tile([P, 2 * P * PACK], BF16, name=name, tag=name, align_bytes=64)
+            for half in range(2):
+                for u in range(2):
+                    dst = w_grouped[g, u][:].rearrange("p (e m j) -> p m j e", e=2, j=PACK)
+                    src = w_raw[g, half][:].rearrange("p j (m t) -> p m j t", t=PACK)
+                    nc.scalar.activation(
+                        dst[:, half * (P // 2) : (half + 1) * (P // 2)], src[:, :, :, 2 * u : 2 * u + 2], COPY
+                    )
 
         def quantize_w(g, u, tag):
             w_codes[g, u] = keep.tile([P, 2 * P], U32, name="w_codes_%d_%d" % (g, u), tag=tag, align_bytes=64)
             w_scales[g, u] = keep.tile([P, 2 * P], U8, name="w_scales_%d_%d" % (g, u), align_bytes=64)
             nc.vector.quantize_mx(out=w_codes[g, u][:].bitcast(FP8X4), scales=w_scales[g, u][:], in_=w_grouped[g, u][:])
 
-        round_w(0, 0, "after_w00", True)
-        round_w(0, 1, "w_grouped_0_1", True)
-        round_w(1, 0, "after_w10", True)
-        pick_scales(0)
-        pick_scales(1)
+        (first_0, count_0), (first_1, count_1), (first_2, count_2) = ENTRY_PIECES
+        pick(picked_scales[:], x_scales, 0)
         quantize_w(0, 0, "w_codes_0_0")
-        pick_words(1, "after_w00")
+        picked_most = picked_tile("picked_most", count_0 + count_1, "w_grouped_0_0")
+        for entry, count in ENTRY_PIECES[:2]:
+            picked_words[1, entry] = picked_most[:, entry : entry + count]
+            pick(picked_words[1, entry], x_words[1], entry)
         quantize_w(1, 0, "w_codes_1_0")
-        round_w(1, 1, "after_w10", False)
+        picked_last = picked_tile("picked_last", count_2, "w_grouped_1_0")
+        picked_words[1, first_2] = picked_last[:]
+        pick(picked_last[:], x_words[1], first_2)
+        quantize_w(0, 1, "x_words_1")
         quantize_w(1, 1, "w_codes_1_1")
-        quantize_w(0, 1, "after_w10")
 
-        h_tiles = []
-        for t in range(PACK):
-            banks = [bank(2 * t + s, "h_bank_%d_%d" % (t, s)) for s in range(2)]
+        def first_product(target, t, g, entry):
             cols = slice((t % 2) * P, (t % 2 + 1) * P)
-            for g in range(PASSES):
-                for s in range(2):
-                    nc.tensor.matmul_mx(
-                        out=banks[s][:],
-                        lhsT=w_codes[g, t // 2][:, cols].bitcast(FP8X4),
-                        lhsT_scale=w_scales[g, t // 2][:, cols],
-                        rhs=picked_words[g][:, s * BANK : (s + 1) * BANK].bitcast(FP8X4),
-                        rhs_scale=picked_scales[s][4 * g :, :],
-                        start=(g == 0),
-                        stop=(g == PASSES - 1),
-                    )
-            h = keep.tile([P, S], F32, name="h_%d" % t)
-            for s in range(2):
-                nc.scalar.activation(h[:, s * BANK : (s + 1) * BANK], banks[s][:], RELU)
-            h_tiles.append(h)
+            nc.tensor.matmul_mx(
+                out=target,
+                lhsT=w_codes[g, t // 2][:, cols].bitcast(FP8X4),
+                lhsT_scale=w_scales[g, t // 2][:, cols],
+                rhs=picked_words[g, entry].bitcast(FP8X4),
+                rhs_scale=picked_scales[SCALE_ROWS * g :, entry : entry + target.shape[1]],
+                start=(g == 0),
+                stop=(g == PASSES - 1),
+            )
+
+        h_tiles = [keep.tile([P, S], F32, name="h_%d" % t) for t in range(PACK)]
+        h_banks = [bank(index, "h_bank_0_%d" % index) for index in range(len(ENTRY_PIECES))]
+        for g in range(PASSES):
+            for index, (entry, count) in enumerate(ENTRY_PIECES):
+                first_product(h_banks[index][:, :count], 0, g, entry)
+        nc.scalar.activation(h_tiles[0][:, first_0 : first_0 + count_0], h_banks[0][:, :count_0], RELU)
+        nc.scalar.activation(h_tiles[0][:, first_1 : first_1 + count_1], h_banks[1][:, :count_1], RELU)
+        nc.vector.tensor_scalar_max(h_tiles[0][:, first_2:], h_banks[2][:, :count_2], 0.0)
+        for t in range(1, PACK):
+            h_banks = [bank(3 * (t % 2) + s, "h_bank_%d_%d" % (t, s)) for s in range(S // BANK)]
+            for entry, count in ENTRY_PIECES:
+                for g in range(PASSES):
+                    first_product(h_banks[entry // BANK][:, entry % BANK : entry % BANK + count], t, g, entry)
+            for s in range(S // BANK):
+                nc.scalar.activation(h_tiles[t][:, s * BANK : (s + 1) * BANK], h_banks[s][:], RELU)
 
         blocks = TURNED // P
-        pieces = ((0, 2 * P), (2 * P, P), (TURNED, V - TURNED))
-        sum_banks = [bank(b, "sum_bank_%d" % b) for b in range(blocks)]
-        back_banks = [bank(blocks + index, "back_bank_%d" % index) for index in range(2)]
+        sum_banks = [bank(5 + b, "sum_bank_%d" % b) for b in range(blocks)]
+        back_banks = [bank(2, "back_bank_0"), bank(0, "back_bank_1")]
         for t in range(PACK):
             terms = [keep.tile([P, TURNED], F32, name="term_%d_%d" % (t, d)) for d in range(2)]
             for d in range(2):
                 nc.vector.tensor_tensor(
                     terms[d][:], h_tiles[t][:].indirect(entries(pos_tiles[d], 0, TURNED)), gate_turned[:, d, :], MULT
                 )
-            for b in range(blocks):
-                for d in range(2):
+            for d in range(2):
+                for b in range(blocks):
                     nc.tensor.matmul(
                         sum_banks[b][:, t * P : (t + 1) * P],
                         terms[d][:, b * P : (b + 1) * P],
@@ -200,15 +215,16 @@ def tile_picked_hop2_relu_e_kernel(
                         sum_banks[b][:, 2 * u * P : (2 * u + 2) * P].rearrange("v (e p) -> v p e", e=2),
                         COPY,
                     )
-                    first, width = pieces[b // 2]
-                    start = u * width + b * P - first
+                    column, width = Z_PIECES[b // 2]
+                    start = u * width + b * P - column
                     nc.tensor.transpose(back_banks[b // 2][:, start : start + P], pairs[:].bitcast(F32), identity[:])
 
         z_grouped = [
-            keep.tile([P, width * PACK], BF16, name="z_grouped_%d" % first, align_bytes=64) for first, width in pieces
+            keep.tile([P, width * PACK], BF16, name="z_grouped_%d" % column, tag="z_grouped_%d" % column, align_bytes=64)
+            for column, width in Z_PIECES[:2]
         ]
         for index in range(2):
-            width = pieces[index][1]
+            width = Z_PIECES[index][1]
             nc.scalar.copy(
                 z_grouped[index][:].bitcast(F32).rearrange("p (v u) -> p v u", u=2),
                 back_banks[index][:, : 2 * width].rearrange("p (u v) -> p v u", u=2),
@@ -224,17 +240,24 @@ def tile_picked_hop2_relu_e_kernel(
                     gate_rest[:, d, :],
                     MULT,
                 )
+        z_codes, z_scales = {}, {}
+
+        def quantize_z(index, tag):
+            column, width = Z_PIECES[index]
+            z_codes[index] = keep.tile([P, width], U32, name="z_codes_%d" % column, tag=tag, align_bytes=64)
+            z_scales[index] = keep.tile([P, width], U8, name="z_scales_%d" % column, align_bytes=64)
+            nc.vector.quantize_mx(out=z_codes[index][:].bitcast(FP8X4), scales=z_scales[index][:], in_=z_grouped[index][:])
+
+        quantize_z(0, "z_codes_0")
+        z_grouped.append(keep.tile([P, rest * PACK], BF16, name="z_grouped_rest", tag="z_grouped_0", align_bytes=64))
         nc.vector.tensor_tensor(
             z_grouped[2][:].rearrange("p (c i t) -> p c t i", i=LINE, t=PACK),
             rest_terms[:, 0].rearrange("p t (c i) -> p c t i", i=LINE),
             rest_terms[:, 1].rearrange("p t (c i) -> p c t i", i=LINE),
             ADD,
         )
-        z_codes, z_scales = [], []
-        for index, (first, width) in enumerate(pieces):
-            z_codes.append(keep.tile([P, width], U32, name="z_codes_%d" % first, align_bytes=64))
-            z_scales.append(keep.tile([P, width], U8, name="z_scales_%d" % first, align_bytes=64))
-            nc.vector.quantize_mx(out=z_codes[index][:].bitcast(FP8X4), scales=z_scales[index][:], in_=z_grouped[index][:])
+        quantize_z(1, "z_codes_1")
+        quantize_z(2, "z_grouped_%d" % Z_PIECES[1][0])
 
         def second_product(target, m, index):
             nc.tensor.matmul_mx(
@@ -248,21 +271,23 @@ def tile_picked_hop2_relu_e_kernel(
             )
 
         g_tiles = [keep.tile([P, V], F32, name="g_%d" % m) for m in range(N // P)]
-        for index, (first, width) in enumerate(pieces):
-            piece_bank = bank(5 + index, "g_bank_0_%d" % index)
+        for index, number in enumerate((1, 3, 4)):
+            column, width = Z_PIECES[index]
+            piece_bank = bank(number, "g_bank_0_%d" % index)
             second_product(piece_bank[:, :width], 0, index)
-            nc.scalar.activation(g_tiles[0][:, first : first + width], piece_bank[:, :width], RELU)
-        whole_bank = bank(0, "g_bank_1")
-        for index, (first, width) in enumerate(pieces):
-            second_product(whole_bank[:, first : first + width], 1, index)
+            nc.scalar.activation(g_tiles[0][:, column : column + width], piece_bank[:, :width], RELU)
+        whole_bank = bank(5, "g_bank_1")
+        for index, (column, width) in enumerate(Z_PIECES):
+            second_product(whole_bank[:, column : column + width], 1, index)
         nc.scalar.activation(g_tiles[1][:], whole_bank[:], RELU)
 
+        root_terms = keep.tile([P, N // P, 2, U], F32, name="root_terms")
         for m in range(N // P):
-            root_terms = [keep.tile([P, U], F32, name="root_term_%d_%d" % (m, d)) for d in range(2)]
             for d in range(2):
                 nc.vector.tensor_tensor(
-                    root_terms[d][:], g_tiles[m][:].indirect(nxt_tiles[d][:]), gate2_tile[:, d, :], MULT
+                    root_terms[:, m, d, :], g_tiles[m][:].indirect(nxt_tiles[d][:]), gate2_tile[:, d, :], MULT
                 )
-            result = keep.tile([P, U], F32, name="result_%d" % m)
-            nc.vector.tensor_tensor(result[:], root_terms[0][:], root_terms[1][:], ADD)
-            nc.sync.dma_start(out[m * P : (m + 1) * P, :], result[:])
+        result = keep.tile([P, N // P, U], F32, name="result", tag="gate2_tile")
+        for m in range(N // P):
+            nc.vector.tensor_tensor(result[:, m, :], root_terms[:, m, 0, :], root_terms[:, m, 1, :], ADD)
+            nc.sync.dma_start(out[m * P : (m + 1) * P, :], result[:, m, :])

@@ -28,9 +28,9 @@ BANK = 512
 QUADRANT = 32
 SCALE_ROWS = 4
 
-LOAD_NODES = ((1024, 512, 256, 256), (512, 512, 256, 256, 256, 128, 128))
+LOAD_NODES = ((1024, 512, 512), (1024, 512, 256, 256))
 BLOCK_NODES = 512
-SCALAR_NODES = {(1, 0): 384, (1, 512): 320}
+SCALAR_SIXTEENTHS = 9
 ENTRY_PIECES = ((0, 512), (512, 256), (768, 256))
 TURNED = 384
 Z_PIECES = ((0, 256), (256, 128), (TURNED, V - TURNED))
@@ -75,12 +75,9 @@ def tile_picked_hop2_relu_e_kernel(
                 load_first = load_first + load_nodes
             if g == 0:
                 offs_tile = load_list("offs_tile", offs)
-        w_raw = {}
+        w_raw = [keep.tile([P, PACK, H], F32, name="w_raw_%d" % g) for g in range(PASSES)]
         for g in range(PASSES):
-            rows = w1[g * K_PASS : (g + 1) * K_PASS, :].rearrange("(p j) c -> p j c", j=PACK)
-            for half in range(2):
-                w_raw[g, half] = keep.tile([P, PACK, H // 2], F32, name="w_raw_%d_%d" % (g, half))
-                nc.sync.dma_start(w_raw[g, half][:], rows[:, :, half * (H // 2) : (half + 1) * (H // 2)])
+            nc.sync.dma_start(w_raw[g][:], w1[g * K_PASS : (g + 1) * K_PASS, :].rearrange("(p j) c -> p j c", j=PACK))
         pos_tiles = [load_list("pos1_tile", pos1), load_list("pos2_tile", pos2)]
         gate_turned = keep.tile([P, 2, TURNED], F32, name="gate_turned", tag="gate_turned")
         nc.sync.dma_start(gate_turned[:], gate[:, :, :TURNED].rearrange("d p v -> p d v"))
@@ -113,7 +110,7 @@ def tile_picked_hop2_relu_e_kernel(
             grouped = keep.tile([P, nodes * PACK], BF16, name="x_grouped_%d_%d" % (g, first), align_bytes=64)
             src = raw.rearrange("p j (c i) -> p c j i", i=LINE)
             dst = grouped[:].rearrange("p (c i j) -> p c j i", i=LINE, j=PACK)
-            split = SCALAR_NODES.get((g, first), nodes // 2) // LINE
+            split = nodes * SCALAR_SIXTEENTHS // 16 // LINE
             nc.scalar.activation(dst[:, :split], src[:, :split], COPY)
             nc.vector.tensor_copy(dst[:, split:], src[:, split:])
             nc.vector.quantize_mx(
@@ -132,13 +129,11 @@ def tile_picked_hop2_relu_e_kernel(
             for u in range(2):
                 name = "w_grouped_%d_%d" % (g, u)
                 w_grouped[g, u] = keep.tile([P, 2 * P * PACK], BF16, name=name, tag=name, align_bytes=64)
-            for half in range(2):
-                for u in range(2):
-                    dst = w_grouped[g, u][:].rearrange("p (e m j) -> p m j e", e=2, j=PACK)
-                    src = w_raw[g, half][:].rearrange("p j (m t) -> p m j t", t=PACK)
-                    nc.scalar.activation(
-                        dst[:, half * (P // 2) : (half + 1) * (P // 2)], src[:, :, :, 2 * u : 2 * u + 2], COPY
-                    )
+                nc.scalar.activation(
+                    w_grouped[g, u][:].rearrange("p (e m j) -> p m j e", e=2, j=PACK),
+                    w_raw[g][:].rearrange("p j (m t) -> p m j t", t=PACK)[:, :, :, 2 * u : 2 * u + 2],
+                    COPY,
+                )
 
         def quantize_w(g, u, tag):
             w_codes[g, u] = keep.tile([P, 2 * P], U32, name="w_codes_%d_%d" % (g, u), tag=tag, align_bytes=64)

@@ -28,9 +28,8 @@ BANK = 512
 QUADRANT = 32
 SCALE_ROWS = 4
 
-LOAD_NODES = ((1024, 512, 512), (1024, 512, 256, 256))
-BLOCK_NODES = 512
-SCALAR_SIXTEENTHS = 9
+LOAD_NODES = (((2048,), (1024, 1024)), ((1024, 1024), (1024, 512, 512)))
+SCALAR_SIXTEENTHS = (((6,), (16, 5)), ((16, 5), (16, 0, 8)))
 ENTRY_PIECES = ((0, 512), (512, 256), (768, 256))
 TURNED = 384
 Z_PIECES = ((0, 256), (256, 128), (TURNED, V - TURNED))
@@ -42,6 +41,7 @@ def tile_picked_hop2_relu_e_kernel(
     nc = tc.nc
     with ExitStack() as ctx:
         keep = ctx.enter_context(tc.tile_pool(name="keep", bufs=1))
+        shared = ctx.enter_context(tc.tile_pool(name="shared", bufs=1))
         psum = ctx.enter_context(tc.psum_pool(name="psum", bufs=1))
 
         def load_list(name, source):
@@ -55,34 +55,32 @@ def tile_picked_hop2_relu_e_kernel(
         def bank(number, name):
             return psum.tile([P, BANK], F32, name=name, tag="bank_%d" % number)
 
-        x_scales = keep.tile([P, T], U8, name="x_scales", align_bytes=64)
-        nc.vector.memset(x_scales[:].bitcast(I32), 0)
         w2_scale_tile = keep.tile([P, N], U8, name="w2_scale_tile", align_bytes=64)
         nc.vector.memset(w2_scale_tile[:].bitcast(I32), 0)
         identity = keep.tile([P, P], F32, name="identity")
         make_identity(nc, identity[:])
 
-        x_blocks = []
+        x_raw = {}
+        w_raw = [keep.tile([P, PACK, H], F32, name="w_raw_%d" % g) for g in range(PASSES)]
         for g in range(PASSES):
             rows = xT[g * K_PASS : (g + 1) * K_PASS, :].rearrange("(p j) c -> p j c", j=PACK)
-            load_first = 0
-            for load_nodes in LOAD_NODES[g]:
-                raw = keep.tile([P, PACK, load_nodes], F32, name="x_raw_%d_%d" % (g, load_first))
-                nc.sync.dma_start(raw[:], rows[:, :, load_first : load_first + load_nodes])
-                nodes = min(load_nodes, BLOCK_NODES)
-                for start in range(0, load_nodes, nodes):
-                    x_blocks.append((g, load_first + start, nodes, raw[:, :, start : start + nodes]))
-                load_first = load_first + load_nodes
-            if g == 0:
-                offs_tile = load_list("offs_tile", offs)
-        w_raw = [keep.tile([P, PACK, H], F32, name="w_raw_%d" % g) for g in range(PASSES)]
+            for u in range(2):
+                x_raw[g, u] = []
+                first = 0
+                for nodes in LOAD_NODES[g][u]:
+                    name = "x_raw_%d_%d_%d" % (g, u, first)
+                    raw = keep.tile([P, 2, nodes], F32, name=name, tag=name, align_bytes=64)
+                    nc.sync.dma_start(raw[:], rows[:, 2 * u : 2 * u + 2, first : first + nodes])
+                    x_raw[g, u].append((first, raw))
+                    first = first + nodes
+                if (g, u) == (0, 0):
+                    offs_tile = load_list("offs_tile", offs)
         for g in range(PASSES):
             nc.sync.dma_start(w_raw[g][:], w1[g * K_PASS : (g + 1) * K_PASS, :].rearrange("(p j) c -> p j c", j=PACK))
         pos_tiles = [load_list("pos1_tile", pos1), load_list("pos2_tile", pos2)]
-        gate_turned = keep.tile([P, 2, TURNED], F32, name="gate_turned", tag="gate_turned")
-        nc.sync.dma_start(gate_turned[:], gate[:, :, :TURNED].rearrange("d p v -> p d v"))
-        gate_rest = keep.tile([P, 2, V - TURNED], F32, name="gate_rest")
-        nc.sync.dma_start(gate_rest[:], gate[:, :, TURNED:].rearrange("d p v -> p d v"))
+        terms = keep.tile([P, 2, PACK, 2 * V], F32, name="terms", tag="terms", align_bytes=64)
+        gate_tile = terms[:, :, 2, TURNED : TURNED + V]
+        nc.sync.dma_start(gate_tile, gate.rearrange("d p v -> p d v"))
         w2_codes = keep.tile([P, N], U32, name="w2_codes", align_bytes=64)
         nc.sync.dma_start(w2_codes[:].bitcast(I32), w2_words[0].rearrange("p n t -> p (n t)").bitcast(I32))
         for q in range(P // QUADRANT):
@@ -94,65 +92,97 @@ def tile_picked_hop2_relu_e_kernel(
         gate2_tile = keep.tile([P, 2, U], F32, name="gate2_tile", tag="gate2_tile")
         nc.sync.dma_start(gate2_tile[:], gate2.rearrange("d p v -> p d v"))
 
-        x_words = [
-            keep.tile([P, T], U32, name="x_words_%d" % g, tag="x_words_%d" % g, align_bytes=64) for g in range(PASSES)
+        (first_0, count_0), (first_1, count_1), (first_2, count_2) = ENTRY_PIECES
+        halves = ((0, S // 2), (S // 2, S // 2))
+        picked_pairs = [
+            keep.tile([P, 2, S], U32, name="picked_pairs_%d" % g, tag="picked_pairs_%d" % g, align_bytes=64)
+            for g in range(PASSES)
         ]
-        picked_words = {}
-        picked_scales = keep.tile([P, S], U8, name="picked_scales", align_bytes=64)
+        picked_words = [keep.tile([P, S], U32, name="picked_words_%d" % g, align_bytes=64) for g in range(PASSES)]
+        picked_scales = [
+            keep.tile([P, S], U8, name="picked_scales_0", align_bytes=64),
+            shared.tile([P, S], U8, name="picked_scales_1", align_bytes=64, offset=0),
+        ]
+        x_grouped = {}
 
-        def pick(target, window, first):
-            nc.vector.tensor_copy(target, window[:].indirect(entries(offs_tile, first, target.shape[1])))
+        def round_and_pick(g, u, pieces, tag):
+            pairs = keep.tile([P, 2 * T], BF16, name="x_pairs_%d_%d" % (g, u), tag=tag, align_bytes=64)
+            for (first, raw), sixteenths in zip(x_raw[g, u], SCALAR_SIXTEENTHS[g][u]):
+                nodes = raw.shape[2]
+                src = raw[:].rearrange("p e c -> p c e")
+                dst = pairs[:, 2 * first : 2 * (first + nodes)].rearrange("p (c e) -> p c e", e=2)
+                split = nodes * sixteenths // 16
+                if split > 0:
+                    nc.scalar.activation(dst[:, :split], src[:, :split], COPY)
+                if split < nodes:
+                    nc.vector.tensor_copy(dst[:, split:], src[:, split:])
+            for entry, count in pieces:
+                nc.vector.tensor_copy(
+                    picked_pairs[g][:, u, entry : entry + count],
+                    pairs[:].bitcast(U32).indirect(entries(offs_tile, entry, count)),
+                )
 
-        def picked_tile(name, count, tag):
-            return keep.tile([P, count], U32, name=name, tag=tag, align_bytes=64)
+        def weave(g, entry, count, on_scalar, tag):
+            name = "x_grouped_%d_%d" % (g, entry)
+            if tag is None:
+                x_grouped[g, entry] = shared.tile([P, count * PACK], BF16, name=name, align_bytes=64, offset=S)
+            else:
+                x_grouped[g, entry] = keep.tile([P, count * PACK], BF16, name=name, tag=tag, align_bytes=64)
+            src = picked_pairs[g][:, :, entry : entry + count].rearrange("p u c -> p c u")
+            if on_scalar:
+                nc.scalar.copy(x_grouped[g, entry][:].bitcast(U32).rearrange("p (c u) -> p c u", u=2), src)
+            else:
+                nc.vector.tensor_copy(
+                    x_grouped[g, entry][:].bitcast(I32).rearrange("p (c u) -> p c u", u=2),
+                    picked_pairs[g][:].bitcast(I32)[:, :, entry : entry + count].rearrange("p u c -> p c u"),
+                )
 
-        for g, first, nodes, raw in x_blocks:
-            grouped = keep.tile([P, nodes * PACK], BF16, name="x_grouped_%d_%d" % (g, first), align_bytes=64)
-            src = raw.rearrange("p j (c i) -> p c j i", i=LINE)
-            dst = grouped[:].rearrange("p (c i j) -> p c j i", i=LINE, j=PACK)
-            split = nodes * SCALAR_SIXTEENTHS // 16 // LINE
-            nc.scalar.activation(dst[:, :split], src[:, :split], COPY)
-            nc.vector.tensor_copy(dst[:, split:], src[:, split:])
+        def quantize_x(g, woven_first, entry, count):
+            start = (entry - woven_first) * PACK
             nc.vector.quantize_mx(
-                out=x_words[g][:, first : first + nodes].bitcast(FP8X4),
-                scales=x_scales[SCALE_ROWS * g :, first : first + nodes],
-                in_=grouped[:],
+                out=picked_words[g][:, entry : entry + count].bitcast(FP8X4),
+                scales=picked_scales[g][:, entry : entry + count],
+                in_=x_grouped[g, woven_first][:, start : start + count * PACK],
             )
-            if g == 0 and first + nodes == T:
-                picked_first = picked_tile("picked_first", S, "picked_first")
-                pick(picked_first[:], x_words[0], 0)
-                for entry, count in ENTRY_PIECES:
-                    picked_words[0, entry] = picked_first[:, entry : entry + count]
 
         w_grouped, w_codes, w_scales = {}, {}, {}
-        for g in range(PASSES):
-            for u in range(2):
-                name = "w_grouped_%d_%d" % (g, u)
-                w_grouped[g, u] = keep.tile([P, 2 * P * PACK], BF16, name=name, tag=name, align_bytes=64)
-                nc.scalar.activation(
-                    w_grouped[g, u][:].rearrange("p (e m j) -> p m j e", e=2, j=PACK),
-                    w_raw[g][:].rearrange("p j (m t) -> p m j t", t=PACK)[:, :, :, 2 * u : 2 * u + 2],
-                    COPY,
-                )
+
+        def round_w(g, u, tag):
+            name = "w_grouped_%d_%d" % (g, u)
+            if tag is None:
+                w_grouped[g, u] = shared.tile([P, 2 * P * PACK], BF16, name=name, align_bytes=64, offset=0)
+            else:
+                w_grouped[g, u] = keep.tile([P, 2 * P * PACK], BF16, name=name, tag=tag, align_bytes=64)
+            nc.scalar.activation(
+                w_grouped[g, u][:].rearrange("p (e m j) -> p m j e", e=2, j=PACK),
+                w_raw[g][:].rearrange("p j (m t) -> p m j t", t=PACK)[:, :, :, 2 * u : 2 * u + 2],
+                COPY,
+            )
 
         def quantize_w(g, u, tag):
             w_codes[g, u] = keep.tile([P, 2 * P], U32, name="w_codes_%d_%d" % (g, u), tag=tag, align_bytes=64)
             w_scales[g, u] = keep.tile([P, 2 * P], U8, name="w_scales_%d_%d" % (g, u), align_bytes=64)
             nc.vector.quantize_mx(out=w_codes[g, u][:].bitcast(FP8X4), scales=w_scales[g, u][:], in_=w_grouped[g, u][:])
 
-        (first_0, count_0), (first_1, count_1), (first_2, count_2) = ENTRY_PIECES
-        pick(picked_scales[:], x_scales, 0)
+        round_and_pick(0, 0, ((0, S),), "x_pairs_0_0")
+        round_and_pick(0, 1, ((0, S),), "x_raw_0_0_0")
+        weave(0, 0, S // 2, False, "x_grouped_0_0")
+        round_and_pick(1, 0, ((0, S),), "x_raw_0_1_1024")
+        weave(0, S // 2, S // 2, True, "x_raw_1_0_1024")
+        for entry, count in halves:
+            quantize_x(0, entry, entry, count)
+        round_and_pick(1, 1, ((0, S),), "picked_pairs_0")
+        weave(1, first_0, count_0, False, "x_grouped_1_0")
+        round_w(0, 0, None)
         quantize_w(0, 0, "w_codes_0_0")
-        picked_most = picked_tile("picked_most", count_0 + count_1, "w_grouped_0_0")
-        for entry, count in ENTRY_PIECES[:2]:
-            picked_words[1, entry] = picked_most[:, entry : entry + count]
-            pick(picked_words[1, entry], x_words[1], entry)
+        weave(1, first_1, count_1 + count_2, False, None)
+        quantize_x(1, first_0, first_0, count_0)
+        quantize_x(1, first_1, first_1, count_1 + count_2)
+        round_w(0, 1, "w_grouped_0_1")
+        round_w(1, 0, "w_grouped_1_0")
         quantize_w(1, 0, "w_codes_1_0")
-        picked_last = picked_tile("picked_last", count_2, "w_grouped_1_0")
-        picked_words[1, first_2] = picked_last[:]
-        pick(picked_last[:], x_words[1], first_2)
-        quantize_w(0, 1, "x_words_1")
-        quantize_w(1, 1, "w_codes_1_1")
+        round_w(1, 1, "w_grouped_1_1")
+        quantize_w(0, 1, "w_grouped_1_0")
 
         def first_product(target, t, g, entry):
             cols = slice((t % 2) * P, (t % 2 + 1) * P)
@@ -160,59 +190,84 @@ def tile_picked_hop2_relu_e_kernel(
                 out=target,
                 lhsT=w_codes[g, t // 2][:, cols].bitcast(FP8X4),
                 lhsT_scale=w_scales[g, t // 2][:, cols],
-                rhs=picked_words[g, entry].bitcast(FP8X4),
-                rhs_scale=picked_scales[SCALE_ROWS * g :, entry : entry + target.shape[1]],
+                rhs=picked_words[g][:, entry : entry + target.shape[1]].bitcast(FP8X4),
+                rhs_scale=picked_scales[g][:, entry : entry + target.shape[1]],
                 start=(g == 0),
                 stop=(g == PASSES - 1),
             )
 
         h_tiles = [keep.tile([P, S], F32, name="h_%d" % t) for t in range(PACK)]
         h_banks = [bank(index, "h_bank_0_%d" % index) for index in range(len(ENTRY_PIECES))]
-        for g in range(PASSES):
-            for index, (entry, count) in enumerate(ENTRY_PIECES):
-                first_product(h_banks[index][:, :count], 0, g, entry)
-        nc.scalar.activation(h_tiles[0][:, first_0 : first_0 + count_0], h_banks[0][:, :count_0], RELU)
+        second_banks = [bank(3 + s, "h_bank_1_%d" % s) for s in range(S // BANK)]
+        for index, (entry, count) in enumerate(ENTRY_PIECES):
+            first_product(h_banks[index][:, :count], 0, 0, entry)
+        for s in range(S // BANK):
+            first_product(second_banks[s][:], 1, 0, s * BANK)
+        for index, (entry, count) in enumerate(ENTRY_PIECES):
+            first_product(h_banks[index][:, :count], 0, 1, entry)
+        nc.vector.tensor_scalar_max(h_tiles[0][:, first_0 : first_0 + count_0], h_banks[0][:, :count_0], 0.0)
         nc.scalar.activation(h_tiles[0][:, first_1 : first_1 + count_1], h_banks[1][:, :count_1], RELU)
         nc.vector.tensor_scalar_max(h_tiles[0][:, first_2:], h_banks[2][:, :count_2], 0.0)
-        for t in range(1, PACK):
-            h_banks = [bank(3 * (t % 2) + s, "h_bank_%d_%d" % (t, s)) for s in range(S // BANK)]
-            for entry, count in ENTRY_PIECES:
-                for g in range(PASSES):
-                    first_product(h_banks[entry // BANK][:, entry % BANK : entry % BANK + count], t, g, entry)
-            for s in range(S // BANK):
-                nc.scalar.activation(h_tiles[t][:, s * BANK : (s + 1) * BANK], h_banks[s][:], RELU)
+        for s in range(S // BANK):
+            first_product(second_banks[s][:], 1, 1, s * BANK)
+            nc.scalar.activation(h_tiles[1][:, s * BANK : (s + 1) * BANK], second_banks[s][:], RELU)
 
         blocks = TURNED // P
         sum_banks = [bank(5 + b, "sum_bank_%d" % b) for b in range(blocks)]
-        back_banks = [bank(2, "back_bank_0"), bank(0, "back_bank_1")]
-        for t in range(PACK):
-            terms = [keep.tile([P, TURNED], F32, name="term_%d_%d" % (t, d)) for d in range(2)]
+
+        def gather_terms(t, first, count):
             for d in range(2):
                 nc.vector.tensor_tensor(
-                    terms[d][:], h_tiles[t][:].indirect(entries(pos_tiles[d], 0, TURNED)), gate_turned[:, d, :], MULT
+                    terms[:, d, t, first : first + count],
+                    h_tiles[t][:].indirect(entries(pos_tiles[d], first, count)),
+                    gate_tile[:, d, first : first + count],
+                    MULT,
                 )
+
+        def turn_terms(t):
             for d in range(2):
                 for b in range(blocks):
                     nc.tensor.matmul(
                         sum_banks[b][:, t * P : (t + 1) * P],
-                        terms[d][:, b * P : (b + 1) * P],
+                        terms[:, d, t, b * P : (b + 1) * P],
                         identity[:],
                         start=(d == 0),
                         stop=(d == 1),
                         is_transpose=True,
                     )
-            if t % 2 == 1:
-                u = t // 2
-                for b in range(blocks):
-                    pairs = keep.tile([P, 2 * P], BF16, name="pairs_%d_%d" % (u, b))
-                    nc.scalar.activation(
-                        pairs[:].rearrange("v (p e) -> v p e", e=2),
-                        sum_banks[b][:, 2 * u * P : (2 * u + 2) * P].rearrange("v (e p) -> v p e", e=2),
-                        COPY,
-                    )
-                    column, width = Z_PIECES[b // 2]
-                    start = u * width + b * P - column
-                    nc.tensor.transpose(back_banks[b // 2][:, start : start + P], pairs[:].bitcast(F32), identity[:])
+
+        def turn_back(u):
+            for b in range(blocks):
+                pairs = keep.tile([P, 2 * P], BF16, name="pairs_%d_%d" % (u, b))
+                nc.scalar.activation(
+                    pairs[:].rearrange("v (p e) -> v p e", e=2),
+                    sum_banks[b][:, 2 * u * P : (2 * u + 2) * P].rearrange("v (e p) -> v p e", e=2),
+                    COPY,
+                )
+                column, width = Z_PIECES[b // 2]
+                start = u * width + b * P - column
+                nc.tensor.transpose(back_banks[b // 2][:, start : start + P], pairs[:].bitcast(F32), identity[:])
+
+        def make_h(t):
+            banks = [bank(3 * (t % 2) + s, "h_bank_%d_%d" % (t, s)) for s in range(S // BANK)]
+            for s in range(S // BANK):
+                for g in range(PASSES):
+                    first_product(banks[s][:], t, g, s * BANK)
+                nc.scalar.activation(h_tiles[t][:, s * BANK : (s + 1) * BANK], banks[s][:], RELU)
+
+        quantize_w(1, 1, "w_codes_1_1")
+        gather_terms(0, 0, V)
+        make_h(2)
+        make_h(3)
+        turn_terms(0)
+        gather_terms(1, 0, V)
+        turn_terms(1)
+        back_banks = [bank(2, "back_bank_0"), bank(0, "back_bank_1")]
+        turn_back(0)
+        for t in range(2, PACK):
+            gather_terms(t, 0, TURNED)
+            turn_terms(t)
+        turn_back(1)
 
         z_grouped = [
             keep.tile([P, width * PACK], BF16, name="z_grouped_%d" % column, tag="z_grouped_%d" % column, align_bytes=64)
@@ -226,15 +281,8 @@ def tile_picked_hop2_relu_e_kernel(
             )
 
         rest = V - TURNED
-        rest_terms = keep.tile([P, 2, PACK, rest], F32, name="rest_terms", tag="gate_turned")
-        for t in range(PACK):
-            for d in range(2):
-                nc.vector.tensor_tensor(
-                    rest_terms[:, d, t, :],
-                    h_tiles[t][:].indirect(entries(pos_tiles[d], TURNED, rest)),
-                    gate_rest[:, d, :],
-                    MULT,
-                )
+        for t in range(2, PACK):
+            gather_terms(t, TURNED, rest)
         z_codes, z_scales = {}, {}
 
         def quantize_z(index, tag):
@@ -243,16 +291,16 @@ def tile_picked_hop2_relu_e_kernel(
             z_scales[index] = keep.tile([P, width], U8, name="z_scales_%d" % column, align_bytes=64)
             nc.vector.quantize_mx(out=z_codes[index][:].bitcast(FP8X4), scales=z_scales[index][:], in_=z_grouped[index][:])
 
-        quantize_z(0, "z_codes_0")
-        z_grouped.append(keep.tile([P, rest * PACK], BF16, name="z_grouped_rest", tag="z_grouped_0", align_bytes=64))
+        z_grouped.append(keep.tile([P, rest * PACK], BF16, name="z_grouped_rest", tag="z_grouped_rest", align_bytes=64))
         nc.vector.tensor_tensor(
             z_grouped[2][:].rearrange("p (c i t) -> p c t i", i=LINE, t=PACK),
-            rest_terms[:, 0].rearrange("p t (c i) -> p c t i", i=LINE),
-            rest_terms[:, 1].rearrange("p t (c i) -> p c t i", i=LINE),
+            terms[:, 0, :, TURNED:V].rearrange("p t (c i) -> p c t i", i=LINE),
+            terms[:, 1, :, TURNED:V].rearrange("p t (c i) -> p c t i", i=LINE),
             ADD,
         )
-        quantize_z(1, "z_codes_1")
-        quantize_z(2, "z_grouped_%d" % Z_PIECES[1][0])
+        quantize_z(0, "terms")
+        quantize_z(2, "z_grouped_0")
+        quantize_z(1, "z_grouped_rest")
 
         def second_product(target, m, index):
             nc.tensor.matmul_mx(
@@ -266,7 +314,7 @@ def tile_picked_hop2_relu_e_kernel(
             )
 
         g_tiles = [keep.tile([P, V], F32, name="g_%d" % m) for m in range(N // P)]
-        for index, number in enumerate((1, 3, 4)):
+        for index, number in ((0, 1), (2, 3), (1, 4)):
             column, width = Z_PIECES[index]
             piece_bank = bank(number, "g_bank_0_%d" % index)
             second_product(piece_bank[:, :width], 0, index)

@@ -29,7 +29,7 @@ QUADRANT = 32
 SCALE_ROWS = 4
 
 LOAD_NODES = (((2048,), (1024, 1024)), ((1024, 1024), (1024, 512, 512)))
-SCALAR_SIXTEENTHS = (((6,), (16, 5)), ((16, 5), (16, 0, 8)))
+SCALAR_SIXTEENTHS = (((6,), (16, 5)), ((16, 8), (16, 6, 5)))
 ENTRY_PIECES = ((0, 512), (512, 256), (768, 256))
 TURNED = 384
 Z_PIECES = ((0, 256), (256, 128), (TURNED, V - TURNED))
@@ -78,8 +78,9 @@ def tile_picked_hop2_relu_e_kernel(
         for g in range(PASSES):
             nc.sync.dma_start(w_raw[g][:], w1[g * K_PASS : (g + 1) * K_PASS, :].rearrange("(p j) c -> p j c", j=PACK))
         pos_tiles = [load_list("pos1_tile", pos1), load_list("pos2_tile", pos2)]
-        terms = keep.tile([P, 2, PACK, 2 * V], F32, name="terms", tag="terms", align_bytes=64)
-        gate_tile = terms[:, :, 2, TURNED : TURNED + V]
+        terms = keep.tile([P, 2, 2 * V], F32, name="terms", tag="terms", align_bytes=64)
+        gate_tile = terms[:, :, V:]
+        rest_terms = terms[:, :, TURNED : TURNED + V].rearrange("p d (t c) -> p d t c", t=PACK)
         nc.sync.dma_start(gate_tile, gate.rearrange("d p v -> p d v"))
         w2_codes = keep.tile([P, N], U32, name="w2_codes", align_bytes=64)
         nc.sync.dma_start(w2_codes[:].bitcast(I32), w2_words[0].rearrange("p n t -> p (n t)").bitcast(I32))
@@ -167,10 +168,10 @@ def tile_picked_hop2_relu_e_kernel(
         round_and_pick(0, 0, ((0, S),), "x_pairs_0_0")
         round_and_pick(0, 1, ((0, S),), "x_raw_0_0_0")
         weave(0, 0, S // 2, False, "x_grouped_0_0")
+        quantize_x(0, 0, 0, S // 2)
         round_and_pick(1, 0, ((0, S),), "x_raw_0_1_1024")
         weave(0, S // 2, S // 2, True, "x_raw_1_0_1024")
-        for entry, count in halves:
-            quantize_x(0, entry, entry, count)
+        quantize_x(0, S // 2, S // 2, S // 2)
         round_and_pick(1, 1, ((0, S),), "picked_pairs_0")
         weave(1, first_0, count_0, False, "x_grouped_1_0")
         round_w(0, 0, None)
@@ -203,11 +204,13 @@ def tile_picked_hop2_relu_e_kernel(
             first_product(h_banks[index][:, :count], 0, 0, entry)
         for s in range(S // BANK):
             first_product(second_banks[s][:], 1, 0, s * BANK)
-        for index, (entry, count) in enumerate(ENTRY_PIECES):
+        for index in (1, 0, 2):
+            entry, count = ENTRY_PIECES[index]
             first_product(h_banks[index][:, :count], 0, 1, entry)
-        nc.vector.tensor_scalar_max(h_tiles[0][:, first_0 : first_0 + count_0], h_banks[0][:, :count_0], 0.0)
+        quantize_w(1, 1, "w_codes_1_1")
         nc.scalar.activation(h_tiles[0][:, first_1 : first_1 + count_1], h_banks[1][:, :count_1], RELU)
-        nc.vector.tensor_scalar_max(h_tiles[0][:, first_2:], h_banks[2][:, :count_2], 0.0)
+        nc.vector.tensor_scalar_max(h_tiles[0][:, first_0 : first_0 + count_0], h_banks[0][:, :count_0], 0.0)
+        nc.scalar.activation(h_tiles[0][:, first_2:], h_banks[2][:, :count_2], RELU)
         for s in range(S // BANK):
             first_product(second_banks[s][:], 1, 1, s * BANK)
             nc.scalar.activation(h_tiles[1][:, s * BANK : (s + 1) * BANK], second_banks[s][:], RELU)
@@ -215,21 +218,21 @@ def tile_picked_hop2_relu_e_kernel(
         blocks = TURNED // P
         sum_banks = [bank(5 + b, "sum_bank_%d" % b) for b in range(blocks)]
 
-        def gather_terms(t, first, count):
+        def gather_terms(targets, t, first, count):
             for d in range(2):
                 nc.vector.tensor_tensor(
-                    terms[:, d, t, first : first + count],
+                    targets[d],
                     h_tiles[t][:].indirect(entries(pos_tiles[d], first, count)),
                     gate_tile[:, d, first : first + count],
                     MULT,
                 )
 
-        def turn_terms(t):
+        def turn_terms(targets, t):
             for d in range(2):
                 for b in range(blocks):
                     nc.tensor.matmul(
                         sum_banks[b][:, t * P : (t + 1) * P],
-                        terms[:, d, t, b * P : (b + 1) * P],
+                        targets[d][:, b * P : (b + 1) * P],
                         identity[:],
                         start=(d == 0),
                         stop=(d == 1),
@@ -255,18 +258,21 @@ def tile_picked_hop2_relu_e_kernel(
                     first_product(banks[s][:], t, g, s * BANK)
                 nc.scalar.activation(h_tiles[t][:, s * BANK : (s + 1) * BANK], banks[s][:], RELU)
 
-        quantize_w(1, 1, "w_codes_1_1")
-        gather_terms(0, 0, V)
+        def turned_columns(t):
+            targets = [keep.tile([P, TURNED], F32, name="term_%d_%d" % (t, d))[:] for d in range(2)]
+            gather_terms(targets, t, 0, TURNED)
+            turn_terms(targets, t)
+
+        first_terms = [terms[:, d, :V] for d in range(2)]
+        gather_terms(first_terms, 0, 0, V)
         make_h(2)
         make_h(3)
-        turn_terms(0)
-        gather_terms(1, 0, V)
-        turn_terms(1)
+        turn_terms(first_terms, 0)
+        turned_columns(1)
         back_banks = [bank(2, "back_bank_0"), bank(0, "back_bank_1")]
         turn_back(0)
-        for t in range(2, PACK):
-            gather_terms(t, 0, TURNED)
-            turn_terms(t)
+        turned_columns(2)
+        turned_columns(3)
         turn_back(1)
 
         z_grouped = [
@@ -281,8 +287,8 @@ def tile_picked_hop2_relu_e_kernel(
             )
 
         rest = V - TURNED
-        for t in range(2, PACK):
-            gather_terms(t, TURNED, rest)
+        for t in range(1, PACK):
+            gather_terms([rest_terms[:, d, t, :] for d in range(2)], t, TURNED, rest)
         z_codes, z_scales = {}, {}
 
         def quantize_z(index, tag):
@@ -294,8 +300,8 @@ def tile_picked_hop2_relu_e_kernel(
         z_grouped.append(keep.tile([P, rest * PACK], BF16, name="z_grouped_rest", tag="z_grouped_rest", align_bytes=64))
         nc.vector.tensor_tensor(
             z_grouped[2][:].rearrange("p (c i t) -> p c t i", i=LINE, t=PACK),
-            terms[:, 0, :, TURNED:V].rearrange("p t (c i) -> p c t i", i=LINE),
-            terms[:, 1, :, TURNED:V].rearrange("p t (c i) -> p c t i", i=LINE),
+            rest_terms[:, 0].rearrange("p t (c i) -> p c t i", i=LINE),
+            rest_terms[:, 1].rearrange("p t (c i) -> p c t i", i=LINE),
             ADD,
         )
         quantize_z(0, "terms")

@@ -29,7 +29,7 @@ QUADRANT = 32
 SCALE_ROWS = 4
 
 LOAD_NODES = (((2048,), (1024, 1024)), ((1024, 1024), (1024, 512, 512)))
-SCALAR_SIXTEENTHS = (((6,), (16, 5)), ((16, 8), (16, 6, 5)))
+SCALAR_SIXTEENTHS = (((6,), (16, 5)), ((16, 7), (16, 0, 5)))
 ENTRY_PIECES = ((0, 512), (512, 256), (768, 256))
 TURNED = 384
 Z_PIECES = ((0, 256), (256, 128), (TURNED, V - TURNED))
@@ -61,7 +61,9 @@ def tile_picked_hop2_relu_e_kernel(
         make_identity(nc, identity[:])
 
         x_raw = {}
-        w_raw = [keep.tile([P, PACK, H], F32, name="w_raw_%d" % g) for g in range(PASSES)]
+        w_raw = [
+            keep.tile([P, PACK, H], F32, name="w_raw_%d" % g, tag="w_raw_%d" % g, align_bytes=64) for g in range(PASSES)
+        ]
         for g in range(PASSES):
             rows = xT[g * K_PASS : (g + 1) * K_PASS, :].rearrange("(p j) c -> p j c", j=PACK)
             for u in range(2):
@@ -78,10 +80,13 @@ def tile_picked_hop2_relu_e_kernel(
         for g in range(PASSES):
             nc.sync.dma_start(w_raw[g][:], w1[g * K_PASS : (g + 1) * K_PASS, :].rearrange("(p j) c -> p j c", j=PACK))
         pos_tiles = [load_list("pos1_tile", pos1), load_list("pos2_tile", pos2)]
-        terms = keep.tile([P, 2, 2 * V], F32, name="terms", tag="terms", align_bytes=64)
-        gate_tile = terms[:, :, V:]
-        rest_terms = terms[:, :, TURNED : TURNED + V].rearrange("p d (t c) -> p d t c", t=PACK)
-        nc.sync.dma_start(gate_tile, gate.rearrange("d p v -> p d v"))
+        gate_turned = []
+        for d in range(2):
+            name = "gate_turned_%d" % d
+            gate_turned.append(keep.tile([P, TURNED], F32, name=name, tag=name, align_bytes=64))
+            nc.sync.dma_start(gate_turned[d][:], gate[d, :, :TURNED])
+        gate_rest = keep.tile([P, 2, V - TURNED], F32, name="gate_rest")
+        nc.sync.dma_start(gate_rest[:], gate[:, :, TURNED:].rearrange("d p v -> p d v"))
         w2_codes = keep.tile([P, N], U32, name="w2_codes", align_bytes=64)
         nc.sync.dma_start(w2_codes[:].bitcast(I32), w2_words[0].rearrange("p n t -> p (n t)").bitcast(I32))
         for q in range(P // QUADRANT):
@@ -166,13 +171,13 @@ def tile_picked_hop2_relu_e_kernel(
             nc.vector.quantize_mx(out=w_codes[g, u][:].bitcast(FP8X4), scales=w_scales[g, u][:], in_=w_grouped[g, u][:])
 
         round_and_pick(0, 0, ((0, S),), "x_pairs_0_0")
-        round_and_pick(0, 1, ((0, S),), "x_raw_0_0_0")
+        round_and_pick(0, 1, halves, "x_raw_0_0_0")
         weave(0, 0, S // 2, False, "x_grouped_0_0")
         quantize_x(0, 0, 0, S // 2)
         round_and_pick(1, 0, ((0, S),), "x_raw_0_1_1024")
         weave(0, S // 2, S // 2, True, "x_raw_1_0_1024")
         quantize_x(0, S // 2, S // 2, S // 2)
-        round_and_pick(1, 1, ((0, S),), "picked_pairs_0")
+        round_and_pick(1, 1, halves, "picked_pairs_0")
         weave(1, first_0, count_0, False, "x_grouped_1_0")
         round_w(0, 0, None)
         quantize_w(0, 0, "w_codes_0_0")
@@ -218,12 +223,12 @@ def tile_picked_hop2_relu_e_kernel(
         blocks = TURNED // P
         sum_banks = [bank(5 + b, "sum_bank_%d" % b) for b in range(blocks)]
 
-        def gather_terms(targets, t, first, count):
+        def gather_terms(targets, t, first, count, gate_tile):
             for d in range(2):
                 nc.vector.tensor_tensor(
                     targets[d],
                     h_tiles[t][:].indirect(entries(pos_tiles[d], first, count)),
-                    gate_tile[:, d, first : first + count],
+                    gate_tile[d],
                     MULT,
                 )
 
@@ -260,19 +265,18 @@ def tile_picked_hop2_relu_e_kernel(
 
         def turned_columns(t):
             targets = [keep.tile([P, TURNED], F32, name="term_%d_%d" % (t, d))[:] for d in range(2)]
-            gather_terms(targets, t, 0, TURNED)
-            turn_terms(targets, t)
+            gather_terms(targets, t, 0, TURNED, [tile[:] for tile in gate_turned])
+            return targets
 
-        first_terms = [terms[:, d, :V] for d in range(2)]
-        gather_terms(first_terms, 0, 0, V)
+        first_terms = turned_columns(0)
         make_h(2)
         make_h(3)
         turn_terms(first_terms, 0)
-        turned_columns(1)
+        turn_terms(turned_columns(1), 1)
         back_banks = [bank(2, "back_bank_0"), bank(0, "back_bank_1")]
         turn_back(0)
-        turned_columns(2)
-        turned_columns(3)
+        turn_terms(turned_columns(2), 2)
+        turn_terms(turned_columns(3), 3)
         turn_back(1)
 
         z_grouped = [
@@ -287,8 +291,12 @@ def tile_picked_hop2_relu_e_kernel(
             )
 
         rest = V - TURNED
-        for t in range(1, PACK):
-            gather_terms([rest_terms[:, d, t, :] for d in range(2)], t, TURNED, rest)
+        rest_terms = [
+            keep.tile([P, PACK, rest], F32, name="rest_terms_%d" % d, tag="gate_turned_%d" % d, align_bytes=64)
+            for d in range(2)
+        ]
+        for t in range(PACK):
+            gather_terms([rest_terms[d][:, t, :] for d in range(2)], t, TURNED, rest, [gate_rest[:, d, :] for d in range(2)])
         z_codes, z_scales = {}, {}
 
         def quantize_z(index, tag):
@@ -297,16 +305,16 @@ def tile_picked_hop2_relu_e_kernel(
             z_scales[index] = keep.tile([P, width], U8, name="z_scales_%d" % column, align_bytes=64)
             nc.vector.quantize_mx(out=z_codes[index][:].bitcast(FP8X4), scales=z_scales[index][:], in_=z_grouped[index][:])
 
-        z_grouped.append(keep.tile([P, rest * PACK], BF16, name="z_grouped_rest", tag="z_grouped_rest", align_bytes=64))
+        quantize_z(0, "z_codes_0")
+        z_grouped.append(keep.tile([P, rest * PACK], BF16, name="z_grouped_rest", tag="z_grouped_0", align_bytes=64))
         nc.vector.tensor_tensor(
             z_grouped[2][:].rearrange("p (c i t) -> p c t i", i=LINE, t=PACK),
-            rest_terms[:, 0].rearrange("p t (c i) -> p c t i", i=LINE),
-            rest_terms[:, 1].rearrange("p t (c i) -> p c t i", i=LINE),
+            rest_terms[0][:].rearrange("p t (c i) -> p c t i", i=LINE),
+            rest_terms[1][:].rearrange("p t (c i) -> p c t i", i=LINE),
             ADD,
         )
-        quantize_z(0, "terms")
-        quantize_z(2, "z_grouped_0")
-        quantize_z(1, "z_grouped_rest")
+        quantize_z(1, "z_codes_1")
+        quantize_z(2, "z_codes_2")
 
         def second_product(target, m, index):
             nc.tensor.matmul_mx(
@@ -320,7 +328,7 @@ def tile_picked_hop2_relu_e_kernel(
             )
 
         g_tiles = [keep.tile([P, V], F32, name="g_%d" % m) for m in range(N // P)]
-        for index, number in ((0, 1), (2, 3), (1, 4)):
+        for index, number in enumerate((1, 3, 4)):
             column, width = Z_PIECES[index]
             piece_bank = bank(number, "g_bank_0_%d" % index)
             second_product(piece_bank[:, :width], 0, index)
@@ -336,7 +344,7 @@ def tile_picked_hop2_relu_e_kernel(
                 nc.vector.tensor_tensor(
                     root_terms[:, m, d, :], g_tiles[m][:].indirect(nxt_tiles[d][:]), gate2_tile[:, d, :], MULT
                 )
-        result = keep.tile([P, N // P, U], F32, name="result", tag="gate2_tile")
+        result = gate2_tile
         for m in range(N // P):
             nc.vector.tensor_tensor(result[:, m, :], root_terms[:, m, 0, :], root_terms[:, m, 1, :], ADD)
             nc.sync.dma_start(out[m * P : (m + 1) * P, :], result[:, m, :])

@@ -29,7 +29,7 @@ QUADRANT = 32
 SCALE_ROWS = 4
 
 LOAD_NODES = (((2048,), (1024, 1024)), ((1024, 1024), (1024, 512, 512)))
-SCALAR_SIXTEENTHS = (((6,), (16, 5)), ((16, 7), (16, 0, 5)))
+SCALAR_SIXTEENTHS = (((6,), (16, 5)), ((16, 13), (16, 8, 6)))
 ENTRY_PIECES = ((0, 512), (512, 256), (768, 256))
 TURNED = 384
 Z_PIECES = ((0, 256), (256, 128), (TURNED, V - TURNED))
@@ -171,13 +171,13 @@ def tile_picked_hop2_relu_e_kernel(
             nc.vector.quantize_mx(out=w_codes[g, u][:].bitcast(FP8X4), scales=w_scales[g, u][:], in_=w_grouped[g, u][:])
 
         round_and_pick(0, 0, ((0, S),), "x_pairs_0_0")
-        round_and_pick(0, 1, halves, "x_raw_0_0_0")
+        round_and_pick(0, 1, halves, "x_pairs_0_1")
         weave(0, 0, S // 2, False, "x_grouped_0_0")
         quantize_x(0, 0, 0, S // 2)
-        round_and_pick(1, 0, ((0, S),), "x_raw_0_1_1024")
-        weave(0, S // 2, S // 2, True, "x_raw_1_0_1024")
+        round_and_pick(1, 0, ((0, S),), "x_pairs_1_0")
+        weave(0, S // 2, S // 2, False, "x_grouped_0_1")
         quantize_x(0, S // 2, S // 2, S // 2)
-        round_and_pick(1, 1, halves, "picked_pairs_0")
+        round_and_pick(1, 1, halves, "x_pairs_1_1")
         weave(1, first_0, count_0, False, "x_grouped_1_0")
         round_w(0, 0, None)
         quantize_w(0, 0, "w_codes_0_0")
@@ -209,13 +209,13 @@ def tile_picked_hop2_relu_e_kernel(
             first_product(h_banks[index][:, :count], 0, 0, entry)
         for s in range(S // BANK):
             first_product(second_banks[s][:], 1, 0, s * BANK)
-        for index in (1, 0, 2):
+        for index in (0, 1, 2):
             entry, count = ENTRY_PIECES[index]
             first_product(h_banks[index][:, :count], 0, 1, entry)
-        quantize_w(1, 1, "w_codes_1_1")
-        nc.scalar.activation(h_tiles[0][:, first_1 : first_1 + count_1], h_banks[1][:, :count_1], RELU)
         nc.vector.tensor_scalar_max(h_tiles[0][:, first_0 : first_0 + count_0], h_banks[0][:, :count_0], 0.0)
+        nc.scalar.activation(h_tiles[0][:, first_1 : first_1 + count_1], h_banks[1][:, :count_1], RELU)
         nc.scalar.activation(h_tiles[0][:, first_2:], h_banks[2][:, :count_2], RELU)
+        quantize_w(1, 1, "w_grouped_0_1")
         for s in range(S // BANK):
             first_product(second_banks[s][:], 1, 1, s * BANK)
             nc.scalar.activation(h_tiles[1][:, s * BANK : (s + 1) * BANK], second_banks[s][:], RELU)

@@ -28,8 +28,8 @@ BANK = 512
 QUADRANT = 32
 SCALE_ROWS = 4
 
-LOAD_NODES = (((2048,), (1024, 1024)), ((1024, 1024), (1024, 512, 512)))
-SCALAR_SIXTEENTHS = (((6,), (16, 5)), ((16, 13), (16, 8, 6)))
+LOAD_NODES = (((2048,), (1024, 1024)), ((1024, 1024), (1024, 768, 256)))
+SCALAR_SIXTEENTHS = (((6,), (16, 5)), ((16, 13), (16, 7, 6)))
 ENTRY_PIECES = ((0, 512), (512, 256), (768, 256))
 TURNED = 384
 Z_PIECES = ((0, 256), (256, 128), (TURNED, V - TURNED))
@@ -345,6 +345,7 @@ def tile_picked_hop2_relu_e_kernel(
                     root_terms[:, m, d, :], g_tiles[m][:].indirect(nxt_tiles[d][:]), gate2_tile[:, d, :], MULT
                 )
         result = gate2_tile
-        for m in range(N // P):
-            nc.vector.tensor_tensor(result[:, m, :], root_terms[:, m, 0, :], root_terms[:, m, 1, :], ADD)
-            nc.sync.dma_start(out[m * P : (m + 1) * P, :], result[:, m, :])
+        for m, first, count in ((0, 0, U), (1, 0, U // 2), (1, U // 2, U // 2)):
+            cols = slice(first, first + count)
+            nc.vector.tensor_tensor(result[:, m, cols], root_terms[:, m, 0, cols], root_terms[:, m, 1, cols], ADD)
+            nc.sync.dma_start(out[m * P : (m + 1) * P, cols], result[:, m, cols])

@@ -28,8 +28,8 @@ BANK = 512
 QUADRANT = 32
 SCALE_ROWS = 4
 
-LOAD_NODES = (((2048,), (1024, 1024)), ((1024, 1024), (1024, 768, 256)))
-SCALAR_SIXTEENTHS = (((6,), (16, 5)), ((16, 13), (16, 7, 6)))
+VECTOR_ENTRIES = ((384, 384, 384, 384), (0, 128, 384, 256))
+PIECE = 256
 ENTRY_PIECES = ((0, 512), (512, 256), (768, 256))
 TURNED = 384
 Z_PIECES = ((0, 256), (256, 128), (TURNED, V - TURNED))
@@ -41,7 +41,6 @@ def tile_picked_hop2_relu_e_kernel(
     nc = tc.nc
     with ExitStack() as ctx:
         keep = ctx.enter_context(tc.tile_pool(name="keep", bufs=1))
-        shared = ctx.enter_context(tc.tile_pool(name="shared", bufs=1))
         psum = ctx.enter_context(tc.psum_pool(name="psum", bufs=1))
 
         def load_list(name, source):
@@ -60,23 +59,16 @@ def tile_picked_hop2_relu_e_kernel(
         identity = keep.tile([P, P], F32, name="identity")
         make_identity(nc, identity[:])
 
+        offs_tile = load_list("offs_tile", offs)
         x_raw = {}
         w_raw = [
             keep.tile([P, PACK, H], F32, name="w_raw_%d" % g, tag="w_raw_%d" % g, align_bytes=64) for g in range(PASSES)
         ]
         for g in range(PASSES):
             rows = xT[g * K_PASS : (g + 1) * K_PASS, :].rearrange("(p j) c -> p j c", j=PACK)
-            for u in range(2):
-                x_raw[g, u] = []
-                first = 0
-                for nodes in LOAD_NODES[g][u]:
-                    name = "x_raw_%d_%d_%d" % (g, u, first)
-                    raw = keep.tile([P, 2, nodes], F32, name=name, tag=name, align_bytes=64)
-                    nc.sync.dma_start(raw[:], rows[:, 2 * u : 2 * u + 2, first : first + nodes])
-                    x_raw[g, u].append((first, raw))
-                    first = first + nodes
-                if (g, u) == (0, 0):
-                    offs_tile = load_list("offs_tile", offs)
+            for j in range(PACK):
+                x_raw[g, j] = keep.tile([P, T], F32, name="x_raw_%d_%d" % (g, j), align_bytes=64)
+                nc.sync.dma_start(x_raw[g, j][:], rows[:, j, :])
         for g in range(PASSES):
             nc.sync.dma_start(w_raw[g][:], w1[g * K_PASS : (g + 1) * K_PASS, :].rearrange("(p j) c -> p j c", j=PACK))
         pos_tiles = [load_list("pos1_tile", pos1), load_list("pos2_tile", pos2)]
@@ -85,8 +77,10 @@ def tile_picked_hop2_relu_e_kernel(
             name = "gate_turned_%d" % d
             gate_turned.append(keep.tile([P, TURNED], F32, name=name, tag=name, align_bytes=64))
             nc.sync.dma_start(gate_turned[d][:], gate[d, :, :TURNED])
-        gate_rest = keep.tile([P, 2, V - TURNED], F32, name="gate_rest")
-        nc.sync.dma_start(gate_rest[:], gate[:, :, TURNED:].rearrange("d p v -> p d v"))
+        gate_rest = keep.tile([P, V - TURNED], F32, name="gate_rest")
+        nc.sync.dma_start(gate_rest[:], gate[0, :, TURNED:])
+        gate_column = keep.tile([P, 1], F32, name="gate_column")
+        nc.sync.dma_start(gate_column[:], gate[1, 0, TURNED:].rearrange("(v o) -> v o", o=1))
         w2_codes = keep.tile([P, N], U32, name="w2_codes", align_bytes=64)
         nc.sync.dma_start(w2_codes[:].bitcast(I32), w2_words[0].rearrange("p n t -> p (n t)").bitcast(I32))
         for q in range(P // QUADRANT):
@@ -99,66 +93,43 @@ def tile_picked_hop2_relu_e_kernel(
         nc.sync.dma_start(gate2_tile[:], gate2.rearrange("d p v -> p d v"))
 
         (first_0, count_0), (first_1, count_1), (first_2, count_2) = ENTRY_PIECES
-        halves = ((0, S // 2), (S // 2, S // 2))
-        picked_pairs = [
-            keep.tile([P, 2, S], U32, name="picked_pairs_%d" % g, tag="picked_pairs_%d" % g, align_bytes=64)
-            for g in range(PASSES)
-        ]
+        picked = [keep.tile([P, PACK, S], BF16, name="picked_%d" % g, align_bytes=64) for g in range(PASSES)]
         picked_words = [keep.tile([P, S], U32, name="picked_words_%d" % g, align_bytes=64) for g in range(PASSES)]
-        picked_scales = [
-            keep.tile([P, S], U8, name="picked_scales_0", align_bytes=64),
-            shared.tile([P, S], U8, name="picked_scales_1", align_bytes=64, offset=0),
-        ]
+        picked_scales = [keep.tile([P, S], U8, name="picked_scales_%d" % g, align_bytes=64) for g in range(PASSES)]
         x_grouped = {}
 
-        def round_and_pick(g, u, pieces, tag):
-            pairs = keep.tile([P, 2 * T], BF16, name="x_pairs_%d_%d" % (g, u), tag=tag, align_bytes=64)
-            for (first, raw), sixteenths in zip(x_raw[g, u], SCALAR_SIXTEENTHS[g][u]):
-                nodes = raw.shape[2]
-                src = raw[:].rearrange("p e c -> p c e")
-                dst = pairs[:, 2 * first : 2 * (first + nodes)].rearrange("p (c e) -> p c e", e=2)
-                split = nodes * sixteenths // 16
-                if split > 0:
-                    nc.scalar.activation(dst[:, :split], src[:, :split], COPY)
-                if split < nodes:
-                    nc.vector.tensor_copy(dst[:, split:], src[:, split:])
-            for entry, count in pieces:
-                nc.vector.tensor_copy(
-                    picked_pairs[g][:, u, entry : entry + count],
-                    pairs[:].bitcast(U32).indirect(entries(offs_tile, entry, count)),
+        def pick(g, j, piece):
+            split = VECTOR_ENTRIES[g][j]
+            if split > 0:
+                nc.vector.tensor_copy(picked[g][:, j, :split], x_raw[g, j][:].indirect(entries(offs_tile, 0, split)))
+            for entry in range(split, S, piece):
+                count = min(piece, S - entry)
+                nc.scalar.activation(
+                    picked[g][:, j, entry : entry + count],
+                    x_raw[g, j][:].indirect(entries(offs_tile, entry, count)),
+                    COPY,
                 )
 
-        def weave(g, entry, count, on_scalar, tag):
+        def weave(g, entry, count, tag=None):
             name = "x_grouped_%d_%d" % (g, entry)
-            if tag is None:
-                x_grouped[g, entry] = shared.tile([P, count * PACK], BF16, name=name, align_bytes=64, offset=S)
-            else:
-                x_grouped[g, entry] = keep.tile([P, count * PACK], BF16, name=name, tag=tag, align_bytes=64)
-            src = picked_pairs[g][:, :, entry : entry + count].rearrange("p u c -> p c u")
-            if on_scalar:
-                nc.scalar.copy(x_grouped[g, entry][:].bitcast(U32).rearrange("p (c u) -> p c u", u=2), src)
-            else:
-                nc.vector.tensor_copy(
-                    x_grouped[g, entry][:].bitcast(I32).rearrange("p (c u) -> p c u", u=2),
-                    picked_pairs[g][:].bitcast(I32)[:, :, entry : entry + count].rearrange("p u c -> p c u"),
-                )
+            x_grouped[g, entry] = keep.tile([P, count * PACK], BF16, name=name, tag=tag or name, align_bytes=64)
+            nc.vector.tensor_copy(
+                x_grouped[g, entry][:].rearrange("p (c i j) -> p c j i", i=LINE, j=PACK),
+                picked[g][:, :, entry : entry + count].rearrange("p j (c i) -> p c j i", i=LINE),
+            )
 
-        def quantize_x(g, woven_first, entry, count):
-            start = (entry - woven_first) * PACK
+        def quantize_x(g, entry, count):
             nc.vector.quantize_mx(
                 out=picked_words[g][:, entry : entry + count].bitcast(FP8X4),
                 scales=picked_scales[g][:, entry : entry + count],
-                in_=x_grouped[g, woven_first][:, start : start + count * PACK],
+                in_=x_grouped[g, entry][:],
             )
 
         w_grouped, w_codes, w_scales = {}, {}, {}
 
         def round_w(g, u, tag):
             name = "w_grouped_%d_%d" % (g, u)
-            if tag is None:
-                w_grouped[g, u] = shared.tile([P, 2 * P * PACK], BF16, name=name, align_bytes=64, offset=0)
-            else:
-                w_grouped[g, u] = keep.tile([P, 2 * P * PACK], BF16, name=name, tag=tag, align_bytes=64)
+            w_grouped[g, u] = keep.tile([P, 2 * P * PACK], BF16, name=name, tag=tag, align_bytes=64)
             nc.scalar.activation(
                 w_grouped[g, u][:].rearrange("p (e m j) -> p m j e", e=2, j=PACK),
                 w_raw[g][:].rearrange("p j (m t) -> p m j t", t=PACK)[:, :, :, 2 * u : 2 * u + 2],
@@ -170,25 +141,30 @@ def tile_picked_hop2_relu_e_kernel(
             w_scales[g, u] = keep.tile([P, 2 * P], U8, name="w_scales_%d_%d" % (g, u), align_bytes=64)
             nc.vector.quantize_mx(out=w_codes[g, u][:].bitcast(FP8X4), scales=w_scales[g, u][:], in_=w_grouped[g, u][:])
 
-        round_and_pick(0, 0, ((0, S),), "x_pairs_0_0")
-        round_and_pick(0, 1, halves, "x_pairs_0_1")
-        weave(0, 0, S // 2, False, "x_grouped_0_0")
-        quantize_x(0, 0, 0, S // 2)
-        round_and_pick(1, 0, ((0, S),), "x_pairs_1_0")
-        weave(0, S // 2, S // 2, False, "x_grouped_0_1")
-        quantize_x(0, S // 2, S // 2, S // 2)
-        round_and_pick(1, 1, halves, "x_pairs_1_1")
-        weave(1, first_0, count_0, False, "x_grouped_1_0")
-        round_w(0, 0, None)
+        for j in range(PACK):
+            pick(0, j, S)
+        weave(0, 0, S // 2)
+        weave(0, S // 2, S // 2)
+        quantize_x(0, 0, S // 2)
+        quantize_x(0, S // 2, S // 2)
+        for j in range(PACK - 1):
+            pick(1, j, S)
+        pick(1, PACK - 1, PIECE)
+        weave(1, 0, PIECE)
+        weave(1, PIECE, PIECE)
+        quantize_x(1, 0, PIECE)
+        weave(1, 2 * PIECE, PIECE)
+        quantize_x(1, PIECE, PIECE)
+        round_w(0, 0, "w_grouped_0_0")
         quantize_w(0, 0, "w_codes_0_0")
-        weave(1, first_1, count_1 + count_2, False, None)
-        quantize_x(1, first_0, first_0, count_0)
-        quantize_x(1, first_1, first_1, count_1 + count_2)
+        weave(1, 3 * PIECE, PIECE, "w_grouped_0_0")
+        quantize_x(1, 2 * PIECE, PIECE)
+        quantize_x(1, 3 * PIECE, PIECE)
         round_w(0, 1, "w_grouped_0_1")
+        quantize_w(0, 1, "w_codes_0_1")
         round_w(1, 0, "w_grouped_1_0")
         quantize_w(1, 0, "w_codes_1_0")
         round_w(1, 1, "w_grouped_1_1")
-        quantize_w(0, 1, "w_grouped_1_0")
 
         def first_product(target, t, g, entry):
             cols = slice((t % 2) * P, (t % 2 + 1) * P)
@@ -220,8 +196,7 @@ def tile_picked_hop2_relu_e_kernel(
             first_product(second_banks[s][:], 1, 1, s * BANK)
             nc.scalar.activation(h_tiles[1][:, s * BANK : (s + 1) * BANK], second_banks[s][:], RELU)
 
-        blocks = TURNED // P
-        sum_banks = [bank(5 + b, "sum_bank_%d" % b) for b in range(blocks)]
+        sums = {}
 
         def gather_terms(targets, t, first, count, gate_tile):
             for d in range(2):
@@ -232,29 +207,33 @@ def tile_picked_hop2_relu_e_kernel(
                     MULT,
                 )
 
-        def turn_terms(targets, t):
-            for d in range(2):
-                for b in range(blocks):
+        def turn_terms(targets, t, first=0, count=TURNED):
+            for b in range(first // P, (first + count) // P):
+                start = (2 * (b % 2) + t % 2) * P
+                for d in range(2):
                     nc.tensor.matmul(
-                        sum_banks[b][:, t * P : (t + 1) * P],
-                        targets[d][:, b * P : (b + 1) * P],
+                        sums[b // 2, t // 2][:, start : start + P],
+                        targets[d][:, b * P - first : (b + 1) * P - first],
                         identity[:],
                         start=(d == 0),
                         stop=(d == 1),
                         is_transpose=True,
                     )
 
-        def turn_back(u):
-            for b in range(blocks):
-                pairs = keep.tile([P, 2 * P], BF16, name="pairs_%d_%d" % (u, b))
+        def turn_back(u, tags):
+            for index, (column, width) in enumerate(Z_PIECES[:2]):
+                name = "pairs_%d_%d" % (u, index)
+                pairs = keep.tile([P, 2 * width], BF16, name=name, tag=tags.get(name, name), align_bytes=64)
                 nc.scalar.activation(
-                    pairs[:].rearrange("v (p e) -> v p e", e=2),
-                    sum_banks[b][:, 2 * u * P : (2 * u + 2) * P].rearrange("v (e p) -> v p e", e=2),
+                    pairs[:].rearrange("v (b p e) -> v b p e", p=P, e=2),
+                    sums[index, u].rearrange("v (b e p) -> v b p e", p=P, e=2),
                     COPY,
                 )
-                column, width = Z_PIECES[b // 2]
-                start = u * width + b * P - column
-                nc.tensor.transpose(back_banks[b // 2][:, start : start + P], pairs[:].bitcast(F32), identity[:])
+                for b in range(width // P):
+                    start = u * width + b * P
+                    nc.tensor.transpose(
+                        back_banks[index][:, start : start + P], pairs[:].bitcast(F32)[:, b * P : (b + 1) * P], identity[:]
+                    )
 
         def make_h(t):
             banks = [bank(3 * (t % 2) + s, "h_bank_%d_%d" % (t, s)) for s in range(S // BANK)]
@@ -263,25 +242,42 @@ def tile_picked_hop2_relu_e_kernel(
                     first_product(banks[s][:], t, g, s * BANK)
                 nc.scalar.activation(h_tiles[t][:, s * BANK : (s + 1) * BANK], banks[s][:], RELU)
 
-        def turned_columns(t):
-            targets = [keep.tile([P, TURNED], F32, name="term_%d_%d" % (t, d))[:] for d in range(2)]
-            gather_terms(targets, t, 0, TURNED, [tile[:] for tile in gate_turned])
+        def turned_columns(t, first=0, count=TURNED, tags=None):
+            names = ["term_%d_%d_%d" % (t, d, first) for d in range(2)]
+            targets = [keep.tile([P, count], F32, name=names[d], tag=(tags or names)[d], align_bytes=64)[:] for d in range(2)]
+            gather_terms(targets, t, first, count, [tile[:, first : first + count] for tile in gate_turned])
             return targets
 
+        rest = V - TURNED
         first_terms = turned_columns(0)
         make_h(2)
         make_h(3)
+        sums[0, 0] = bank(5, "sum_bank_0_0")[:]
+        sums[1, 0] = bank(6, "sum_bank_1_0")[:, : 2 * P]
         turn_terms(first_terms, 0)
         turn_terms(turned_columns(1), 1)
-        back_banks = [bank(2, "back_bank_0"), bank(0, "back_bank_1")]
-        turn_back(0)
+        plain_bank = bank(7, "plain_bank")
+        for t in range(PACK):
+            plain = keep.tile([P, rest], F32, name="plain_%d" % t, tag="plain_%d" % t, align_bytes=64)
+            nc.scalar.activation(plain[:], h_tiles[t][:].indirect(entries(pos_tiles[1], TURNED, rest)), COPY)
+            nc.tensor.transpose(plain_bank[:, t * P : (t + 1) * P], plain[:], identity[:])
+        scaled = keep.tile([P, PACK * P], F32, name="scaled")
+        nc.scalar.activation(scaled[:], plain_bank[:], COPY, scale=gate_column[:])
+        scaled_bank = bank(2, "scaled_bank")
+        for t in range(PACK):
+            nc.tensor.transpose(scaled_bank[:, t * P : (t + 1) * P], scaled[:, t * P : (t + 1) * P], identity[:])
+        back_banks = [bank(0, "back_bank_0"), bank(1, "back_bank_1")]
+        turn_back(0, {"pairs_0_0": "plain_3", "pairs_0_1": "plain_0"})
+        sums[0, 1] = bank(7, "sum_bank_0_1")[:]
+        sums[1, 1] = bank(5, "sum_bank_1_1")[:, : 2 * P]
         turn_terms(turned_columns(2), 2)
-        turn_terms(turned_columns(3), 3)
-        turn_back(1)
+        for (column, width), tags in zip(Z_PIECES[:2], (None, None)):
+            turn_terms(turned_columns(3, column, width, tags), 3, column, width)
+        turn_back(1, {})
 
         z_grouped = [
-            keep.tile([P, width * PACK], BF16, name="z_grouped_%d" % column, tag="z_grouped_%d" % column, align_bytes=64)
-            for column, width in Z_PIECES[:2]
+            keep.tile([P, width * PACK], BF16, name="z_grouped_%d" % column, tag=tag, align_bytes=64)
+            for (column, width), tag in zip(Z_PIECES[:2], ("z_grouped_0", "z_grouped_1"))
         ]
         for index in range(2):
             width = Z_PIECES[index][1]
@@ -290,13 +286,11 @@ def tile_picked_hop2_relu_e_kernel(
                 back_banks[index][:, : 2 * width].rearrange("p (u v) -> p v u", u=2),
             )
 
-        rest = V - TURNED
-        rest_terms = [
-            keep.tile([P, PACK, rest], F32, name="rest_terms_%d" % d, tag="gate_turned_%d" % d, align_bytes=64)
-            for d in range(2)
-        ]
+        rest_terms = keep.tile([P, PACK, rest], F32, name="rest_terms", tag="gate_turned_0", align_bytes=64)
         for t in range(PACK):
-            gather_terms([rest_terms[d][:, t, :] for d in range(2)], t, TURNED, rest, [gate_rest[:, d, :] for d in range(2)])
+            nc.vector.tensor_tensor(
+                rest_terms[:, t, :], h_tiles[t][:].indirect(entries(pos_tiles[0], TURNED, rest)), gate_rest[:], MULT
+            )
         z_codes, z_scales = {}, {}
 
         def quantize_z(index, tag):
@@ -305,16 +299,16 @@ def tile_picked_hop2_relu_e_kernel(
             z_scales[index] = keep.tile([P, width], U8, name="z_scales_%d" % column, align_bytes=64)
             nc.vector.quantize_mx(out=z_codes[index][:].bitcast(FP8X4), scales=z_scales[index][:], in_=z_grouped[index][:])
 
-        quantize_z(0, "z_codes_0")
-        z_grouped.append(keep.tile([P, rest * PACK], BF16, name="z_grouped_rest", tag="z_grouped_0", align_bytes=64))
+        z_grouped.append(keep.tile([P, rest * PACK], BF16, name="z_grouped_rest", align_bytes=64))
         nc.vector.tensor_tensor(
             z_grouped[2][:].rearrange("p (c i t) -> p c t i", i=LINE, t=PACK),
-            rest_terms[0][:].rearrange("p t (c i) -> p c t i", i=LINE),
-            rest_terms[1][:].rearrange("p t (c i) -> p c t i", i=LINE),
+            scaled_bank[:].rearrange("p (t c i) -> p c t i", t=PACK, i=LINE),
+            rest_terms[:].rearrange("p t (c i) -> p c t i", i=LINE),
             ADD,
         )
-        quantize_z(1, "z_codes_1")
+        quantize_z(0, "z_codes_0")
         quantize_z(2, "z_codes_2")
+        quantize_z(1, "z_codes_1")
 
         def second_product(target, m, index):
             nc.tensor.matmul_mx(
@@ -328,24 +322,36 @@ def tile_picked_hop2_relu_e_kernel(
             )
 
         g_tiles = [keep.tile([P, V], F32, name="g_%d" % m) for m in range(N // P)]
-        for index, number in enumerate((1, 3, 4)):
+        half = V // 2
+        for m in range(N // P):
+            first_bank = bank(3 + m, "g_bank_first_%d" % m)
+            second_product(first_bank[:, :half], m, 0)
+            nc.scalar.activation(g_tiles[m][:, :half], first_bank[:, :half], RELU)
+        last_bank = bank(0, "g_bank_last_1")
+        for index, number in ((2, 1), (1, 5)):
             column, width = Z_PIECES[index]
             piece_bank = bank(number, "g_bank_0_%d" % index)
             second_product(piece_bank[:, :width], 0, index)
             nc.scalar.activation(g_tiles[0][:, column : column + width], piece_bank[:, :width], RELU)
-        whole_bank = bank(5, "g_bank_1")
-        for index, (column, width) in enumerate(Z_PIECES):
-            second_product(whole_bank[:, column : column + width], 1, index)
-        nc.scalar.activation(g_tiles[1][:], whole_bank[:], RELU)
+            second_product(last_bank[:, column - half : column - half + width], 1, index)
+        nc.scalar.activation(g_tiles[1][:, half:], last_bank[:, :half], RELU)
 
         root_terms = keep.tile([P, N // P, 2, U], F32, name="root_terms")
-        for m in range(N // P):
-            for d in range(2):
-                nc.vector.tensor_tensor(
-                    root_terms[:, m, d, :], g_tiles[m][:].indirect(nxt_tiles[d][:]), gate2_tile[:, d, :], MULT
-                )
-        result = gate2_tile
-        for m, first, count in ((0, 0, U), (1, 0, U // 2), (1, U // 2, U // 2)):
+        root_plain = keep.tile([P, 2, U], F32, name="root_plain")
+        for d in range(2):
+            nc.scalar.activation(root_plain[:, d, :], g_tiles[1][:].indirect(nxt_tiles[d][:]), COPY)
+            nc.vector.tensor_tensor(root_terms[:, 0, d, :], g_tiles[0][:].indirect(nxt_tiles[d][:]), gate2_tile[:, d, :], MULT)
+        result = keep.tile([P, N // P, U], F32, name="result")
+
+        def add_and_store(m, first, count):
             cols = slice(first, first + count)
             nc.vector.tensor_tensor(result[:, m, cols], root_terms[:, m, 0, cols], root_terms[:, m, 1, cols], ADD)
             nc.sync.dma_start(out[m * P : (m + 1) * P, cols], result[:, m, cols])
+
+        nc.vector.tensor_tensor(root_terms[:, 1, 0, :], root_plain[:, 0, :], gate2_tile[:, 0, :], MULT)
+        add_and_store(0, 0, U)
+        for first in (0, U // 2):
+            cols = slice(first, first + U // 2)
+            nc.vector.tensor_tensor(root_terms[:, 1, 1, cols], root_plain[:, 1, cols], gate2_tile[:, 1, cols], MULT)
+        for first in (0, U // 2):
+            add_and_store(1, first, U // 2)

@@ -77,10 +77,8 @@ def tile_picked_hop2_relu_e_kernel(
             name = "gate_turned_%d" % d
             gate_turned.append(keep.tile([P, TURNED], F32, name=name, tag=name, align_bytes=64))
             nc.sync.dma_start(gate_turned[d][:], gate[d, :, :TURNED])
-        gate_rest = keep.tile([P, V - TURNED], F32, name="gate_rest")
-        nc.sync.dma_start(gate_rest[:], gate[0, :, TURNED:])
-        gate_column = keep.tile([P, 1], F32, name="gate_column")
-        nc.sync.dma_start(gate_column[:], gate[1, 0, TURNED:].rearrange("(v o) -> v o", o=1))
+        gate_rest = keep.tile([P, 2, V - TURNED], F32, name="gate_rest")
+        nc.sync.dma_start(gate_rest[:], gate[:, :, TURNED:].rearrange("d p v -> p d v"))
         w2_codes = keep.tile([P, N], U32, name="w2_codes", align_bytes=64)
         nc.sync.dma_start(w2_codes[:].bitcast(I32), w2_words[0].rearrange("p n t -> p (n t)").bitcast(I32))
         for q in range(P // QUADRANT):
@@ -196,7 +194,8 @@ def tile_picked_hop2_relu_e_kernel(
             first_product(second_banks[s][:], 1, 1, s * BANK)
             nc.scalar.activation(h_tiles[1][:, s * BANK : (s + 1) * BANK], second_banks[s][:], RELU)
 
-        sums = {}
+        blocks = TURNED // P
+        sum_banks = [bank(5 + b, "sum_bank_%d" % b) for b in range(blocks)]
 
         def gather_terms(targets, t, first, count, gate_tile):
             for d in range(2):
@@ -207,33 +206,29 @@ def tile_picked_hop2_relu_e_kernel(
                     MULT,
                 )
 
-        def turn_terms(targets, t, first=0, count=TURNED):
-            for b in range(first // P, (first + count) // P):
-                start = (2 * (b % 2) + t % 2) * P
-                for d in range(2):
+        def turn_terms(targets, t):
+            for d in range(2):
+                for b in range(blocks):
                     nc.tensor.matmul(
-                        sums[b // 2, t // 2][:, start : start + P],
-                        targets[d][:, b * P - first : (b + 1) * P - first],
+                        sum_banks[b][:, t * P : (t + 1) * P],
+                        targets[d][:, b * P : (b + 1) * P],
                         identity[:],
                         start=(d == 0),
                         stop=(d == 1),
                         is_transpose=True,
                     )
 
-        def turn_back(u, tags):
-            for index, (column, width) in enumerate(Z_PIECES[:2]):
-                name = "pairs_%d_%d" % (u, index)
-                pairs = keep.tile([P, 2 * width], BF16, name=name, tag=tags.get(name, name), align_bytes=64)
+        def turn_back(u):
+            for b in range(blocks):
+                pairs = keep.tile([P, 2 * P], BF16, name="pairs_%d_%d" % (u, b))
                 nc.scalar.activation(
-                    pairs[:].rearrange("v (b p e) -> v b p e", p=P, e=2),
-                    sums[index, u].rearrange("v (b e p) -> v b p e", p=P, e=2),
+                    pairs[:].rearrange("v (p e) -> v p e", e=2),
+                    sum_banks[b][:, 2 * u * P : (2 * u + 2) * P].rearrange("v (e p) -> v p e", e=2),
                     COPY,
                 )
-                for b in range(width // P):
-                    start = u * width + b * P
-                    nc.tensor.transpose(
-                        back_banks[index][:, start : start + P], pairs[:].bitcast(F32)[:, b * P : (b + 1) * P], identity[:]
-                    )
+                column, width = Z_PIECES[b // 2]
+                start = u * width + b * P - column
+                nc.tensor.transpose(back_banks[b // 2][:, start : start + P], pairs[:].bitcast(F32), identity[:])
 
         def make_h(t):
             banks = [bank(3 * (t % 2) + s, "h_bank_%d_%d" % (t, s)) for s in range(S // BANK)]
@@ -242,42 +237,25 @@ def tile_picked_hop2_relu_e_kernel(
                     first_product(banks[s][:], t, g, s * BANK)
                 nc.scalar.activation(h_tiles[t][:, s * BANK : (s + 1) * BANK], banks[s][:], RELU)
 
-        def turned_columns(t, first=0, count=TURNED, tags=None):
-            names = ["term_%d_%d_%d" % (t, d, first) for d in range(2)]
-            targets = [keep.tile([P, count], F32, name=names[d], tag=(tags or names)[d], align_bytes=64)[:] for d in range(2)]
-            gather_terms(targets, t, first, count, [tile[:, first : first + count] for tile in gate_turned])
+        def turned_columns(t):
+            targets = [keep.tile([P, TURNED], F32, name="term_%d_%d" % (t, d))[:] for d in range(2)]
+            gather_terms(targets, t, 0, TURNED, [tile[:] for tile in gate_turned])
             return targets
 
-        rest = V - TURNED
         first_terms = turned_columns(0)
         make_h(2)
         make_h(3)
-        sums[0, 0] = bank(5, "sum_bank_0_0")[:]
-        sums[1, 0] = bank(6, "sum_bank_1_0")[:, : 2 * P]
         turn_terms(first_terms, 0)
         turn_terms(turned_columns(1), 1)
-        plain_bank = bank(7, "plain_bank")
-        for t in range(PACK):
-            plain = keep.tile([P, rest], F32, name="plain_%d" % t, tag="plain_%d" % t, align_bytes=64)
-            nc.scalar.activation(plain[:], h_tiles[t][:].indirect(entries(pos_tiles[1], TURNED, rest)), COPY)
-            nc.tensor.transpose(plain_bank[:, t * P : (t + 1) * P], plain[:], identity[:])
-        scaled = keep.tile([P, PACK * P], F32, name="scaled")
-        nc.scalar.activation(scaled[:], plain_bank[:], COPY, scale=gate_column[:])
-        scaled_bank = bank(2, "scaled_bank")
-        for t in range(PACK):
-            nc.tensor.transpose(scaled_bank[:, t * P : (t + 1) * P], scaled[:, t * P : (t + 1) * P], identity[:])
-        back_banks = [bank(0, "back_bank_0"), bank(1, "back_bank_1")]
-        turn_back(0, {"pairs_0_0": "plain_3", "pairs_0_1": "plain_0"})
-        sums[0, 1] = bank(7, "sum_bank_0_1")[:]
-        sums[1, 1] = bank(5, "sum_bank_1_1")[:, : 2 * P]
+        back_banks = [bank(2, "back_bank_0"), bank(0, "back_bank_1")]
+        turn_back(0)
         turn_terms(turned_columns(2), 2)
-        for (column, width), tags in zip(Z_PIECES[:2], (None, None)):
-            turn_terms(turned_columns(3, column, width, tags), 3, column, width)
-        turn_back(1, {})
+        turn_terms(turned_columns(3), 3)
+        turn_back(1)
 
         z_grouped = [
-            keep.tile([P, width * PACK], BF16, name="z_grouped_%d" % column, tag=tag, align_bytes=64)
-            for (column, width), tag in zip(Z_PIECES[:2], ("z_grouped_0", "z_grouped_1"))
+            keep.tile([P, width * PACK], BF16, name="z_grouped_%d" % column, tag="z_grouped_%d" % column, align_bytes=64)
+            for column, width in Z_PIECES[:2]
         ]
         for index in range(2):
             width = Z_PIECES[index][1]
@@ -286,11 +264,13 @@ def tile_picked_hop2_relu_e_kernel(
                 back_banks[index][:, : 2 * width].rearrange("p (u v) -> p v u", u=2),
             )
 
-        rest_terms = keep.tile([P, PACK, rest], F32, name="rest_terms", tag="gate_turned_0", align_bytes=64)
+        rest = V - TURNED
+        rest_terms = [
+            keep.tile([P, PACK, rest], F32, name="rest_terms_%d" % d, tag="gate_turned_%d" % d, align_bytes=64)
+            for d in range(2)
+        ]
         for t in range(PACK):
-            nc.vector.tensor_tensor(
-                rest_terms[:, t, :], h_tiles[t][:].indirect(entries(pos_tiles[0], TURNED, rest)), gate_rest[:], MULT
-            )
+            gather_terms([rest_terms[d][:, t, :] for d in range(2)], t, TURNED, rest, [gate_rest[:, d, :] for d in range(2)])
         z_codes, z_scales = {}, {}
 
         def quantize_z(index, tag):
@@ -299,16 +279,16 @@ def tile_picked_hop2_relu_e_kernel(
             z_scales[index] = keep.tile([P, width], U8, name="z_scales_%d" % column, align_bytes=64)
             nc.vector.quantize_mx(out=z_codes[index][:].bitcast(FP8X4), scales=z_scales[index][:], in_=z_grouped[index][:])
 
-        z_grouped.append(keep.tile([P, rest * PACK], BF16, name="z_grouped_rest", align_bytes=64))
+        quantize_z(0, "z_codes_0")
+        z_grouped.append(keep.tile([P, rest * PACK], BF16, name="z_grouped_rest", tag="z_grouped_0", align_bytes=64))
         nc.vector.tensor_tensor(
             z_grouped[2][:].rearrange("p (c i t) -> p c t i", i=LINE, t=PACK),
-            scaled_bank[:].rearrange("p (t c i) -> p c t i", t=PACK, i=LINE),
-            rest_terms[:].rearrange("p t (c i) -> p c t i", i=LINE),
+            rest_terms[0][:].rearrange("p t (c i) -> p c t i", i=LINE),
+            rest_terms[1][:].rearrange("p t (c i) -> p c t i", i=LINE),
             ADD,
         )
-        quantize_z(0, "z_codes_0")
-        quantize_z(2, "z_codes_2")
         quantize_z(1, "z_codes_1")
+        quantize_z(2, "z_codes_2")
 
         def second_product(target, m, index):
             nc.tensor.matmul_mx(
@@ -327,8 +307,8 @@ def tile_picked_hop2_relu_e_kernel(
             first_bank = bank(3 + m, "g_bank_first_%d" % m)
             second_product(first_bank[:, :half], m, 0)
             nc.scalar.activation(g_tiles[m][:, :half], first_bank[:, :half], RELU)
-        last_bank = bank(0, "g_bank_last_1")
-        for index, number in ((2, 1), (1, 5)):
+        last_bank = bank(5, "g_bank_last_1")
+        for index, number in ((1, 1), (2, 6)):
             column, width = Z_PIECES[index]
             piece_bank = bank(number, "g_bank_0_%d" % index)
             second_product(piece_bank[:, :width], 0, index)

@@ -194,8 +194,11 @@ def tile_picked_hop2_relu_e_kernel(
             first_product(second_banks[s][:], 1, 1, s * BANK)
             nc.scalar.activation(h_tiles[1][:, s * BANK : (s + 1) * BANK], second_banks[s][:], RELU)
 
-        blocks = TURNED // P
-        sum_banks = [bank(5 + b, "sum_bank_%d" % b) for b in range(blocks)]
+        sums = {}
+        short_bank = bank(6, "sum_bank_1")
+        for u in range(2):
+            sums[0, u] = bank(5 + 2 * u, "sum_bank_0_%d" % u)[:]
+            sums[1, u] = short_bank[:, 2 * u * P : 2 * (u + 1) * P]
 
         def gather_terms(targets, t, first, count, gate_tile):
             for d in range(2):
@@ -206,12 +209,13 @@ def tile_picked_hop2_relu_e_kernel(
                     MULT,
                 )
 
-        def turn_terms(targets, t):
-            for d in range(2):
-                for b in range(blocks):
+        def turn_terms(targets, t, first=0, count=TURNED):
+            for b in range(first // P, (first + count) // P):
+                start = (2 * (b % 2) + t % 2) * P
+                for d in range(2):
                     nc.tensor.matmul(
-                        sum_banks[b][:, t * P : (t + 1) * P],
-                        targets[d][:, b * P : (b + 1) * P],
+                        sums[b // 2, t // 2][:, start : start + P],
+                        targets[d][:, b * P - first : (b + 1) * P - first],
                         identity[:],
                         start=(d == 0),
                         stop=(d == 1),
@@ -219,16 +223,18 @@ def tile_picked_hop2_relu_e_kernel(
                     )
 
         def turn_back(u):
-            for b in range(blocks):
-                pairs = keep.tile([P, 2 * P], BF16, name="pairs_%d_%d" % (u, b))
+            for index, (column, width) in enumerate(Z_PIECES[:2]):
+                pairs = keep.tile([P, 2 * width], BF16, name="pairs_%d_%d" % (u, index))
                 nc.scalar.activation(
-                    pairs[:].rearrange("v (p e) -> v p e", e=2),
-                    sum_banks[b][:, 2 * u * P : (2 * u + 2) * P].rearrange("v (e p) -> v p e", e=2),
+                    pairs[:].rearrange("v (b p e) -> v b p e", p=P, e=2),
+                    sums[index, u].rearrange("v (b e p) -> v b p e", p=P, e=2),
                     COPY,
                 )
-                column, width = Z_PIECES[b // 2]
-                start = u * width + b * P - column
-                nc.tensor.transpose(back_banks[b // 2][:, start : start + P], pairs[:].bitcast(F32), identity[:])
+                for b in range(width // P):
+                    start = u * width + b * P
+                    nc.tensor.transpose(
+                        back_banks[index][:, start : start + P], pairs[:].bitcast(F32)[:, b * P : (b + 1) * P], identity[:]
+                    )
 
         def make_h(t):
             banks = [bank(3 * (t % 2) + s, "h_bank_%d_%d" % (t, s)) for s in range(S // BANK)]
@@ -237,9 +243,9 @@ def tile_picked_hop2_relu_e_kernel(
                     first_product(banks[s][:], t, g, s * BANK)
                 nc.scalar.activation(h_tiles[t][:, s * BANK : (s + 1) * BANK], banks[s][:], RELU)
 
-        def turned_columns(t):
-            targets = [keep.tile([P, TURNED], F32, name="term_%d_%d" % (t, d))[:] for d in range(2)]
-            gather_terms(targets, t, 0, TURNED, [tile[:] for tile in gate_turned])
+        def turned_columns(t, first=0, count=TURNED):
+            targets = [keep.tile([P, count], F32, name="term_%d_%d_%d" % (t, d, first))[:] for d in range(2)]
+            gather_terms(targets, t, first, count, [tile[:, first : first + count] for tile in gate_turned])
             return targets
 
         first_terms = turned_columns(0)
@@ -247,10 +253,15 @@ def tile_picked_hop2_relu_e_kernel(
         make_h(3)
         turn_terms(first_terms, 0)
         turn_terms(turned_columns(1), 1)
+        rest = V - TURNED
+        plain = keep.tile([P, PACK, rest], F32, name="plain")
+        for t in range(PACK):
+            nc.scalar.activation(plain[:, t, :], h_tiles[t][:].indirect(entries(pos_tiles[1], TURNED, rest)), COPY)
         back_banks = [bank(2, "back_bank_0"), bank(0, "back_bank_1")]
         turn_back(0)
         turn_terms(turned_columns(2), 2)
-        turn_terms(turned_columns(3), 3)
+        for column, width in Z_PIECES[:2]:
+            turn_terms(turned_columns(3, column, width), 3, column, width)
         turn_back(1)
 
         z_grouped = [
@@ -264,13 +275,18 @@ def tile_picked_hop2_relu_e_kernel(
                 back_banks[index][:, : 2 * width].rearrange("p (u v) -> p v u", u=2),
             )
 
-        rest = V - TURNED
         rest_terms = [
             keep.tile([P, PACK, rest], F32, name="rest_terms_%d" % d, tag="gate_turned_%d" % d, align_bytes=64)
             for d in range(2)
         ]
         for t in range(PACK):
-            gather_terms([rest_terms[d][:, t, :] for d in range(2)], t, TURNED, rest, [gate_rest[:, d, :] for d in range(2)])
+            if t == PACK - 1:
+                nc.vector.tensor_tensor(
+                    rest_terms[1][:], plain[:], gate_rest[:, 1:2, :].to_broadcast([P, PACK, rest]), MULT
+                )
+            nc.vector.tensor_tensor(
+                rest_terms[0][:, t, :], h_tiles[t][:].indirect(entries(pos_tiles[0], TURNED, rest)), gate_rest[:, 0, :], MULT
+            )
         z_codes, z_scales = {}, {}
 
         def quantize_z(index, tag):

@@ -31,8 +31,8 @@ SCALE_ROWS = 4
 VECTOR_ENTRIES = ((384, 384, 384, 384), (0, 128, 384, 256))
 PIECE = 256
 ENTRY_PIECES = ((0, 512), (512, 256), (768, 256))
-TURNED = 384
-Z_PIECES = ((0, 256), (256, 128), (TURNED, V - TURNED))
+TURNED = 256
+Z_PIECES = ((0, TURNED), (TURNED, P), (TURNED + P, P))
 
 
 def tile_picked_hop2_relu_e_kernel(
@@ -194,47 +194,9 @@ def tile_picked_hop2_relu_e_kernel(
             first_product(second_banks[s][:], 1, 1, s * BANK)
             nc.scalar.activation(h_tiles[1][:, s * BANK : (s + 1) * BANK], second_banks[s][:], RELU)
 
-        sums = {}
-        short_bank = bank(6, "sum_bank_1")
-        for u in range(2):
-            sums[0, u] = bank(5 + 2 * u, "sum_bank_0_%d" % u)[:]
-            sums[1, u] = short_bank[:, 2 * u * P : 2 * (u + 1) * P]
-
-        def gather_terms(targets, t, first, count, gate_tile):
-            for d in range(2):
-                nc.vector.tensor_tensor(
-                    targets[d],
-                    h_tiles[t][:].indirect(entries(pos_tiles[d], first, count)),
-                    gate_tile[d],
-                    MULT,
-                )
-
-        def turn_terms(targets, t, first=0, count=TURNED):
-            for b in range(first // P, (first + count) // P):
-                start = (2 * (b % 2) + t % 2) * P
-                for d in range(2):
-                    nc.tensor.matmul(
-                        sums[b // 2, t // 2][:, start : start + P],
-                        targets[d][:, b * P - first : (b + 1) * P - first],
-                        identity[:],
-                        start=(d == 0),
-                        stop=(d == 1),
-                        is_transpose=True,
-                    )
-
-        def turn_back(u):
-            for index, (column, width) in enumerate(Z_PIECES[:2]):
-                pairs = keep.tile([P, 2 * width], BF16, name="pairs_%d_%d" % (u, index))
-                nc.scalar.activation(
-                    pairs[:].rearrange("v (b p e) -> v b p e", p=P, e=2),
-                    sums[index, u].rearrange("v (b e p) -> v b p e", p=P, e=2),
-                    COPY,
-                )
-                for b in range(width // P):
-                    start = u * width + b * P
-                    nc.tensor.transpose(
-                        back_banks[index][:, start : start + P], pairs[:].bitcast(F32)[:, b * P : (b + 1) * P], identity[:]
-                    )
+        blocks = TURNED // P
+        rest = V - TURNED
+        sum_banks = [bank(5 + b, "sum_bank_%d" % b) for b in range(blocks)]
 
         def make_h(t):
             banks = [bank(3 * (t % 2) + s, "h_bank_%d_%d" % (t, s)) for s in range(S // BANK)]
@@ -243,68 +205,100 @@ def tile_picked_hop2_relu_e_kernel(
                     first_product(banks[s][:], t, g, s * BANK)
                 nc.scalar.activation(h_tiles[t][:, s * BANK : (s + 1) * BANK], banks[s][:], RELU)
 
-        def turned_columns(t, first=0, count=TURNED):
-            targets = [keep.tile([P, count], F32, name="term_%d_%d_%d" % (t, d, first))[:] for d in range(2)]
-            gather_terms(targets, t, first, count, [tile[:, first : first + count] for tile in gate_turned])
-            return targets
+        def gather_turned(t):
+            terms = [keep.tile([P, TURNED], F32, name="term_%d_%d" % (t, d)) for d in range(2)]
+            for d in range(2):
+                nc.vector.tensor_tensor(
+                    terms[d][:], h_tiles[t][:].indirect(entries(pos_tiles[d], 0, TURNED)), gate_turned[d][:], MULT
+                )
+            return terms
 
-        first_terms = turned_columns(0)
+        def turn(terms, t):
+            for d in range(2):
+                for b in range(blocks):
+                    nc.tensor.matmul(
+                        sum_banks[b][:, t * P : (t + 1) * P],
+                        terms[d][:, b * P : (b + 1) * P],
+                        identity[:],
+                        start=(d == 0),
+                        stop=(d == 1),
+                        is_transpose=True,
+                    )
+
+        def turn_back(u):
+            for b in range(blocks):
+                name = "pairs_%d_%d" % (u, b)
+                pairs = keep.tile([P, 2 * P], BF16, name=name, tag=name, align_bytes=64)
+                nc.scalar.activation(
+                    pairs[:].rearrange("v (p e) -> v p e", e=2),
+                    sum_banks[b][:, 2 * u * P : (2 * u + 2) * P].rearrange("v (e p) -> v p e", e=2),
+                    COPY,
+                )
+                start = u * TURNED + b * P
+                nc.tensor.transpose(back_bank[:, start : start + P], pairs[:].bitcast(F32), identity[:])
+
+        plain = keep.tile([P, PACK, rest], F32, name="plain")
+
+        def gather_plain(t):
+            nc.scalar.activation(plain[:, t, :], h_tiles[t][:].indirect(entries(pos_tiles[1], TURNED, rest)), COPY)
+
+        first_terms = gather_turned(0)
         make_h(2)
         make_h(3)
-        turn_terms(first_terms, 0)
-        turn_terms(turned_columns(1), 1)
-        rest = V - TURNED
-        plain = keep.tile([P, PACK, rest], F32, name="plain")
-        for t in range(PACK):
-            nc.scalar.activation(plain[:, t, :], h_tiles[t][:].indirect(entries(pos_tiles[1], TURNED, rest)), COPY)
-        back_banks = [bank(2, "back_bank_0"), bank(0, "back_bank_1")]
+        turn(first_terms, 0)
+        turn(gather_turned(1), 1)
+        back_bank = bank(2, "back_bank")
         turn_back(0)
-        turn_terms(turned_columns(2), 2)
-        for column, width in Z_PIECES[:2]:
-            turn_terms(turned_columns(3, column, width), 3, column, width)
+        gather_plain(0)
+        gather_plain(1)
+        turn(gather_turned(2), 2)
+        turn(gather_turned(3), 3)
         turn_back(1)
-
-        z_grouped = [
-            keep.tile([P, width * PACK], BF16, name="z_grouped_%d" % column, tag="z_grouped_%d" % column, align_bytes=64)
-            for column, width in Z_PIECES[:2]
-        ]
-        for index in range(2):
-            width = Z_PIECES[index][1]
-            nc.scalar.copy(
-                z_grouped[index][:].bitcast(F32).rearrange("p (v u) -> p v u", u=2),
-                back_banks[index][:, : 2 * width].rearrange("p (u v) -> p v u", u=2),
-            )
+        gather_plain(2)
+        gather_plain(3)
+        z_turned = keep.tile([P, TURNED * PACK], BF16, name="z_turned", align_bytes=64)
+        nc.scalar.copy(
+            z_turned[:].bitcast(F32).rearrange("p (v u) -> p v u", u=2),
+            back_bank[:].rearrange("p (u v) -> p v u", u=2),
+        )
 
         rest_terms = [
             keep.tile([P, PACK, rest], F32, name="rest_terms_%d" % d, tag="gate_turned_%d" % d, align_bytes=64)
             for d in range(2)
         ]
         for t in range(PACK):
-            if t == PACK - 1:
-                nc.vector.tensor_tensor(
-                    rest_terms[1][:], plain[:], gate_rest[:, 1:2, :].to_broadcast([P, PACK, rest]), MULT
-                )
             nc.vector.tensor_tensor(
                 rest_terms[0][:, t, :], h_tiles[t][:].indirect(entries(pos_tiles[0], TURNED, rest)), gate_rest[:, 0, :], MULT
             )
+        for first in (0, P):
+            cols = slice(first, first + P)
+            nc.vector.tensor_tensor(
+                rest_terms[1][:, :, cols], plain[:, :, cols], gate_rest[:, 1:2, cols].to_broadcast([P, PACK, P]), MULT
+            )
+        z_rest = keep.tile([P, rest * PACK], BF16, name="z_rest", tag="pairs_1_1", align_bytes=64)
+        z_grouped = [z_turned[:], z_rest[:, : P * PACK], z_rest[:, P * PACK :]]
         z_codes, z_scales = {}, {}
 
-        def quantize_z(index, tag):
-            column, width = Z_PIECES[index]
-            z_codes[index] = keep.tile([P, width], U32, name="z_codes_%d" % column, tag=tag, align_bytes=64)
-            z_scales[index] = keep.tile([P, width], U8, name="z_scales_%d" % column, align_bytes=64)
-            nc.vector.quantize_mx(out=z_codes[index][:].bitcast(FP8X4), scales=z_scales[index][:], in_=z_grouped[index][:])
+        def add_rest(index):
+            cols = slice(Z_PIECES[index][0] - TURNED, Z_PIECES[index][0] - TURNED + P)
+            nc.vector.tensor_tensor(
+                z_grouped[index].rearrange("p (c i t) -> p c t i", i=LINE, t=PACK),
+                rest_terms[0][:, :, cols].rearrange("p t (c i) -> p c t i", i=LINE),
+                rest_terms[1][:, :, cols].rearrange("p t (c i) -> p c t i", i=LINE),
+                ADD,
+            )
 
-        quantize_z(0, "z_codes_0")
-        z_grouped.append(keep.tile([P, rest * PACK], BF16, name="z_grouped_rest", tag="z_grouped_0", align_bytes=64))
-        nc.vector.tensor_tensor(
-            z_grouped[2][:].rearrange("p (c i t) -> p c t i", i=LINE, t=PACK),
-            rest_terms[0][:].rearrange("p t (c i) -> p c t i", i=LINE),
-            rest_terms[1][:].rearrange("p t (c i) -> p c t i", i=LINE),
-            ADD,
-        )
-        quantize_z(1, "z_codes_1")
-        quantize_z(2, "z_codes_2")
+        def quantize_z(index):
+            column, width = Z_PIECES[index]
+            z_codes[index] = keep.tile([P, width], U32, name="z_codes_%d" % column, align_bytes=64)
+            z_scales[index] = keep.tile([P, width], U8, name="z_scales_%d" % column, align_bytes=64)
+            nc.vector.quantize_mx(out=z_codes[index][:].bitcast(FP8X4), scales=z_scales[index][:], in_=z_grouped[index])
+
+        quantize_z(0)
+        add_rest(1)
+        add_rest(2)
+        quantize_z(1)
+        quantize_z(2)
 
         def second_product(target, m, index):
             nc.tensor.matmul_mx(
@@ -323,8 +317,8 @@ def tile_picked_hop2_relu_e_kernel(
             first_bank = bank(3 + m, "g_bank_first_%d" % m)
             second_product(first_bank[:, :half], m, 0)
             nc.scalar.activation(g_tiles[m][:, :half], first_bank[:, :half], RELU)
-        last_bank = bank(5, "g_bank_last_1")
-        for index, number in ((1, 1), (2, 6)):
+        last_bank = bank(7, "g_bank_last_1")
+        for index, number in ((1, 1), (2, 0)):
             column, width = Z_PIECES[index]
             piece_bank = bank(number, "g_bank_0_%d" % index)
             second_product(piece_bank[:, :width], 0, index)

@@ -28,7 +28,7 @@ BANK = 512
 QUADRANT = 32
 SCALE_ROWS = 4
 
-VECTOR_ENTRIES = ((384, 384, 384, 384), (0, 128, 384, 256))
+VECTOR_ENTRIES = ((384, 384, 512, 512), (0, 128, 384, 256))
 PIECE = 256
 ENTRY_PIECES = ((0, 512), (512, 256), (768, 256))
 TURNED = 256
@@ -68,7 +68,8 @@ def tile_picked_hop2_relu_e_kernel(
             rows = xT[g * K_PASS : (g + 1) * K_PASS, :].rearrange("(p j) c -> p j c", j=PACK)
             for j in range(PACK):
                 x_raw[g, j] = keep.tile([P, T], F32, name="x_raw_%d_%d" % (g, j), align_bytes=64)
-                nc.sync.dma_start(x_raw[g, j][:], rows[:, j, :])
+                queue = nc.scalar if g == 0 and j % 2 == 1 else nc.sync
+                queue.dma_start(x_raw[g, j][:], rows[:, j, :])
         for g in range(PASSES):
             nc.sync.dma_start(w_raw[g][:], w1[g * K_PASS : (g + 1) * K_PASS, :].rearrange("(p j) c -> p j c", j=PACK))
         pos_tiles = [load_list("pos1_tile", pos1), load_list("pos2_tile", pos2)]

@@ -28,7 +28,7 @@ BANK = 512
 QUADRANT = 32
 SCALE_ROWS = 4
 
-VECTOR_ENTRIES = ((384, 384, 512, 512), (0, 128, 384, 256))
+VECTOR_ENTRIES = ((512, 512, 512, 576), (0, 512, 640, 256))
 PIECE = 256
 ENTRY_PIECES = ((0, 512), (512, 256), (768, 256))
 TURNED = 256
@@ -68,7 +68,7 @@ def tile_picked_hop2_relu_e_kernel(
             rows = xT[g * K_PASS : (g + 1) * K_PASS, :].rearrange("(p j) c -> p j c", j=PACK)
             for j in range(PACK):
                 x_raw[g, j] = keep.tile([P, T], F32, name="x_raw_%d_%d" % (g, j), align_bytes=64)
-                queue = nc.scalar if g == 0 and j % 2 == 1 else nc.sync
+                queue = nc.scalar if (g, j) == (0, 1) else nc.sync
                 queue.dma_start(x_raw[g, j][:], rows[:, j, :])
         for g in range(PASSES):
             nc.sync.dma_start(w_raw[g][:], w1[g * K_PASS : (g + 1) * K_PASS, :].rearrange("(p j) c -> p j c", j=PACK))

@@ -207,7 +207,8 @@ def tile_picked_hop2_relu_e_kernel(
                 nc.scalar.activation(h_tiles[t][:, s * BANK : (s + 1) * BANK], banks[s][:], RELU)
 
         def gather_turned(t):
-            terms = [keep.tile([P, TURNED], F32, name="term_%d_%d" % (t, d)) for d in range(2)]
+            names = ["term_%d_%d" % (t, d) for d in range(2)]
+            terms = [keep.tile([P, TURNED], F32, name=name, tag=name, align_bytes=64) for name in names]
             for d in range(2):
                 nc.vector.tensor_tensor(
                     terms[d][:], h_tiles[t][:].indirect(entries(pos_tiles[d], 0, TURNED)), gate_turned[d][:], MULT
@@ -238,10 +239,8 @@ def tile_picked_hop2_relu_e_kernel(
                 start = u * TURNED + b * P
                 nc.tensor.transpose(back_bank[:, start : start + P], pairs[:].bitcast(F32), identity[:])
 
-        plain = keep.tile([P, PACK, rest], F32, name="plain")
-
-        def gather_plain(t):
-            nc.scalar.activation(plain[:, t, :], h_tiles[t][:].indirect(entries(pos_tiles[1], TURNED, rest)), COPY)
+        def gather_plain(target, t, d):
+            nc.scalar.activation(target, h_tiles[t][:].indirect(entries(pos_tiles[d], TURNED, rest)), COPY)
 
         first_terms = gather_turned(0)
         make_h(2)
@@ -250,31 +249,34 @@ def tile_picked_hop2_relu_e_kernel(
         turn(gather_turned(1), 1)
         back_bank = bank(2, "back_bank")
         turn_back(0)
-        gather_plain(0)
-        gather_plain(1)
+        plain = keep.tile([P, PACK - 1, rest], F32, name="plain", tag="term_1_1", align_bytes=64)
+        for t in range(PACK - 1):
+            gather_plain(plain[:, t, :], t, 1)
         turn(gather_turned(2), 2)
         turn(gather_turned(3), 3)
         turn_back(1)
-        gather_plain(2)
-        gather_plain(3)
+        plain_last = keep.tile([P, 2, rest], F32, name="plain_last", tag="term_3_1", align_bytes=64)
+        gather_plain(plain_last[:, 1, :], PACK - 1, 1)
+        gather_plain(plain_last[:, 0, :], 0, 0)
         z_turned = keep.tile([P, TURNED * PACK], BF16, name="z_turned", align_bytes=64)
         nc.scalar.copy(
             z_turned[:].bitcast(F32).rearrange("p (v u) -> p v u", u=2),
             back_bank[:].rearrange("p (u v) -> p v u", u=2),
         )
 
-        rest_terms = [
-            keep.tile([P, PACK, rest], F32, name="rest_terms_%d" % d, tag="gate_turned_%d" % d, align_bytes=64)
-            for d in range(2)
-        ]
-        for t in range(PACK):
+        both_terms = keep.tile([P, 2 * PACK, rest], F32, name="both_terms", tag="gate_turned_0", align_bytes=64)
+        rest_terms = [both_terms[:, d * PACK : (d + 1) * PACK, :] for d in range(2)]
+        for t in range(1, PACK):
             nc.vector.tensor_tensor(
                 rest_terms[0][:, t, :], h_tiles[t][:].indirect(entries(pos_tiles[0], TURNED, rest)), gate_rest[:, 0, :], MULT
             )
+        nc.vector.tensor_tensor(
+            rest_terms[1][:, : PACK - 1, :], plain[:], gate_rest[:, 1:2, :].to_broadcast([P, PACK - 1, rest]), MULT
+        )
         for first in (0, P):
             cols = slice(first, first + P)
             nc.vector.tensor_tensor(
-                rest_terms[1][:, :, cols], plain[:, :, cols], gate_rest[:, 1:2, cols].to_broadcast([P, PACK, P]), MULT
+                both_terms[:, 0 : 2 * PACK : 2 * PACK - 1, cols], plain_last[:, :, cols], gate_rest[:, :, cols], MULT
             )
         z_rest = keep.tile([P, rest * PACK], BF16, name="z_rest", tag="pairs_1_1", align_bytes=64)
         z_grouped = [z_turned[:], z_rest[:, : P * PACK], z_rest[:, P * PACK :]]

@@ -135,10 +135,16 @@ def tile_picked_hop2_relu_e_kernel(
                 COPY,
             )
 
-        def quantize_w(g, u, tag):
+        def quantize_w(g, u, tag, parts=1):
             w_codes[g, u] = keep.tile([P, 2 * P], U32, name="w_codes_%d_%d" % (g, u), tag=tag, align_bytes=64)
             w_scales[g, u] = keep.tile([P, 2 * P], U8, name="w_scales_%d_%d" % (g, u), align_bytes=64)
-            nc.vector.quantize_mx(out=w_codes[g, u][:].bitcast(FP8X4), scales=w_scales[g, u][:], in_=w_grouped[g, u][:])
+            width = 2 * P // parts
+            for first in range(0, 2 * P, width):
+                nc.vector.quantize_mx(
+                    out=w_codes[g, u][:, first : first + width].bitcast(FP8X4),
+                    scales=w_scales[g, u][:, first : first + width],
+                    in_=w_grouped[g, u][:, first * PACK : (first + width) * PACK],
+                )
 
         for j in range(PACK):
             pick(0, j, S)
@@ -162,7 +168,7 @@ def tile_picked_hop2_relu_e_kernel(
         round_w(0, 1, "w_grouped_0_1")
         quantize_w(0, 1, "w_codes_0_1")
         round_w(1, 0, "w_grouped_1_0")
-        quantize_w(1, 0, "w_codes_1_0")
+        quantize_w(1, 0, "w_codes_1_0", 2)
         round_w(1, 1, "w_grouped_1_1")
 
         def first_product(target, t, g, entry):
@@ -280,7 +286,8 @@ def tile_picked_hop2_relu_e_kernel(
             )
         z_rest = keep.tile([P, rest * PACK], BF16, name="z_rest", tag="pairs_1_1", align_bytes=64)
         z_grouped = [z_turned[:], z_rest[:, : P * PACK], z_rest[:, P * PACK :]]
-        z_codes, z_scales = {}, {}
+        z_codes = keep.tile([P, V], U32, name="z_codes", align_bytes=64)
+        z_scales = keep.tile([P, V], U8, name="z_scales", align_bytes=64)
 
         def add_rest(index):
             cols = slice(Z_PIECES[index][0] - TURNED, Z_PIECES[index][0] - TURNED + P)
@@ -293,9 +300,11 @@ def tile_picked_hop2_relu_e_kernel(
 
         def quantize_z(index):
             column, width = Z_PIECES[index]
-            z_codes[index] = keep.tile([P, width], U32, name="z_codes_%d" % column, align_bytes=64)
-            z_scales[index] = keep.tile([P, width], U8, name="z_scales_%d" % column, align_bytes=64)
-            nc.vector.quantize_mx(out=z_codes[index][:].bitcast(FP8X4), scales=z_scales[index][:], in_=z_grouped[index])
+            nc.vector.quantize_mx(
+                out=z_codes[:, column : column + width].bitcast(FP8X4),
+                scales=z_scales[:, column : column + width],
+                in_=z_grouped[index],
+            )
 
         quantize_z(0)
         add_rest(1)
@@ -303,13 +312,13 @@ def tile_picked_hop2_relu_e_kernel(
         quantize_z(1)
         quantize_z(2)
 
-        def second_product(target, m, index):
+        def second_product(target, m, column):
             nc.tensor.matmul_mx(
                 out=target,
                 lhsT=w2_codes[:, m * P : (m + 1) * P].bitcast(FP8X4),
                 lhsT_scale=w2_scale_tile[:, m * P : (m + 1) * P],
-                rhs=z_codes[index][:].bitcast(FP8X4),
-                rhs_scale=z_scales[index][:],
+                rhs=z_codes[:, column : column + target.shape[1]].bitcast(FP8X4),
+                rhs_scale=z_scales[:, column : column + target.shape[1]],
                 start=True,
                 stop=True,
             )
@@ -324,9 +333,9 @@ def tile_picked_hop2_relu_e_kernel(
         for index, number in ((1, 1), (2, 0)):
             column, width = Z_PIECES[index]
             piece_bank = bank(number, "g_bank_0_%d" % index)
-            second_product(piece_bank[:, :width], 0, index)
+            second_product(piece_bank[:, :width], 0, column)
             nc.scalar.activation(g_tiles[0][:, column : column + width], piece_bank[:, :width], RELU)
-            second_product(last_bank[:, column - half : column - half + width], 1, index)
+        second_product(last_bank[:, :half], 1, half)
         nc.scalar.activation(g_tiles[1][:, half:], last_bank[:, :half], RELU)
 
         root_terms = keep.tile([P, N // P, 2, U], F32, name="root_terms")

@@ -28,7 +28,8 @@ BANK = 512
 QUADRANT = 32
 SCALE_ROWS = 4
 
-VECTOR_ENTRIES = ((512, 512, 512, 576), (0, 512, 640, 256))
+VECTOR_ENTRIES = ((512, 512, 512, 512), (0, 512, 256, 256))
+X_LOADS = ((0, 0, 1), (0, 1, 1), (0, 2, 1), (0, 3, 1), (1, 0, 1), (1, 1, 1), (1, 2, 1), (1, 3, 1))
 PIECE = 256
 ENTRY_PIECES = ((0, 512), (512, 256), (768, 256))
 TURNED = 256
@@ -60,17 +61,17 @@ def tile_picked_hop2_relu_e_kernel(
         make_identity(nc, identity[:])
 
         offs_tile = load_list("offs_tile", offs)
-        x_raw = {}
-        w_raw = [
-            keep.tile([P, PACK, H], F32, name="w_raw_%d" % g, tag="w_raw_%d" % g, align_bytes=64) for g in range(PASSES)
-        ]
-        for g in range(PASSES):
+        planes = {}
+        for g, first, count in X_LOADS:
             rows = xT[g * K_PASS : (g + 1) * K_PASS, :].rearrange("(p j) c -> p j c", j=PACK)
-            for j in range(PACK):
-                x_raw[g, j] = keep.tile([P, T], F32, name="x_raw_%d_%d" % (g, j), align_bytes=64)
-                queue = nc.scalar if (g, j) == (0, 1) else nc.sync
-                queue.dma_start(x_raw[g, j][:], rows[:, j, :])
+            raw = keep.tile([P, count * T], F32, name="x_raw_%d_%d" % (g, first), align_bytes=64)
+            queue = nc.scalar if (g, first) == (0, 1) else nc.sync
+            queue.dma_start(raw[:], rows[:, first : first + count, :].rearrange("p j c -> p (j c)"))
+            for j in range(count):
+                planes[g, first + j] = raw[:, j * T : (j + 1) * T]
+        w_raw = []
         for g in range(PASSES):
+            w_raw.append(keep.tile([P, PACK, H], F32, name="w_raw_%d" % g, tag="w_raw_%d" % g, align_bytes=64))
             nc.sync.dma_start(w_raw[g][:], w1[g * K_PASS : (g + 1) * K_PASS, :].rearrange("(p j) c -> p j c", j=PACK))
         pos_tiles = [load_list("pos1_tile", pos1), load_list("pos2_tile", pos2)]
         gate_turned = []
@@ -92,114 +93,152 @@ def tile_picked_hop2_relu_e_kernel(
         nc.sync.dma_start(gate2_tile[:], gate2.rearrange("d p v -> p d v"))
 
         (first_0, count_0), (first_1, count_1), (first_2, count_2) = ENTRY_PIECES
-        picked = [keep.tile([P, PACK, S], BF16, name="picked_%d" % g, align_bytes=64) for g in range(PASSES)]
-        picked_words = [keep.tile([P, S], U32, name="picked_words_%d" % g, align_bytes=64) for g in range(PASSES)]
+        picked = {}
+        for g, first, count in X_LOADS:
+            if first % 2 == 0:
+                dtype = F32 if count > 1 else BF16
+                picked[g, first // 2] = keep.tile([P, 2, S], dtype, name="picked_%d_%d" % (g, first // 2), align_bytes=64)
+        picked_words = [keep.tile([P, S - g * PIECE], U32, name="picked_words_%d" % g, align_bytes=64) for g in range(PASSES)]
         picked_scales = [keep.tile([P, S], U8, name="picked_scales_%d" % g, align_bytes=64) for g in range(PASSES)]
-        x_grouped = {}
 
         def pick(g, j, piece):
             split = VECTOR_ENTRIES[g][j]
             if split > 0:
-                nc.vector.tensor_copy(picked[g][:, j, :split], x_raw[g, j][:].indirect(entries(offs_tile, 0, split)))
+                nc.vector.tensor_copy(picked[g, j // 2][:, j % 2, :split], planes[g, j].indirect(entries(offs_tile, 0, split)))
             for entry in range(split, S, piece):
                 count = min(piece, S - entry)
                 nc.scalar.activation(
-                    picked[g][:, j, entry : entry + count],
-                    x_raw[g, j][:].indirect(entries(offs_tile, entry, count)),
+                    picked[g, j // 2][:, j % 2, entry : entry + count],
+                    planes[g, j].indirect(entries(offs_tile, entry, count)),
                     COPY,
                 )
 
-        def weave(g, entry, count, tag=None):
-            name = "x_grouped_%d_%d" % (g, entry)
-            x_grouped[g, entry] = keep.tile([P, count * PACK], BF16, name=name, tag=tag or name, align_bytes=64)
+        def weave(target, g, entry, h):
+            width = target.shape[1] // PACK
             nc.vector.tensor_copy(
-                x_grouped[g, entry][:].rearrange("p (c i j) -> p c j i", i=LINE, j=PACK),
-                picked[g][:, :, entry : entry + count].rearrange("p j (c i) -> p c j i", i=LINE),
+                target[:].rearrange("p (c i j) -> p c j i", i=LINE, j=PACK)[:, :, 2 * h : 2 * h + 2, :],
+                picked[g, h][:, :, entry : entry + width].rearrange("p j (c i) -> p c j i", i=LINE),
             )
 
-        def quantize_x(g, entry, count):
+        def quantize_x(source, g, entry, words):
+            width = source.shape[1] // PACK
             nc.vector.quantize_mx(
-                out=picked_words[g][:, entry : entry + count].bitcast(FP8X4),
-                scales=picked_scales[g][:, entry : entry + count],
-                in_=x_grouped[g, entry][:],
+                out=words.bitcast(FP8X4),
+                scales=picked_scales[g][:, entry : entry + width],
+                in_=source[:],
             )
 
-        w_grouped, w_codes, w_scales = {}, {}, {}
+        w_codes, w_scales = {}, {}
 
-        def round_w(g, u, tag):
-            name = "w_grouped_%d_%d" % (g, u)
-            w_grouped[g, u] = keep.tile([P, 2 * P * PACK], BF16, name=name, tag=tag, align_bytes=64)
-            nc.scalar.activation(
-                w_grouped[g, u][:].rearrange("p (e m j) -> p m j e", e=2, j=PACK),
-                w_raw[g][:].rearrange("p j (m t) -> p m j t", t=PACK)[:, :, :, 2 * u : 2 * u + 2],
-                COPY,
+        def w_operands(g, first, count, tag=None):
+            name = "w_codes_%d_%d" % (g, first)
+            codes = keep.tile([P, count * P], U32, name=name, tag=tag or name, align_bytes=64)
+            scales = keep.tile([P, count * P], U8, name="w_scales_%d_%d" % (g, first), align_bytes=64)
+            for t in range(count):
+                w_codes[g, first + t] = codes[:, t * P : (t + 1) * P]
+                w_scales[g, first + t] = scales[:, t * P : (t + 1) * P]
+            return codes[:], scales[:]
+
+        def round_w(engine_copy, g, pairs, first, count):
+            name = "w_grouped_%d_%d_%d" % (g, pairs[0], first)
+            target = keep.tile([P, len(pairs) * 2 * count * PACK], BF16, name=name, tag=name, align_bytes=64)
+            engine_copy(
+                target[:].rearrange("p (u e m j) -> p u m j e", e=2, m=count, j=PACK),
+                w_raw[g][:].rearrange("p j (m u e) -> p u m j e", u=2, e=2)[
+                    :, pairs[0] : pairs[-1] + 1, first : first + count
+                ],
             )
+            return target
 
-        def quantize_w(g, u, tag, parts=1):
-            w_codes[g, u] = keep.tile([P, 2 * P], U32, name="w_codes_%d_%d" % (g, u), tag=tag, align_bytes=64)
-            w_scales[g, u] = keep.tile([P, 2 * P], U8, name="w_scales_%d_%d" % (g, u), align_bytes=64)
-            width = 2 * P // parts
-            for first in range(0, 2 * P, width):
-                nc.vector.quantize_mx(
-                    out=w_codes[g, u][:, first : first + width].bitcast(FP8X4),
-                    scales=w_scales[g, u][:, first : first + width],
-                    in_=w_grouped[g, u][:, first * PACK : (first + width) * PACK],
-                )
+        def scalar_copy(target, source):
+            nc.scalar.activation(target, source, COPY)
 
-        for j in range(PACK):
-            pick(0, j, S)
-        weave(0, 0, S // 2)
-        weave(0, S // 2, S // 2)
-        quantize_x(0, 0, S // 2)
-        quantize_x(0, S // 2, S // 2)
-        for j in range(PACK - 1):
-            pick(1, j, S)
-        pick(1, PACK - 1, PIECE)
-        weave(1, 0, PIECE)
-        weave(1, PIECE, PIECE)
-        quantize_x(1, 0, PIECE)
-        weave(1, 2 * PIECE, PIECE)
-        quantize_x(1, PIECE, PIECE)
-        round_w(0, 0, "w_grouped_0_0")
-        quantize_w(0, 0, "w_codes_0_0")
-        weave(1, 3 * PIECE, PIECE, "w_grouped_0_0")
-        quantize_x(1, 2 * PIECE, PIECE)
-        quantize_x(1, 3 * PIECE, PIECE)
-        round_w(0, 1, "w_grouped_0_1")
-        quantize_w(0, 1, "w_codes_0_1")
-        round_w(1, 0, "w_grouped_1_0")
-        quantize_w(1, 0, "w_codes_1_0", 2)
-        round_w(1, 1, "w_grouped_1_1")
+        def quantize_w(source, codes, scales):
+            nc.vector.quantize_mx(out=codes.bitcast(FP8X4), scales=scales, in_=source)
 
-        def first_product(target, t, g, entry):
-            cols = slice((t % 2) * P, (t % 2 + 1) * P)
+        halves = [keep.tile([P, S // 2 * PACK], BF16, name="x_grouped_0_%d" % n, align_bytes=64) for n in range(2)]
+        for h in range(2):
+            pick(0, 2 * h, S)
+            pick(0, 2 * h + 1, S)
+            for n in range(2):
+                weave(halves[n], 0, n * S // 2, h)
+        for n in range(2):
+            quantize_x(halves[n], 0, n * S // 2, picked_words[0][:, n * S // 2 : (n + 1) * S // 2])
+        pieces = [
+            keep.tile([P, PIECE * PACK], BF16, name="x_grouped_1_%d" % n, tag="x_grouped_1_%d" % n, align_bytes=64)
+            for n in range(S // PIECE)
+        ]
+        pick(1, 0, S)
+        pick(1, 1, S)
+        for n in range(S // PIECE):
+            weave(pieces[n], 1, n * PIECE, 0)
+        pick(1, 2, S)
+        pick(1, 3, 384)
+        weave(pieces[0], 1, 0, 1)
+        weave(pieces[1], 1, PIECE, 1)
+        quantize_x(pieces[0], 1, 0, picked_words[1][:, :PIECE])
+        weave(pieces[2], 1, 2 * PIECE, 1)
+        quantize_x(pieces[1], 1, PIECE, picked_words[1][:, PIECE : 2 * PIECE])
+        weave(pieces[3], 1, 3 * PIECE, 1)
+        quantize_x(pieces[2], 1, 2 * PIECE, picked_words[1][:, 2 * PIECE :])
+        first_pair = round_w(scalar_copy, 0, [0], 0, P)
+        quantize_w(first_pair[:], *w_operands(0, 0, 2))
+        last_words = keep.tile([P, PIECE], U32, name="last_words", tag="w_grouped_0_0_0", align_bytes=64)
+        quantize_x(pieces[3], 1, 3 * PIECE, last_words[:])
+        second_pair = round_w(scalar_copy, 0, [1], 0, P)
+        groups = P // 2
+        lower = round_w(nc.vector.tensor_copy, 1, [0, 1], 0, groups)
+        upper = [round_w(scalar_copy, 1, [u], groups, groups) for u in range(2)]
+
+        def quantize_last(t):
+            width = groups * PACK
+            codes, scales = w_operands(1, t, 1)
+            quantize_w(lower[:, t * width : (t + 1) * width], codes[:, :groups], scales[:, :groups])
+            quantize_w(upper[t // 2][:, (t % 2) * width : (t % 2 + 1) * width], codes[:, groups:], scales[:, groups:])
+
+        quantize_w(second_pair[:], *w_operands(0, 2, 2))
+        quantize_last(0)
+        quantize_last(1)
+
+        def first_product(target, t, g, entry, start, stop):
+            width = target.shape[1]
+            words = last_words[:] if (g, entry) == (1, S - PIECE) else picked_words[g][:, entry : entry + width]
             nc.tensor.matmul_mx(
                 out=target,
-                lhsT=w_codes[g, t // 2][:, cols].bitcast(FP8X4),
-                lhsT_scale=w_scales[g, t // 2][:, cols],
-                rhs=picked_words[g][:, entry : entry + target.shape[1]].bitcast(FP8X4),
-                rhs_scale=picked_scales[g][:, entry : entry + target.shape[1]],
-                start=(g == 0),
-                stop=(g == PASSES - 1),
+                lhsT=w_codes[g, t].bitcast(FP8X4),
+                lhsT_scale=w_scales[g, t],
+                rhs=words.bitcast(FP8X4),
+                rhs_scale=picked_scales[g][:, entry : entry + width],
+                start=start,
+                stop=stop,
             )
+
+        def second_pass(target, t, s, start, stop):
+            if s == 0:
+                first_product(target[:], t, 1, 0, start, stop)
+            else:
+                first_product(target[:, :PIECE], t, 1, BANK, start, False)
+                first_product(target[:, PIECE:], t, 1, BANK + PIECE, False, stop)
 
         h_tiles = [keep.tile([P, S], F32, name="h_%d" % t) for t in range(PACK)]
         h_banks = [bank(index, "h_bank_0_%d" % index) for index in range(len(ENTRY_PIECES))]
         second_banks = [bank(3 + s, "h_bank_1_%d" % s) for s in range(S // BANK)]
         for index, (entry, count) in enumerate(ENTRY_PIECES):
-            first_product(h_banks[index][:, :count], 0, 0, entry)
-        for s in range(S // BANK):
-            first_product(second_banks[s][:], 1, 0, s * BANK)
+            first_product(h_banks[index][:, :count], 0, 0, entry, True, False)
+        first_product(second_banks[0][:], 1, 0, 0, True, False)
         for index in (0, 1, 2):
             entry, count = ENTRY_PIECES[index]
-            first_product(h_banks[index][:, :count], 0, 1, entry)
+            first_product(h_banks[index][:, :count], 0, 1, entry, False, True)
         nc.vector.tensor_scalar_max(h_tiles[0][:, first_0 : first_0 + count_0], h_banks[0][:, :count_0], 0.0)
         nc.scalar.activation(h_tiles[0][:, first_1 : first_1 + count_1], h_banks[1][:, :count_1], RELU)
         nc.scalar.activation(h_tiles[0][:, first_2:], h_banks[2][:, :count_2], RELU)
-        quantize_w(1, 1, "w_grouped_0_1")
-        for s in range(S // BANK):
-            first_product(second_banks[s][:], 1, 1, s * BANK)
-            nc.scalar.activation(h_tiles[1][:, s * BANK : (s + 1) * BANK], second_banks[s][:], RELU)
+        quantize_last(2)
+        quantize_last(3)
+        second_pass(second_banks[0], 1, 0, False, True)
+        nc.scalar.activation(h_tiles[1][:, :BANK], second_banks[0][:], RELU)
+        second_pass(second_banks[1], 1, 1, True, False)
+        first_product(second_banks[1][:], 1, 0, BANK, False, True)
+        nc.scalar.activation(h_tiles[1][:, BANK:], second_banks[1][:], RELU)
 
         blocks = TURNED // P
         rest = V - TURNED
@@ -208,8 +247,8 @@ def tile_picked_hop2_relu_e_kernel(
         def make_h(t):
             banks = [bank(3 * (t % 2) + s, "h_bank_%d_%d" % (t, s)) for s in range(S // BANK)]
             for s in range(S // BANK):
-                for g in range(PASSES):
-                    first_product(banks[s][:], t, g, s * BANK)
+                first_product(banks[s][:], t, 0, s * BANK, True, False)
+                second_pass(banks[s], t, s, False, True)
                 nc.scalar.activation(h_tiles[t][:, s * BANK : (s + 1) * BANK], banks[s][:], RELU)
 
         def gather_turned(t):

@@ -28,7 +28,7 @@ BANK = 512
 QUADRANT = 32
 SCALE_ROWS = 4
 
-VECTOR_ENTRIES = ((512, 512, 512, 512), (0, 512, 256, 256))
+VECTOR_ENTRIES = ((384, 384, 384, 384), (0, 384, 256, 256))
 X_LOADS = ((0, 0, 1), (0, 1, 1), (0, 2, 1), (0, 3, 1), (1, 0, 1), (1, 1, 1), (1, 2, 1), (1, 3, 1))
 PIECE = 256
 ENTRY_PIECES = ((0, 512), (512, 256), (768, 256))

@@ -31,7 +31,7 @@ SCALE_ROWS = 4
 VECTOR_ENTRIES = ((384, 384, 384, 384), (0, 384, 256, 256))
 X_LOADS = ((0, 0, 1), (0, 1, 1), (0, 2, 1), (0, 3, 1), (1, 0, 1), (1, 1, 1), (1, 2, 1), (1, 3, 1))
 PIECE = 256
-ENTRY_PIECES = ((0, 512), (512, 256), (768, 256))
+ENTRY_PIECES = ((0, 256), (256, 256), (512, 256), (768, 256))
 TURNED = 256
 Z_PIECES = ((0, TURNED), (TURNED, P), (TURNED + P, P))
 
@@ -92,13 +92,12 @@ def tile_picked_hop2_relu_e_kernel(
         gate2_tile = keep.tile([P, 2, U], F32, name="gate2_tile", tag="gate2_tile")
         nc.sync.dma_start(gate2_tile[:], gate2.rearrange("d p v -> p d v"))
 
-        (first_0, count_0), (first_1, count_1), (first_2, count_2) = ENTRY_PIECES
         picked = {}
         for g, first, count in X_LOADS:
             if first % 2 == 0:
                 dtype = F32 if count > 1 else BF16
                 picked[g, first // 2] = keep.tile([P, 2, S], dtype, name="picked_%d_%d" % (g, first // 2), align_bytes=64)
-        picked_words = [keep.tile([P, S - g * PIECE], U32, name="picked_words_%d" % g, align_bytes=64) for g in range(PASSES)]
+        picked_words = [keep.tile([P, S - g * BANK], U32, name="picked_words_%d" % g, align_bytes=64) for g in range(PASSES)]
         picked_scales = [keep.tile([P, S], U8, name="picked_scales_%d" % g, align_bytes=64) for g in range(PASSES)]
 
         def pick(g, j, piece):
@@ -180,11 +179,11 @@ def tile_picked_hop2_relu_e_kernel(
         weave(pieces[2], 1, 2 * PIECE, 1)
         quantize_x(pieces[1], 1, PIECE, picked_words[1][:, PIECE : 2 * PIECE])
         weave(pieces[3], 1, 3 * PIECE, 1)
-        quantize_x(pieces[2], 1, 2 * PIECE, picked_words[1][:, 2 * PIECE :])
         first_pair = round_w(scalar_copy, 0, [0], 0, P)
         quantize_w(first_pair[:], *w_operands(0, 0, 2))
-        last_words = keep.tile([P, PIECE], U32, name="last_words", tag="w_grouped_0_0_0", align_bytes=64)
-        quantize_x(pieces[3], 1, 3 * PIECE, last_words[:])
+        last_words = keep.tile([P, BANK], U32, name="last_words", tag="w_grouped_0_0_0", align_bytes=64)
+        quantize_x(pieces[2], 1, 2 * PIECE, last_words[:, :PIECE])
+        quantize_x(pieces[3], 1, 3 * PIECE, last_words[:, PIECE:])
         second_pair = round_w(scalar_copy, 0, [1], 0, P)
         groups = P // 2
         lower = round_w(nc.vector.tensor_copy, 1, [0, 1], 0, groups)
@@ -196,13 +195,16 @@ def tile_picked_hop2_relu_e_kernel(
             quantize_w(lower[:, t * width : (t + 1) * width], codes[:, :groups], scales[:, :groups])
             quantize_w(upper[t // 2][:, (t % 2) * width : (t % 2 + 1) * width], codes[:, groups:], scales[:, groups:])
 
-        quantize_w(second_pair[:], *w_operands(0, 2, 2))
         quantize_last(0)
         quantize_last(1)
+        quantize_w(second_pair[:], *w_operands(0, 2, 2, "w_grouped_1_0_%d" % groups))
 
         def first_product(target, t, g, entry, start, stop):
             width = target.shape[1]
-            words = last_words[:] if (g, entry) == (1, S - PIECE) else picked_words[g][:, entry : entry + width]
+            if g == 1 and entry >= BANK:
+                words = last_words[:, entry - BANK : entry - BANK + width]
+            else:
+                words = picked_words[g][:, entry : entry + width]
             nc.tensor.matmul_mx(
                 out=target,
                 lhsT=w_codes[g, t].bitcast(FP8X4),
@@ -214,27 +216,25 @@ def tile_picked_hop2_relu_e_kernel(
             )
 
         def second_pass(target, t, s, start, stop):
-            if s == 0:
-                first_product(target[:], t, 1, 0, start, stop)
-            else:
-                first_product(target[:, :PIECE], t, 1, BANK, start, False)
-                first_product(target[:, PIECE:], t, 1, BANK + PIECE, False, stop)
+            first_product(target[:], t, 1, s * BANK, start, stop)
 
         h_tiles = [keep.tile([P, S], F32, name="h_%d" % t) for t in range(PACK)]
-        h_banks = [bank(index, "h_bank_0_%d" % index) for index in range(len(ENTRY_PIECES))]
+        h_banks = [bank(number, "h_bank_0_%d" % number) for number in (0, 1, 2, 7)]
         second_banks = [bank(3 + s, "h_bank_1_%d" % s) for s in range(S // BANK)]
         for index, (entry, count) in enumerate(ENTRY_PIECES):
             first_product(h_banks[index][:, :count], 0, 0, entry, True, False)
-        first_product(second_banks[0][:], 1, 0, 0, True, False)
-        for index in (0, 1, 2):
-            entry, count = ENTRY_PIECES[index]
+        first_product(second_banks[0][:, :PIECE], 1, 0, 0, True, False)
+        for index, (entry, count) in enumerate(ENTRY_PIECES):
             first_product(h_banks[index][:, :count], 0, 1, entry, False, True)
-        nc.vector.tensor_scalar_max(h_tiles[0][:, first_0 : first_0 + count_0], h_banks[0][:, :count_0], 0.0)
-        nc.scalar.activation(h_tiles[0][:, first_1 : first_1 + count_1], h_banks[1][:, :count_1], RELU)
-        nc.scalar.activation(h_tiles[0][:, first_2:], h_banks[2][:, :count_2], RELU)
+            if index % 2 == 0:
+                nc.vector.tensor_scalar_max(h_tiles[0][:, entry : entry + count], h_banks[index][:, :count], 0.0)
+            else:
+                nc.scalar.activation(h_tiles[0][:, entry : entry + count], h_banks[index][:, :count], RELU)
         quantize_last(2)
         quantize_last(3)
-        second_pass(second_banks[0], 1, 0, False, True)
+        first_product(second_banks[0][:, PIECE:], 1, 1, PIECE, False, False)
+        first_product(second_banks[0][:, :PIECE], 1, 1, 0, False, False)
+        first_product(second_banks[0][:, PIECE:], 1, 0, PIECE, False, True)
         nc.scalar.activation(h_tiles[1][:, :BANK], second_banks[0][:], RELU)
         second_pass(second_banks[1], 1, 1, True, False)
         first_product(second_banks[1][:], 1, 0, BANK, False, True)
@@ -318,11 +318,7 @@ def tile_picked_hop2_relu_e_kernel(
         nc.vector.tensor_tensor(
             rest_terms[1][:, : PACK - 1, :], plain[:], gate_rest[:, 1:2, :].to_broadcast([P, PACK - 1, rest]), MULT
         )
-        for first in (0, P):
-            cols = slice(first, first + P)
-            nc.vector.tensor_tensor(
-                both_terms[:, 0 : 2 * PACK : 2 * PACK - 1, cols], plain_last[:, :, cols], gate_rest[:, :, cols], MULT
-            )
+        nc.vector.tensor_tensor(both_terms[:, 0 : 2 * PACK : 2 * PACK - 1, :], plain_last[:], gate_rest[:], MULT)
         z_rest = keep.tile([P, rest * PACK], BF16, name="z_rest", tag="pairs_1_1", align_bytes=64)
         z_grouped = [z_turned[:], z_rest[:, : P * PACK], z_rest[:, P * PACK :]]
         z_codes = keep.tile([P, V], U32, name="z_codes", align_bytes=64)

from contextlib import ExitStack

import concourse.mybir as mybir
from concourse.masks import make_identity

K, T, S, V, H, N, U = 1024, 2048, 1024, 512, 512, 256, 256
FLOPS = 2 * K * H * S + 2 * H * N * V

F32 = mybir.dt.float32
BF16 = mybir.dt.bfloat16
I32 = mybir.dt.int32
U32 = mybir.dt.uint32
U16 = mybir.dt.uint16
U8 = mybir.dt.uint8
FP8X4 = mybir.dt.float8_e4m3fn_x4
COPY = mybir.ActivationFunctionType.Copy
RELU = mybir.ActivationFunctionType.Relu
MULT = mybir.AluOpType.mult
ADD = mybir.AluOpType.add

P = 128
PACK = 4
K_PASS = P * PACK
PASSES = K // K_PASS
LIST_ROWS = 16
LINE = 4
BANK = 512
QUADRANT = 32
SCALE_ROWS = 4

VECTOR_ENTRIES = ((384, 384, 384, 384), (0, 384, 256, 256))
X_LOADS = ((0, 0, 1), (0, 1, 1), (0, 2, 1), (0, 3, 1), (1, 0, 1), (1, 1, 1), (1, 2, 1), (1, 3, 1))
PIECE = 256
ENTRY_PIECES = ((0, 256), (256, 256), (512, 256), (768, 256))
TURNED = 256
Z_PIECES = ((0, TURNED), (TURNED, P), (TURNED + P, P))


def tile_picked_hop2_relu_e_kernel(
    tc, xT, w1, w2_words, w2_scales, gate, gate2, offs, pos1, pos2, nxt1, nxt2, out
):
    nc = tc.nc
    with ExitStack() as ctx:
        keep = ctx.enter_context(tc.tile_pool(name="keep", bufs=1))
        psum = ctx.enter_context(tc.psum_pool(name="psum", bufs=1))

        def load_list(name, source):
            tile = keep.tile(list(source.shape), U16, name=name)
            nc.sync.dma_start(tile[:], source)
            return tile

        def entries(tile, first, count):
            return tile[:, first // LIST_ROWS : (first + count) // LIST_ROWS]

        def bank(number, name):
            return psum.tile([P, BANK], F32, name=name, tag="bank_%d" % number)

        w2_scale_tile = keep.tile([P, N], U8, name="w2_scale_tile", align_bytes=64)
        nc.vector.memset(w2_scale_tile[:].bitcast(I32), 0)
        identity = keep.tile([P, P], F32, name="identity")
        make_identity(nc, identity[:])

        offs_tile = load_list("offs_tile", offs)
        planes = {}
        for g, first, count in X_LOADS:
            rows = xT[g * K_PASS : (g + 1) * K_PASS, :].rearrange("(p j) c -> p j c", j=PACK)
            raw = keep.tile([P, count * T], F32, name="x_raw_%d_%d" % (g, first), align_bytes=64)
            queue = nc.scalar if (g, first) == (0, 1) else nc.sync
            queue.dma_start(raw[:], rows[:, first : first + count, :].rearrange("p j c -> p (j c)"))
            for j in range(count):
                planes[g, first + j] = raw[:, j * T : (j + 1) * T]
        w_raw = []
        for g in range(PASSES):
            w_raw.append(keep.tile([P, PACK, H], F32, name="w_raw_%d" % g, tag="w_raw_%d" % g, align_bytes=64))
            nc.sync.dma_start(w_raw[g][:], w1[g * K_PASS : (g + 1) * K_PASS, :].rearrange("(p j) c -> p j c", j=PACK))
        pos_tiles = [load_list("pos1_tile", pos1), load_list("pos2_tile", pos2)]
        gate_turned = []
        for d in range(2):
            name = "gate_turned_%d" % d
            gate_turned.append(keep.tile([P, TURNED], F32, name=name, tag=name, align_bytes=64))
            nc.sync.dma_start(gate_turned[d][:], gate[d, :, :TURNED])
        gate_rest = keep.tile([P, 2, V - TURNED], F32, name="gate_rest")
        nc.sync.dma_start(gate_rest[:], gate[:, :, TURNED:].rearrange("d p v -> p d v"))
        w2_codes = keep.tile([P, N], U32, name="w2_codes", align_bytes=64)
        nc.sync.dma_start(w2_codes[:].bitcast(I32), w2_words[0].rearrange("p n t -> p (n t)").bitcast(I32))
        for q in range(P // QUADRANT):
            nc.sync.dma_start(
                w2_scale_tile[QUADRANT * q : QUADRANT * q + SCALE_ROWS, :].bitcast(I32),
                w2_scales[0, SCALE_ROWS * q : SCALE_ROWS * (q + 1), :].bitcast(I32),
            )
        nxt_tiles = [load_list("nxt1_tile", nxt1), load_list("nxt2_tile", nxt2)]
        gate2_tile = keep.tile([P, 2, U], F32, name="gate2_tile", tag="gate2_tile")
        nc.sync.dma_start(gate2_tile[:], gate2.rearrange("d p v -> p d v"))

        picked = {}
        for g, first, count in X_LOADS:
            if first % 2 == 0:
                dtype = F32 if count > 1 else BF16
                picked[g, first // 2] = keep.tile([P, 2, S], dtype, name="picked_%d_%d" % (g, first // 2), align_bytes=64)
        picked_words = [keep.tile([P, S - g * BANK], U32, name="picked_words_%d" % g, align_bytes=64) for g in range(PASSES)]
        picked_scales = [keep.tile([P, S], U8, name="picked_scales_%d" % g, align_bytes=64) for g in range(PASSES)]

        def pick(g, j, piece):
            split = VECTOR_ENTRIES[g][j]
            if split > 0:
                nc.vector.tensor_copy(picked[g, j // 2][:, j % 2, :split], planes[g, j].indirect(entries(offs_tile, 0, split)))
            for entry in range(split, S, piece):
                count = min(piece, S - entry)
                nc.scalar.activation(
                    picked[g, j // 2][:, j % 2, entry : entry + count],
                    planes[g, j].indirect(entries(offs_tile, entry, count)),
                    COPY,
                )

        def weave(target, g, entry, h):
            width = target.shape[1] // PACK
            nc.vector.tensor_copy(
                target[:].rearrange("p (c i j) -> p c j i", i=LINE, j=PACK)[:, :, 2 * h : 2 * h + 2, :],
                picked[g, h][:, :, entry : entry + width].rearrange("p j (c i) -> p c j i", i=LINE),
            )

        def quantize_x(source, g, entry, words):
            width = source.shape[1] // PACK
            nc.vector.quantize_mx(
                out=words.bitcast(FP8X4),
                scales=picked_scales[g][:, entry : entry + width],
                in_=source[:],
            )

        w_codes, w_scales = {}, {}

        def w_operands(g, first, count, tag=None):
            name = "w_codes_%d_%d" % (g, first)
            codes = keep.tile([P, count * P], U32, name=name, tag=tag or name, align_bytes=64)
            scales = keep.tile([P, count * P], U8, name="w_scales_%d_%d" % (g, first), align_bytes=64)
            for t in range(count):
                w_codes[g, first + t] = codes[:, t * P : (t + 1) * P]
                w_scales[g, first + t] = scales[:, t * P : (t + 1) * P]
            return codes[:], scales[:]

        def round_w(engine_copy, g, pairs, first, count):
            name = "w_grouped_%d_%d_%d" % (g, pairs[0], first)
            target = keep.tile([P, len(pairs) * 2 * count * PACK], BF16, name=name, tag=name, align_bytes=64)
            engine_copy(
                target[:].rearrange("p (u e m j) -> p u m j e", e=2, m=count, j=PACK),
                w_raw[g][:].rearrange("p j (m u e) -> p u m j e", u=2, e=2)[
                    :, pairs[0] : pairs[-1] + 1, first : first + count
                ],
            )
            return target

        def scalar_copy(target, source):
            nc.scalar.activation(target, source, COPY)

        def quantize_w(source, codes, scales):
            nc.vector.quantize_mx(out=codes.bitcast(FP8X4), scales=scales, in_=source)

        halves = [keep.tile([P, S // 2 * PACK], BF16, name="x_grouped_0_%d" % n, align_bytes=64) for n in range(2)]
        for h in range(2):
            pick(0, 2 * h, S)
            pick(0, 2 * h + 1, S)
            for n in range(2):
                weave(halves[n], 0, n * S // 2, h)
        for n in range(2):
            quantize_x(halves[n], 0, n * S // 2, picked_words[0][:, n * S // 2 : (n + 1) * S // 2])
        pieces = [
            keep.tile([P, PIECE * PACK], BF16, name="x_grouped_1_%d" % n, tag="x_grouped_1_%d" % n, align_bytes=64)
            for n in range(S // PIECE)
        ]
        pick(1, 0, S)
        pick(1, 1, S)
        for n in range(S // PIECE):
            weave(pieces[n], 1, n * PIECE, 0)
        pick(1, 2, S)
        pick(1, 3, 384)
        weave(pieces[0], 1, 0, 1)
        weave(pieces[1], 1, PIECE, 1)
        quantize_x(pieces[0], 1, 0, picked_words[1][:, :PIECE])
        weave(pieces[2], 1, 2 * PIECE, 1)
        quantize_x(pieces[1], 1, PIECE, picked_words[1][:, PIECE : 2 * PIECE])
        weave(pieces[3], 1, 3 * PIECE, 1)
        first_pair = round_w(scalar_copy, 0, [0], 0, P)
        quantize_w(first_pair[:], *w_operands(0, 0, 2))
        last_words = keep.tile([P, BANK], U32, name="last_words", tag="w_grouped_0_0_0", align_bytes=64)
        quantize_x(pieces[2], 1, 2 * PIECE, last_words[:, :PIECE])
        quantize_x(pieces[3], 1, 3 * PIECE, last_words[:, PIECE:])
        second_pair = round_w(scalar_copy, 0, [1], 0, P)
        groups = P // 2
        lower = round_w(nc.vector.tensor_copy, 1, [0, 1], 0, groups)
        upper = [round_w(scalar_copy, 1, [u], groups, groups) for u in range(2)]

        def quantize_last(t):
            width = groups * PACK
            codes, scales = w_operands(1, t, 1)
            quantize_w(lower[:, t * width : (t + 1) * width], codes[:, :groups], scales[:, :groups])
            quantize_w(upper[t // 2][:, (t % 2) * width : (t % 2 + 1) * width], codes[:, groups:], scales[:, groups:])

        quantize_last(0)
        quantize_last(1)
        quantize_w(second_pair[:], *w_operands(0, 2, 2, "w_grouped_1_0_%d" % groups))

        def first_product(target, t, g, entry, start, stop):
            width = target.shape[1]
            if g == 1 and entry >= BANK:
                words = last_words[:, entry - BANK : entry - BANK + width]
            else:
                words = picked_words[g][:, entry : entry + width]
            nc.tensor.matmul_mx(
                out=target,
                lhsT=w_codes[g, t].bitcast(FP8X4),
                lhsT_scale=w_scales[g, t],
                rhs=words.bitcast(FP8X4),
                rhs_scale=picked_scales[g][:, entry : entry + width],
                start=start,
                stop=stop,
            )

        def second_pass(target, t, s, start, stop):
            first_product(target[:], t, 1, s * BANK, start, stop)

        h_tiles = [keep.tile([P, S], F32, name="h_%d" % t) for t in range(PACK)]
        h_banks = [bank(number, "h_bank_0_%d" % number) for number in (0, 1, 2, 7)]
        second_banks = [bank(3 + s, "h_bank_1_%d" % s) for s in range(S // BANK)]
        for index, (entry, count) in enumerate(ENTRY_PIECES):
            first_product(h_banks[index][:, :count], 0, 0, entry, True, False)
        first_product(second_banks[0][:, :PIECE], 1, 0, 0, True, False)
        for index, (entry, count) in enumerate(ENTRY_PIECES):
            first_product(h_banks[index][:, :count], 0, 1, entry, False, True)
            if index % 2 == 0:
                nc.vector.tensor_scalar_max(h_tiles[0][:, entry : entry + count], h_banks[index][:, :count], 0.0)
            else:
                nc.scalar.activation(h_tiles[0][:, entry : entry + count], h_banks[index][:, :count], RELU)
        quantize_last(2)
        quantize_last(3)
        first_product(second_banks[0][:, PIECE:], 1, 1, PIECE, False, False)
        first_product(second_banks[0][:, :PIECE], 1, 1, 0, False, False)
        first_product(second_banks[0][:, PIECE:], 1, 0, PIECE, False, True)
        nc.scalar.activation(h_tiles[1][:, :BANK], second_banks[0][:], RELU)
        second_pass(second_banks[1], 1, 1, True, False)
        first_product(second_banks[1][:], 1, 0, BANK, False, True)
        nc.scalar.activation(h_tiles[1][:, BANK:], second_banks[1][:], RELU)

        blocks = TURNED // P
        rest = V - TURNED
        sum_banks = [bank(5 + b, "sum_bank_%d" % b) for b in range(blocks)]

        def make_h(t):
            banks = [bank(3 * (t % 2) + s, "h_bank_%d_%d" % (t, s)) for s in range(S // BANK)]
            for s in range(S // BANK):
                first_product(banks[s][:], t, 0, s * BANK, True, False)
                second_pass(banks[s], t, s, False, True)
                nc.scalar.activation(h_tiles[t][:, s * BANK : (s + 1) * BANK], banks[s][:], RELU)

        def gather_turned(t):
            names = ["term_%d_%d" % (t, d) for d in range(2)]
            terms = [keep.tile([P, TURNED], F32, name=name, tag=name, align_bytes=64) for name in names]
            for d in range(2):
                nc.vector.tensor_tensor(
                    terms[d][:], h_tiles[t][:].indirect(entries(pos_tiles[d], 0, TURNED)), gate_turned[d][:], MULT
                )
            return terms

        def turn(terms, t):
            for d in range(2):
                for b in range(blocks):
                    nc.tensor.matmul(
                        sum_banks[b][:, t * P : (t + 1) * P],
                        terms[d][:, b * P : (b + 1) * P],
                        identity[:],
                        start=(d == 0),
                        stop=(d == 1),
                        is_transpose=True,
                    )

        def turn_back(u):
            for b in range(blocks):
                name = "pairs_%d_%d" % (u, b)
                pairs = keep.tile([P, 2 * P], BF16, name=name, tag=name, align_bytes=64)
                nc.scalar.activation(
                    pairs[:].rearrange("v (p e) -> v p e", e=2),
                    sum_banks[b][:, 2 * u * P : (2 * u + 2) * P].rearrange("v (e p) -> v p e", e=2),
                    COPY,
                )
                start = u * TURNED + b * P
                nc.tensor.transpose(back_bank[:, start : start + P], pairs[:].bitcast(F32), identity[:])

        def gather_plain(target, t, d):
            nc.scalar.activation(target, h_tiles[t][:].indirect(entries(pos_tiles[d], TURNED, rest)), COPY)

        first_terms = gather_turned(0)
        make_h(2)
        make_h(3)
        turn(first_terms, 0)
        turn(gather_turned(1), 1)
        back_bank = bank(2, "back_bank")
        turn_back(0)
        plain = keep.tile([P, PACK - 1, rest], F32, name="plain", tag="term_1_1", align_bytes=64)
        for t in range(PACK - 1):
            gather_plain(plain[:, t, :], t, 1)
        turn(gather_turned(2), 2)
        turn(gather_turned(3), 3)
        turn_back(1)
        plain_last = keep.tile([P, 2, rest], F32, name="plain_last", tag="term_3_1", align_bytes=64)
        gather_plain(plain_last[:, 1, :], PACK - 1, 1)
        gather_plain(plain_last[:, 0, :], 0, 0)
        z_turned = keep.tile([P, TURNED * PACK], BF16, name="z_turned", align_bytes=64)
        nc.scalar.copy(
            z_turned[:].bitcast(F32).rearrange("p (v u) -> p v u", u=2),
            back_bank[:].rearrange("p (u v) -> p v u", u=2),
        )

        both_terms = keep.tile([P, 2 * PACK, rest], F32, name="both_terms", tag="gate_turned_0", align_bytes=64)
        rest_terms = [both_terms[:, d * PACK : (d + 1) * PACK, :] for d in range(2)]
        for t in range(1, PACK):
            nc.vector.tensor_tensor(
                rest_terms[0][:, t, :], h_tiles[t][:].indirect(entries(pos_tiles[0], TURNED, rest)), gate_rest[:, 0, :], MULT
            )
        nc.vector.tensor_tensor(
            rest_terms[1][:, : PACK - 1, :], plain[:], gate_rest[:, 1:2, :].to_broadcast([P, PACK - 1, rest]), MULT
        )
        nc.vector.tensor_tensor(both_terms[:, 0 : 2 * PACK : 2 * PACK - 1, :], plain_last[:], gate_rest[:], MULT)
        z_rest = keep.tile([P, rest * PACK], BF16, name="z_rest", tag="pairs_1_1", align_bytes=64)
        z_grouped = [z_turned[:], z_rest[:, : P * PACK], z_rest[:, P * PACK :]]
        z_codes = keep.tile([P, V], U32, name="z_codes", align_bytes=64)
        z_scales = keep.tile([P, V], U8, name="z_scales", align_bytes=64)

        def add_rest(index):
            cols = slice(Z_PIECES[index][0] - TURNED, Z_PIECES[index][0] - TURNED + P)
            nc.vector.tensor_tensor(
                z_grouped[index].rearrange("p (c i t) -> p c t i", i=LINE, t=PACK),
                rest_terms[0][:, :, cols].rearrange("p t (c i) -> p c t i", i=LINE),
                rest_terms[1][:, :, cols].rearrange("p t (c i) -> p c t i", i=LINE),
                ADD,
            )

        def quantize_z(index):
            column, width = Z_PIECES[index]
            nc.vector.quantize_mx(
                out=z_codes[:, column : column + width].bitcast(FP8X4),
                scales=z_scales[:, column : column + width],
                in_=z_grouped[index],
            )

        quantize_z(0)
        add_rest(1)
        add_rest(2)
        quantize_z(1)
        quantize_z(2)

        def second_product(target, m, column):
            nc.tensor.matmul_mx(
                out=target,
                lhsT=w2_codes[:, m * P : (m + 1) * P].bitcast(FP8X4),
                lhsT_scale=w2_scale_tile[:, m * P : (m + 1) * P],
                rhs=z_codes[:, column : column + target.shape[1]].bitcast(FP8X4),
                rhs_scale=z_scales[:, column : column + target.shape[1]],
                start=True,
                stop=True,
            )

        g_tiles = [keep.tile([P, V], F32, name="g_%d" % m) for m in range(N // P)]
        half = V // 2
        for m in range(N // P):
            first_bank = bank(3 + m, "g_bank_first_%d" % m)
            second_product(first_bank[:, :half], m, 0)
            nc.scalar.activation(g_tiles[m][:, :half], first_bank[:, :half], RELU)
        last_bank = bank(7, "g_bank_last_1")
        for index, number in ((1, 1), (2, 0)):
            column, width = Z_PIECES[index]
            piece_bank = bank(number, "g_bank_0_%d" % index)
            second_product(piece_bank[:, :width], 0, column)
            nc.scalar.activation(g_tiles[0][:, column : column + width], piece_bank[:, :width], RELU)
        second_product(last_bank[:, :half], 1, half)
        nc.scalar.activation(g_tiles[1][:, half:], last_bank[:, :half], RELU)

        root_terms = keep.tile([P, N // P, 2, U], F32, name="root_terms")
        root_plain = keep.tile([P, 2, U], F32, name="root_plain")
        for d in range(2):
            nc.scalar.activation(root_plain[:, d, :], g_tiles[1][:].indirect(nxt_tiles[d][:]), COPY)
            nc.vector.tensor_tensor(root_terms[:, 0, d, :], g_tiles[0][:].indirect(nxt_tiles[d][:]), gate2_tile[:, d, :], MULT)
        result = keep.tile([P, N // P, U], F32, name="result")

        def add_and_store(m, first, count):
            cols = slice(first, first + count)
            nc.vector.tensor_tensor(result[:, m, cols], root_terms[:, m, 0, cols], root_terms[:, m, 1, cols], ADD)
            nc.sync.dma_start(out[m * P : (m + 1) * P, cols], result[:, m, cols])

        nc.vector.tensor_tensor(root_terms[:, 1, 0, :], root_plain[:, 0, :], gate2_tile[:, 0, :], MULT)
        add_and_store(0, 0, U)
        for first in (0, U // 2):
            cols = slice(first, first + U // 2)
            nc.vector.tensor_tensor(root_terms[:, 1, 1, cols], root_plain[:, 1, cols], gate2_tile[:, 1, cols], MULT)
        for first in (0, U // 2):
            add_and_store(1, first, U // 2)
